import numpy as np
import ml_dtypes


def mxq(x, axis, fmt="e4m3"):
    dtype, down = {"e4m3": (ml_dtypes.float8_e4m3fn, 7), "e5m2": (ml_dtypes.float8_e5m2, 14)}[fmt]
    v = np.moveaxis(np.asarray(x, np.float32).astype(ml_dtypes.bfloat16).astype(np.float64), axis, -1)
    blocks = v.reshape(v.shape[:-1] + (-1, 32))
    amax = np.abs(blocks).max(-1, keepdims=True)
    byte = np.maximum(np.where(amax > 0, np.frexp(amax)[1] - 1 + 127, 0) - down, 1)
    scale = np.exp2(byte - 127.0)
    codes = (blocks / scale).astype(np.float32).astype(dtype).astype(np.float64)
    return np.moveaxis((codes * scale).reshape(v.shape), -1, axis)


WIDE = False


def mx_kscale(k):
    if not WIDE:
        return np.ones(k)
    levels = np.array([10, -10, 5, -5, 0])
    if k % 512:
        return np.exp2(np.random.permutation(np.resize(levels, k // 32))).repeat(32)
    a = np.empty((k // 512, 16))
    for p in range(k // 512):
        a[p, :8] = np.random.permutation(np.resize(levels, 8))
        for g in range(8):
            far = levels[np.abs(levels - a[p, g]) >= 10]
            a[p, g + 8] = far[np.random.randint(len(far))]
    return np.exp2(a.ravel()).repeat(32)


def f64(x):
    return np.asarray(x).astype(np.float64)


def striped(idx):
    return np.tile(idx.reshape(-1, 16).T, (8, 1)).astype(np.uint16)


def unstriped(offs):
    return offs[:16].T.reshape(-1).astype(np.int64)


E2M1 = np.array([0.0, 0.5, 1.0, 1.5, 2.0, 3.0, 4.0, 6.0, -0.0, -0.5, -1.0, -1.5, -2.0, -3.0, -4.0, -6.0])


def pack_weight(w, fmt):
    k, n = w.shape
    w = f64(np.asarray(w, np.float32).astype(ml_dtypes.bfloat16)).reshape(k // 32, 32, n)
    amax = np.abs(w).max(1)
    if fmt == "e4m3":
        byte = np.frexp(amax)[1] - 1 + 127 - 7
    else:
        mant, ex = np.frexp(amax / 6.0)
        byte = np.where(mant > 0.5, ex, ex - 1) + 127
    byte = np.clip(np.where(amax > 0, byte, 1), 1, 254)
    scaled = (w * np.exp2(127.0 - byte)[:, None, :]).reshape(k, n).astype(np.float32)
    by_word = np.ascontiguousarray(scaled.reshape(k // 512, 128, 4, n).transpose(0, 1, 3, 2))
    if fmt == "e4m3":
        words = by_word.astype(ml_dtypes.float8_e4m3fn).view(np.uint8)
    else:
        c = by_word.astype(ml_dtypes.float4_e2m1fn).view(np.uint8) & 0xF
        words = (c[..., 0::2] | (c[..., 1::2] << 4)).reshape(k // 512, 128, 2 * n)
    return np.ascontiguousarray(words), np.ascontiguousarray(byte.astype(np.uint8).reshape(k // 512, 16, n))


def unpack_weight(words, scales, fmt):
    g, _, n = scales.shape
    words = np.ascontiguousarray(words).reshape(g, 128, n, -1)
    if fmt == "e4m3":
        vals = words.view(ml_dtypes.float8_e4m3fn).astype(np.float64)
    else:
        nib = np.empty((g, 128, n, 4), np.uint8)
        nib[..., 0::2] = words & 0xF
        nib[..., 1::2] = words >> 4
        vals = E2M1[nib]
    vals = vals * np.repeat(np.exp2(scales.astype(np.float64) - 127.0), 8, axis=1)[..., None]
    return vals.transpose(0, 1, 3, 2).reshape(g * 512, n)


def gelu(v):
    return 0.5 * v * (1.0 + np.tanh(np.sqrt(2.0 / np.pi) * (v + 0.044715 * v**3)))


K, T, S, H, N = 1024, 4096, 1024, 1024, 512

def setup_inputs():
    n = np.random.standard_normal
    s = mx_kscale(K)[:, None]
    u = mx_kscale(H)[:, None]
    tab_words, tab_scales = pack_weight(n((K, T)) * s, "e4m3")
    w3_words, w3_scales = pack_weight(n((K, N)) / np.sqrt(K) / s, "e4m3")
    w4_words, w4_scales = pack_weight(1.5 * n((H, N)) / np.sqrt(H) / u, "e2m1")
    return {
        "tab_words": tab_words, "tab_scales": tab_scales,
        "offs": striped(np.random.permutation(T)[:S]),
        "offs2": striped(np.random.permutation(S)),
        "w1": (n((K, H)) / np.sqrt(K) / s).astype(np.float32),
        "gain": (np.exp(0.3 * n(H)) * u[:, 0]).astype(np.float32),
        "w3_words": w3_words, "w3_scales": w3_scales,
        "w4_words": w4_words, "w4_scales": w4_scales,
        "wgo": np.exp(0.3 * n((128, S))).astype(np.float32),
        "x0": n((N, S)).astype(np.float32),
    }

def reference(tab_words, tab_scales, offs, offs2, w1, gain, w3_words, w3_scales,
              w4_words, w4_scales, wgo, x0):
    v = unpack_weight(tab_words, tab_scales, "e4m3")[:, unstriped(offs)]
    w3 = unpack_weight(w3_words, w3_scales, "e4m3")
    w4 = unpack_weight(w4_words, w4_scales, "e2m1")
    h = np.tanh(mxq(f64(w1), 0, "e4m3").T @ v) * f64(gain)[:, None]
    y = (w3.T @ v) - (w4.T @ mxq(h, 0, "e4m3"))
    page = np.zeros((N, S))
    page[:, unstriped(offs2)] = np.tile(f64(wgo), (N // 128, 1)) * y
    return np.abs(page * f64(x0))

@@ -1,0 +1,259 @@
+from contextlib import ExitStack
+
+import concourse.mybir as mybir
+
+K, T, S, H, N = 1024, 4096, 1024, 1024, 512
+FLOPS = 2 * S * (K * H + K * N + H * N)
+
+F32 = mybir.dt.float32
+BF16 = mybir.dt.bfloat16
+I32 = mybir.dt.int32
+U32 = mybir.dt.uint32
+U16 = mybir.dt.uint16
+U8 = mybir.dt.uint8
+FP8X4 = mybir.dt.float8_e4m3fn_x4
+FP4X4 = mybir.dt.float4_e2m1fn_x4
+ACT = mybir.ActivationFunctionType
+MULT = mybir.AluOpType.mult
+
+P = 128
+PACK = 4
+PASS = P * PACK
+PASSES = 2
+N_TILES = N // P
+HALF = S // 2
+PIECE = 128
+
+
+def tile_list_tape_restore_residuals_kernel(
+    tc, tab_words, tab_scales, offs, offs2, w1, gain, w3_words, w3_scales, w4_words, w4_scales, wgo, x0, out
+):
+    nc = tc.nc
+    with ExitStack() as ctx:
+        keep = ctx.enter_context(tc.tile_pool(name="keep", bufs=1))
+        ring = ctx.enter_context(tc.tile_pool(name="ring", bufs=4))
+        psum = ctx.enter_context(tc.psum_pool(name="psum", bufs=2))
+
+        def held(shape, dtype, name):
+            return keep.tile(shape, dtype, name=name, align_bytes=64)
+
+        picks = keep.tile([P, S // 16], U16, name="picks")
+        places = keep.tile([P, S // 16], U16, name="places")
+        tab = [held([P, T], I32, "tab%d" % a) for a in range(PASSES)]
+        tab_sc = held([P, T], U8, "tab_sc")
+        w3_sc = held([P, PASSES, N], U8, "w3_sc")
+        w4_sc = held([P, PASSES, N], U8, "w4_sc")
+        nc.vector.memset(tab_sc[:].bitcast(I32), 0)
+        nc.vector.memset(w3_sc[:].bitcast(I32), 0)
+        nc.vector.memset(w4_sc[:].bitcast(I32), 0)
+
+        warm_in = held([P, 1], F32, "warm_in")
+        warm_out = held([P, 1], F32, "warm_out")
+        nc.vector.memset(warm_in[:], 0.0)
+        nc.scalar.activation(out=warm_out[:], in_=warm_in[:], func=ACT.Tanh)
+
+        def load_tab(a):
+            nc.sync.dma_start(out=tab[a][:], in_=tab_words[a].rearrange("p t i -> p (t i)").bitcast(I32))
+
+        gains = held([P, PASSES, PACK], F32, "gains")
+        chunks = [(0, 0), (1, 0), (0, 1), (1, 1)]
+        raw = {}
+
+        def load_w1(a, b, parts):
+            width = PASS // parts
+            raw[(a, b)] = []
+            for u in range(parts):
+                t_raw = held([P, PACK, width], F32, "raw%d%d%d" % (a, b, u))
+                c0 = PASS * b + width * u
+                nc.sync.dma_start(
+                    out=t_raw[:],
+                    in_=w1[PASS * a : PASS * (a + 1), c0 : c0 + width].rearrange("(p j) c -> p j c", j=PACK),
+                )
+                raw[(a, b)].append(t_raw)
+
+        def load_scales(sc, src):
+            for q in range(4):
+                nc.sync.dma_start(
+                    out=sc[32 * q : 32 * q + 4, :, :].bitcast(I32),
+                    in_=src[:, 4 * q : 4 * q + 4, :].rearrange("a r c -> r a c").bitcast(I32),
+                )
+
+        w3 = held([P, PASSES, N], U32, "w3")
+        w4 = held([P, PASSES, 2 * N], U8, "w4")
+        weight = held([P, S], F32, "weight")
+
+        nc.sync.dma_start(picks[:], offs)
+        load_w1(0, 0, 1)
+        for q in range(4):
+            nc.sync.dma_start(
+                out=tab_sc[32 * q : 32 * q + 8, :].bitcast(I32), in_=tab_scales[:, 4 * q : 4 * q + 4, :].bitcast(I32)
+            )
+        load_w1(1, 0, 1)
+        load_tab(0)
+        load_scales(w3_sc, w3_scales)
+        load_tab(1)
+        nc.sync.dma_start(out=w3[:].bitcast(I32), in_=w3_words.rearrange("a p c i -> p a (c i)").bitcast(I32))
+        load_scales(w4_sc, w4_scales)
+        nc.sync.dma_start(out=gains[:], in_=gain.rearrange("(b p t) -> p b t", b=PASSES, t=PACK))
+        load_w1(0, 1, 1)
+        nc.sync.dma_start(out=w4[:].bitcast(I32), in_=w4_words.rearrange("a p c -> p a c").bitcast(I32))
+        load_w1(1, 1, 2)
+        nc.sync.dma_start(places[:], offs2)
+        nc.sync.dma_start(out=weight[:], in_=wgo)
+
+        v = [held([P, S], U32, "v%d" % a) for a in range(PASSES)]
+        v_sc = held([P, S], U8, "v_sc")
+        nc.vector.tensor_copy(v_sc[:], tab_sc[:].indirect(picks[:]))
+        nc.vector.tensor_copy(v[0][:], tab[0][:].bitcast(U32).indirect(picks[:]))
+        nc.vector.tensor_copy(v[1][:, :HALF], tab[1][:].bitcast(U32).indirect(picks[:, : HALF // 16]))
+
+        w1c, w1s = {}, {}
+        for a, b in chunks:
+            grouped = keep.tile([P, PACK, P, PACK], BF16, tag="grouped%d%d" % (a, b), name="grouped", align_bytes=64)
+            w1c[(a, b)] = held([P, PASS], U32, "w1c%d%d" % (a, b))
+            w1s[(a, b)] = held([P, PASS], U8, "w1s%d%d" % (a, b))
+            parts = len(raw[(a, b)])
+            for u, t_raw in enumerate(raw[(a, b)]):
+                m0, m1 = u * P // parts, (u + 1) * P // parts
+                nc.vector.tensor_copy(
+                    out=grouped[:, :, m0:m1, :].rearrange("p t m j -> p m t j"),
+                    in_=t_raw[:].rearrange("p j (m t) -> p m t j", t=PACK),
+                )
+            tw = PACK // parts
+            for u in range(parts):
+                nc.vector.quantize_mx(
+                    out=w1c[(a, b)][:, u * tw * P : (u + 1) * tw * P].bitcast(FP8X4),
+                    scales=w1s[(a, b)][:, u * tw * P : (u + 1) * tw * P],
+                    in_=grouped[:, u * tw : (u + 1) * tw, :, :].rearrange("p t m j -> p (t m j)"),
+                )
+
+        hc = [held([P, S], U32, "hc%d" % b) for b in range(PASSES)]
+        hs = [held([P, S], U8, "hs%d" % b) for b in range(PASSES)]
+
+        def z_pass(dst, a, b, t, cols, start, stop):
+            nc.tensor.matmul_mx(
+                out=dst,
+                lhsT=w1c[(a, b)][:, P * t : P * (t + 1)].bitcast(FP8X4),
+                lhsT_scale=w1s[(a, b)][:, P * t : P * (t + 1)],
+                rhs=v[a][:, cols].bitcast(FP8X4),
+                rhs_scale=v_sc[4 * a :, cols],
+                start=start,
+                stop=stop,
+            )
+
+        def y_pass(dst, step, n, cols, start, stop):
+            ncols = slice(P * n, P * (n + 1))
+            if step < PASSES:
+                a = step
+                nc.tensor.matmul_mx(
+                    out=dst,
+                    lhsT=w3[:, a, ncols].bitcast(FP8X4),
+                    lhsT_scale=w3_sc[:, a, ncols],
+                    rhs=v[a][:, cols].bitcast(FP8X4),
+                    rhs_scale=v_sc[4 * a :, cols],
+                    start=start,
+                    stop=stop,
+                )
+            else:
+                b = step - PASSES
+                nc.tensor.matmul_mx(
+                    out=dst,
+                    lhsT=w4[:, b, 2 * P * n : 2 * P * (n + 1)].bitcast(FP4X4),
+                    lhsT_scale=w4_sc[:, b, ncols],
+                    rhs=hc[b][:, cols].bitcast(FP8X4),
+                    rhs_scale=hs[b][:, cols],
+                    start=start,
+                    stop=stop,
+                )
+
+        def code_piece(b, cols, hb):
+            z = psum.tile([P, PACK, PIECE], F32, tag="z%d" % b, name="z")
+            for a in range(PASSES):
+                for t in range(PACK):
+                    z_pass(z[:, t, :], a, b, t, cols, (a, t) == (0, 0), (a, t) == (PASSES - 1, PACK - 1))
+            if b == 1 and cols.stop == HALF:
+                th = keep.tile([P, PIECE, PACK], F32, tag="page1", name="th", align_bytes=64)
+            else:
+                th = ring.tile([P, PIECE, PACK], F32, tag="th", name="th", align_bytes=64, bufs=3)
+            nc.scalar.activation(out=th[:], in_=z[:].rearrange("p t j -> p j t"), func=ACT.Tanh, scale=-1.0)
+            nc.vector.tensor_tensor(hb, th[:], gains[:, b : b + 1, :].to_broadcast([P, PIECE, PACK]), MULT)
+            nc.vector.quantize_mx(
+                out=hc[b][:, cols].bitcast(FP8X4), scales=hs[b][:, cols], in_=hb.rearrange("p j t -> p (j t)")
+            )
+
+        pages = {}
+
+        def scatter(n, values, j0, width):
+            nc.vector.tensor_tensor(
+                pages[n][:].indirect(places[:, j0 // 16 : (j0 + width) // 16]), values, weight[:, j0 : j0 + width], MULT
+            )
+
+        pieces = [slice(c0, c0 + PIECE) for c0 in range(0, HALF, PIECE)]
+        hb_first = held([P, PIECE, PACK], BF16, "hb_first")
+        code_piece(0, pieces[0], hb_first[:])
+        hb_rest = keep.tile([P, HALF - PIECE, PACK], BF16, tag="grouped11", name="hb_rest", align_bytes=64)
+        for cols in pieces[1:]:
+            code_piece(0, cols, hb_rest[:, cols.start - PIECE : cols.stop - PIECE, :])
+        nc.vector.tensor_copy(v[1][:, HALF:], tab[1][:].bitcast(U32).indirect(picks[:, HALF // 16 :]))
+        last = N_TILES - 1
+        ysb = held([P, N_TILES, HALF], F32, "ysb")
+        hb_upper = keep.tile([P, HALF, PACK], BF16, tag="page0", name="hb_upper", align_bytes=64)
+        for cols in pieces:
+            code_piece(1, cols, hb_upper[:, cols, :])
+        for cols in pieces:
+            y = psum.tile([P, N_TILES, PIECE], F32, tag="y", name="y", bufs=4)
+            for step in range(2 * PASSES):
+                for n in range(N_TILES):
+                    y_pass(y[:, n, :], step, n, cols, (step, n) == (0, 0), (step, n) == (2 * PASSES - 1, last))
+            nc.scalar.activation(out=ysb[:, :, cols], in_=y[:], func=ACT.Abs)
+        for n in range(last):
+            pages[n] = keep.tile([P, S], F32, tag="page%d" % n, name="page", align_bytes=64)
+        quarter = HALF // 2
+        for n, j0, width in ((0, 0, quarter), (1, 0, quarter), (2, 0, HALF), (0, quarter, quarter), (1, quarter, quarter)):
+            scatter(n, ysb[:, n, j0 : j0 + width], j0, width)
+
+        cols = slice(HALF, S)
+        for b in range(PASSES):
+            planes = keep.tile([P, PACK, HALF], BF16, tag="planes%d" % b, name="planes", align_bytes=64)
+            for t in range(PACK):
+                z = psum.tile([P, HALF], F32, tag="z0", name="z")
+                for a in range(PASSES):
+                    z_pass(z[:], a, b, t, cols, a == 0, a == PASSES - 1)
+                if (b, t) >= (0, PACK - 1):
+                    th = ring.tile([P, HALF], F32, tag="th", name="th", align_bytes=64, bufs=3)
+                else:
+                    th = ring.tile([P, HALF], F32, tag="th2", name="th", align_bytes=64, bufs=2)
+                nc.scalar.activation(out=th[:], in_=z[:], func=ACT.Tanh, scale=-1.0)
+                nc.scalar.activation(out=planes[:, t, :], in_=th[:], func=ACT.Copy, scale=gains[:, b, t : t + 1])
+            woven = keep.tile([P, HALF, PACK], BF16, tag="page3" if b else "woven0", name="woven", align_bytes=64)
+            for part in pieces:
+                nc.scalar.copy(
+                    out=woven[:, part, :].rearrange("p (c i) t -> p c t i", i=4),
+                    in_=planes[:, :, part].rearrange("p t (c i) -> p c t i", i=4),
+                )
+            nc.vector.quantize_mx(
+                out=hc[b][:, cols].bitcast(FP8X4), scales=hs[b][:, cols], in_=woven[:].rearrange("p j t -> p (j t)")
+            )
+
+        feats = keep.tile([P, N_TILES, S], F32, tag="planes0", name="feats", align_bytes=64)
+        for n in range(N_TILES):
+            nc.sync.dma_start(out=feats[:, n, :], in_=x0[P * n : P * (n + 1), :])
+
+        pages[last] = keep.tile([P, S], F32, tag="page3", name="page", align_bytes=64)
+        scatter(last, ysb[:, last, :], 0, HALF)
+
+        for n in range(N_TILES):
+            y = psum.tile([P, HALF], F32, tag="y", name="y", bufs=4)
+            for step in range(2 * PASSES):
+                y_pass(y[:], step, n, cols, step == 0, step == 2 * PASSES - 1)
+            y_sb = held([P, HALF], F32, "ylast%d" % n)
+            nc.scalar.activation(out=y_sb[:], in_=y[:], func=ACT.Abs)
+            scatter(n, y_sb[:], HALF, HALF)
+            nc.scalar.activation(out=feats[:, n, :], in_=feats[:, n, :], func=ACT.Abs)
+            parts = 4 if n == last else 1
+            width = S // parts
+            for u in range(parts):
+                res = held([P, width], F32, "res%d%d" % (n, u))
+                part = slice(u * width, (u + 1) * width)
+                nc.vector.tensor_tensor(res[:], pages[n][:, part], feats[:, n, part], MULT)
+                nc.sync.dma_start(out=out[P * n : P * (n + 1), part], in_=res[:])

@@ -73,9 +73,16 @@ def tile_list_tape_restore_residuals_kernel(
 
         def load_scales(sc, src):
             for q in range(4):
-                nc.sync.dma_start(
+                nc.gpsimd.dma_start(
                     out=sc[32 * q : 32 * q + 4, :, :].bitcast(I32),
                     in_=src[:, 4 * q : 4 * q + 4, :].rearrange("a r c -> r a c").bitcast(I32),
+                )
+
+        def load_tab_scales(a):
+            for q in range(4):
+                row = 32 * q + 4 * a
+                nc.sync.dma_start(
+                    out=tab_sc[row : row + 4, :].bitcast(I32), in_=tab_scales[a, 4 * q : 4 * q + 4, :].bitcast(I32)
                 )
 
         w3 = held([P, PASSES, N], U32, "w3")
@@ -84,22 +91,20 @@ def tile_list_tape_restore_residuals_kernel(
 
         nc.sync.dma_start(picks[:], offs)
         load_w1(0, 0, 1)
-        for q in range(4):
-            nc.sync.dma_start(
-                out=tab_sc[32 * q : 32 * q + 8, :].bitcast(I32), in_=tab_scales[:, 4 * q : 4 * q + 4, :].bitcast(I32)
-            )
+        load_tab_scales(0)
         load_w1(1, 0, 1)
+        load_tab_scales(1)
         load_tab(0)
-        load_scales(w3_sc, w3_scales)
         load_tab(1)
-        nc.sync.dma_start(out=w3[:].bitcast(I32), in_=w3_words.rearrange("a p c i -> p a (c i)").bitcast(I32))
-        load_scales(w4_sc, w4_scales)
         nc.sync.dma_start(out=gains[:], in_=gain.rearrange("(b p t) -> p b t", b=PASSES, t=PACK))
+        nc.sync.dma_start(out=w3[:].bitcast(I32), in_=w3_words.rearrange("a p c i -> p a (c i)").bitcast(I32))
         load_w1(0, 1, 1)
         nc.sync.dma_start(out=w4[:].bitcast(I32), in_=w4_words.rearrange("a p c -> p a c").bitcast(I32))
         load_w1(1, 1, 2)
         nc.sync.dma_start(places[:], offs2)
         nc.sync.dma_start(out=weight[:], in_=wgo)
+        load_scales(w3_sc, w3_scales)
+        load_scales(w4_sc, w4_scales)
 
         v = [held([P, S], U32, "v%d" % a) for a in range(PASSES)]
         v_sc = held([P, S], U8, "v_sc")
@@ -167,7 +172,7 @@ def tile_list_tape_restore_residuals_kernel(
                 )
 
         def code_piece(b, cols, hb):
-            z = psum.tile([P, PACK, PIECE], F32, tag="z%d" % b, name="z")
+            z = psum.tile([P, PACK, PIECE], F32, tag="z1" if b == 1 and cols.start < 2 * PIECE else "z0", name="z")
             for a in range(PASSES):
                 for t in range(PACK):
                     z_pass(z[:, t, :], a, b, t, cols, (a, t) == (0, 0), (a, t) == (PASSES - 1, PACK - 1))
@@ -180,6 +185,22 @@ def tile_list_tape_restore_residuals_kernel(
             nc.vector.quantize_mx(
                 out=hc[b][:, cols].bitcast(FP8X4), scales=hs[b][:, cols], in_=hb.rearrange("p j t -> p (j t)")
             )
+
+        upper = slice(HALF, S)
+        planes = [
+            keep.tile([P, PACK, HALF], BF16, tag="planes%d" % b, name="planes", align_bytes=64) for b in range(PASSES)
+        ]
+
+        def code_plane(b, t, early):
+            z = psum.tile([P, HALF], F32, tag="z0", name="z")
+            for a in range(PASSES):
+                z_pass(z[:], a, b, t, upper, a == 0, a == PASSES - 1)
+            if early:
+                th = ring.tile([P, HALF], F32, tag="th2", name="th", align_bytes=64, bufs=2)
+            else:
+                th = ring.tile([P, HALF], F32, tag="th", name="th", align_bytes=64, bufs=3)
+            nc.scalar.activation(out=th[:], in_=z[:], func=ACT.Tanh, scale=-1.0)
+            nc.scalar.activation(out=planes[b][:, t, :], in_=th[:], func=ACT.Copy, scale=gains[:, b, t : t + 1])
 
         pages = {}
 
@@ -195,13 +216,16 @@ def tile_list_tape_restore_residuals_kernel(
         for cols in pieces[1:]:
             code_piece(0, cols, hb_rest[:, cols.start - PIECE : cols.stop - PIECE, :])
         nc.vector.tensor_copy(v[1][:, HALF:], tab[1][:].bitcast(U32).indirect(picks[:, HALF // 16 :]))
+        early_planes = [(0, t) for t in range(PACK - 1)]
+        for b, t in early_planes:
+            code_plane(b, t, True)
         last = N_TILES - 1
         ysb = held([P, N_TILES, HALF], F32, "ysb")
         hb_upper = keep.tile([P, HALF, PACK], BF16, tag="page0", name="hb_upper", align_bytes=64)
         for cols in pieces:
             code_piece(1, cols, hb_upper[:, cols, :])
         for cols in pieces:
-            y = psum.tile([P, N_TILES, PIECE], F32, tag="y", name="y", bufs=4)
+            y = psum.tile([P, N_TILES, PIECE], F32, tag="y" if cols.start < 2 * PIECE else "z1", name="y")
             for step in range(2 * PASSES):
                 for n in range(N_TILES):
                     y_pass(y[:, n, :], step, n, cols, (step, n) == (0, 0), (step, n) == (2 * PASSES - 1, last))
@@ -212,24 +236,16 @@ def tile_list_tape_restore_residuals_kernel(
         for n, j0, width in ((0, 0, quarter), (1, 0, quarter), (2, 0, HALF), (0, quarter, quarter), (1, quarter, quarter)):
             scatter(n, ysb[:, n, j0 : j0 + width], j0, width)
 
-        cols = slice(HALF, S)
+        cols = upper
         for b in range(PASSES):
-            planes = keep.tile([P, PACK, HALF], BF16, tag="planes%d" % b, name="planes", align_bytes=64)
             for t in range(PACK):
-                z = psum.tile([P, HALF], F32, tag="z0", name="z")
-                for a in range(PASSES):
-                    z_pass(z[:], a, b, t, cols, a == 0, a == PASSES - 1)
-                if (b, t) >= (0, PACK - 1):
-                    th = ring.tile([P, HALF], F32, tag="th", name="th", align_bytes=64, bufs=3)
-                else:
-                    th = ring.tile([P, HALF], F32, tag="th2", name="th", align_bytes=64, bufs=2)
-                nc.scalar.activation(out=th[:], in_=z[:], func=ACT.Tanh, scale=-1.0)
-                nc.scalar.activation(out=planes[:, t, :], in_=th[:], func=ACT.Copy, scale=gains[:, b, t : t + 1])
+                if (b, t) not in early_planes:
+                    code_plane(b, t, False)
             woven = keep.tile([P, HALF, PACK], BF16, tag="page3" if b else "woven0", name="woven", align_bytes=64)
             for part in pieces:
                 nc.scalar.copy(
                     out=woven[:, part, :].rearrange("p (c i) t -> p c t i", i=4),
-                    in_=planes[:, :, part].rearrange("p t (c i) -> p c t i", i=4),
+                    in_=planes[b][:, :, part].rearrange("p t (c i) -> p c t i", i=4),
                 )
             nc.vector.quantize_mx(
                 out=hc[b][:, cols].bitcast(FP8X4), scales=hs[b][:, cols], in_=woven[:].rearrange("p j t -> p (j t)")
@@ -243,7 +259,7 @@ def tile_list_tape_restore_residuals_kernel(
         scatter(last, ysb[:, last, :], 0, HALF)
 
         for n in range(N_TILES):
-            y = psum.tile([P, HALF], F32, tag="y", name="y", bufs=4)
+            y = psum.tile([P, HALF], F32, tag="z0", name="y")
             for step in range(2 * PASSES):
                 y_pass(y[:], step, n, cols, step == 0, step == 2 * PASSES - 1)
             y_sb = held([P, HALF], F32, "ylast%d" % n)

@@ -23,6 +23,7 @@ PASSES = 2
 N_TILES = N // P
 HALF = S // 2
 PIECE = 128
+QUARTER = 256
 
 
 def tile_list_tape_restore_residuals_kernel(
@@ -31,11 +32,10 @@ def tile_list_tape_restore_residuals_kernel(
     nc = tc.nc
     with ExitStack() as ctx:
         keep = ctx.enter_context(tc.tile_pool(name="keep", bufs=1))
-        ring = ctx.enter_context(tc.tile_pool(name="ring", bufs=4))
-        psum = ctx.enter_context(tc.psum_pool(name="psum", bufs=2))
+        psum = ctx.enter_context(tc.psum_pool(name="psum", bufs=1))
 
-        def held(shape, dtype, name):
-            return keep.tile(shape, dtype, name=name, align_bytes=64)
+        def held(shape, dtype, name, tag=None):
+            return keep.tile(shape, dtype, name=name, tag=tag or name, align_bytes=64)
 
         picks = keep.tile([P, S // 16], U16, name="picks")
         places = keep.tile([P, S // 16], U16, name="places")
@@ -44,19 +44,20 @@ def tile_list_tape_restore_residuals_kernel(
         w3_sc = held([P, PASSES, N], U8, "w3_sc")
         w4_sc = held([P, PASSES, N], U8, "w4_sc")
         nc.vector.memset(tab_sc[:].bitcast(I32), 0)
-        nc.vector.memset(w3_sc[:].bitcast(I32), 0)
         nc.vector.memset(w4_sc[:].bitcast(I32), 0)
+        nc.vector.memset(w3_sc[:].bitcast(I32), 0)
 
         warm_in = held([P, 1], F32, "warm_in")
         warm_out = held([P, 1], F32, "warm_out")
         nc.vector.memset(warm_in[:], 0.0)
         nc.scalar.activation(out=warm_out[:], in_=warm_in[:], func=ACT.Tanh)
 
-        def load_tab(a):
-            nc.sync.dma_start(out=tab[a][:], in_=tab_words[a].rearrange("p t i -> p (t i)").bitcast(I32))
+        def load_tab(a, c0, c1):
+            nc.sync.dma_start(
+                out=tab[a][:, c0:c1], in_=tab_words[a].rearrange("p t i -> p (t i)").bitcast(I32)[:, c0:c1]
+            )
 
         gains = held([P, PASSES, PACK], F32, "gains")
-        chunks = [(0, 0), (1, 0), (0, 1), (1, 1)]
         raw = {}
 
         def load_w1(a, b, parts):
@@ -73,7 +74,7 @@ def tile_list_tape_restore_residuals_kernel(
 
         def load_scales(sc, src):
             for q in range(4):
-                nc.gpsimd.dma_start(
+                nc.sync.dma_start(
                     out=sc[32 * q : 32 * q + 4, :, :].bitcast(I32),
                     in_=src[:, 4 * q : 4 * q + 4, :].rearrange("a r c -> r a c").bitcast(I32),
                 )
@@ -92,184 +93,220 @@ def tile_list_tape_restore_residuals_kernel(
         nc.sync.dma_start(picks[:], offs)
         load_w1(0, 0, 1)
         load_tab_scales(0)
-        load_w1(1, 0, 1)
+        load_tab(0, 0, T // 2)
         load_tab_scales(1)
-        load_tab(0)
-        load_tab(1)
+        load_tab(0, T // 2, T)
+        load_tab(1, 0, T)
+        load_scales(w4_sc, w4_scales)
         nc.sync.dma_start(out=gains[:], in_=gain.rearrange("(b p t) -> p b t", b=PASSES, t=PACK))
-        nc.sync.dma_start(out=w3[:].bitcast(I32), in_=w3_words.rearrange("a p c i -> p a (c i)").bitcast(I32))
-        load_w1(0, 1, 1)
-        nc.sync.dma_start(out=w4[:].bitcast(I32), in_=w4_words.rearrange("a p c -> p a c").bitcast(I32))
+        load_w1(1, 0, 2)
+        load_scales(w3_sc, w3_scales)
+        load_w1(0, 1, 2)
         load_w1(1, 1, 2)
+        nc.sync.dma_start(out=w4[:].bitcast(I32), in_=w4_words.rearrange("a p c -> p a c").bitcast(I32))
+        nc.sync.dma_start(out=w3[:].bitcast(I32), in_=w3_words.rearrange("a p c i -> p a (c i)").bitcast(I32))
         nc.sync.dma_start(places[:], offs2)
         nc.sync.dma_start(out=weight[:], in_=wgo)
-        load_scales(w3_sc, w3_scales)
-        load_scales(w4_sc, w4_scales)
 
         v = [held([P, S], U32, "v%d" % a) for a in range(PASSES)]
         v_sc = held([P, S], U8, "v_sc")
-        nc.vector.tensor_copy(v_sc[:], tab_sc[:].indirect(picks[:]))
-        nc.vector.tensor_copy(v[0][:], tab[0][:].bitcast(U32).indirect(picks[:]))
-        nc.vector.tensor_copy(v[1][:, :HALF], tab[1][:].bitcast(U32).indirect(picks[:, : HALF // 16]))
-
         w1c, w1s = {}, {}
-        for a, b in chunks:
-            grouped = keep.tile([P, PACK, P, PACK], BF16, tag="grouped%d%d" % (a, b), name="grouped", align_bytes=64)
+
+        def quantise_w1(a, b, calls, copies):
+            grouped = held([P, PACK, P, PACK], BF16, "grouped%d%d" % (a, b))
             w1c[(a, b)] = held([P, PASS], U32, "w1c%d%d" % (a, b))
             w1s[(a, b)] = held([P, PASS], U8, "w1s%d%d" % (a, b))
             parts = len(raw[(a, b)])
             for u, t_raw in enumerate(raw[(a, b)]):
                 m0, m1 = u * P // parts, (u + 1) * P // parts
-                nc.vector.tensor_copy(
+                copies[u](
                     out=grouped[:, :, m0:m1, :].rearrange("p t m j -> p m t j"),
                     in_=t_raw[:].rearrange("p j (m t) -> p m t j", t=PACK),
                 )
-            tw = PACK // parts
-            for u in range(parts):
+            tw = PACK // calls
+            for u in range(calls):
                 nc.vector.quantize_mx(
                     out=w1c[(a, b)][:, u * tw * P : (u + 1) * tw * P].bitcast(FP8X4),
                     scales=w1s[(a, b)][:, u * tw * P : (u + 1) * tw * P],
                     in_=grouped[:, u * tw : (u + 1) * tw, :, :].rearrange("p t m j -> p (t m j)"),
                 )
 
-        hc = [held([P, S], U32, "hc%d" % b) for b in range(PASSES)]
-        hs = [held([P, S], U8, "hs%d" % b) for b in range(PASSES)]
-
-        def z_pass(dst, a, b, t, cols, start, stop):
-            nc.tensor.matmul_mx(
-                out=dst,
-                lhsT=w1c[(a, b)][:, P * t : P * (t + 1)].bitcast(FP8X4),
-                lhsT_scale=w1s[(a, b)][:, P * t : P * (t + 1)],
-                rhs=v[a][:, cols].bitcast(FP8X4),
-                rhs_scale=v_sc[4 * a :, cols],
-                start=start,
-                stop=stop,
-            )
-
-        def y_pass(dst, step, n, cols, start, stop):
-            ncols = slice(P * n, P * (n + 1))
-            if step < PASSES:
-                a = step
-                nc.tensor.matmul_mx(
-                    out=dst,
-                    lhsT=w3[:, a, ncols].bitcast(FP8X4),
-                    lhsT_scale=w3_sc[:, a, ncols],
-                    rhs=v[a][:, cols].bitcast(FP8X4),
-                    rhs_scale=v_sc[4 * a :, cols],
-                    start=start,
-                    stop=stop,
-                )
-            else:
-                b = step - PASSES
-                nc.tensor.matmul_mx(
-                    out=dst,
-                    lhsT=w4[:, b, 2 * P * n : 2 * P * (n + 1)].bitcast(FP4X4),
-                    lhsT_scale=w4_sc[:, b, ncols],
-                    rhs=hc[b][:, cols].bitcast(FP8X4),
-                    rhs_scale=hs[b][:, cols],
-                    start=start,
-                    stop=stop,
-                )
-
-        def code_piece(b, cols, hb):
-            z = psum.tile([P, PACK, PIECE], F32, tag="z1" if b == 1 and cols.start < 2 * PIECE else "z0", name="z")
-            for a in range(PASSES):
-                for t in range(PACK):
-                    z_pass(z[:, t, :], a, b, t, cols, (a, t) == (0, 0), (a, t) == (PASSES - 1, PACK - 1))
-            if b == 1 and cols.stop == HALF:
-                th = keep.tile([P, PIECE, PACK], F32, tag="page1", name="th", align_bytes=64)
-            else:
-                th = ring.tile([P, PIECE, PACK], F32, tag="th", name="th", align_bytes=64, bufs=3)
-            nc.scalar.activation(out=th[:], in_=z[:].rearrange("p t j -> p j t"), func=ACT.Tanh, scale=-1.0)
-            nc.vector.tensor_tensor(hb, th[:], gains[:, b : b + 1, :].to_broadcast([P, PIECE, PACK]), MULT)
-            nc.vector.quantize_mx(
-                out=hc[b][:, cols].bitcast(FP8X4), scales=hs[b][:, cols], in_=hb.rearrange("p j t -> p (j t)")
-            )
-
-        upper = slice(HALF, S)
-        planes = [
-            keep.tile([P, PACK, HALF], BF16, tag="planes%d" % b, name="planes", align_bytes=64) for b in range(PASSES)
-        ]
-
-        def code_plane(b, t, early):
-            z = psum.tile([P, HALF], F32, tag="z0", name="z")
-            for a in range(PASSES):
-                z_pass(z[:], a, b, t, upper, a == 0, a == PASSES - 1)
-            if early:
-                th = ring.tile([P, HALF], F32, tag="th2", name="th", align_bytes=64, bufs=2)
-            else:
-                th = ring.tile([P, HALF], F32, tag="th", name="th", align_bytes=64, bufs=3)
-            nc.scalar.activation(out=th[:], in_=z[:], func=ACT.Tanh, scale=-1.0)
-            nc.scalar.activation(out=planes[b][:, t, :], in_=th[:], func=ACT.Copy, scale=gains[:, b, t : t + 1])
-
-        pages = {}
-
-        def scatter(n, values, j0, width):
-            nc.vector.tensor_tensor(
-                pages[n][:].indirect(places[:, j0 // 16 : (j0 + width) // 16]), values, weight[:, j0 : j0 + width], MULT
-            )
-
-        pieces = [slice(c0, c0 + PIECE) for c0 in range(0, HALF, PIECE)]
-        hb_first = held([P, PIECE, PACK], BF16, "hb_first")
-        code_piece(0, pieces[0], hb_first[:])
-        hb_rest = keep.tile([P, HALF - PIECE, PACK], BF16, tag="grouped11", name="hb_rest", align_bytes=64)
-        for cols in pieces[1:]:
-            code_piece(0, cols, hb_rest[:, cols.start - PIECE : cols.stop - PIECE, :])
+        on_vector, on_scalar = nc.vector.tensor_copy, nc.scalar.copy
+        quantise_w1(0, 0, 1, [on_vector])
+        nc.vector.tensor_copy(v_sc[:], tab_sc[:].indirect(picks[:]))
+        nc.vector.tensor_copy(v[0][:], tab[0][:].bitcast(U32).indirect(picks[:]))
+        nc.vector.tensor_copy(v[1][:, :HALF], tab[1][:].bitcast(U32).indirect(picks[:, : HALF // 16]))
         nc.vector.tensor_copy(v[1][:, HALF:], tab[1][:].bitcast(U32).indirect(picks[:, HALF // 16 :]))
-        early_planes = [(0, t) for t in range(PACK - 1)]
-        for b, t in early_planes:
-            code_plane(b, t, True)
-        last = N_TILES - 1
-        ysb = held([P, N_TILES, HALF], F32, "ysb")
-        hb_upper = keep.tile([P, HALF, PACK], BF16, tag="page0", name="hb_upper", align_bytes=64)
-        for cols in pieces:
-            code_piece(1, cols, hb_upper[:, cols, :])
-        for cols in pieces:
-            y = psum.tile([P, N_TILES, PIECE], F32, tag="y" if cols.start < 2 * PIECE else "z1", name="y")
-            for step in range(2 * PASSES):
-                for n in range(N_TILES):
-                    y_pass(y[:, n, :], step, n, cols, (step, n) == (0, 0), (step, n) == (2 * PASSES - 1, last))
-            nc.scalar.activation(out=ysb[:, :, cols], in_=y[:], func=ACT.Abs)
-        for n in range(last):
-            pages[n] = keep.tile([P, S], F32, tag="page%d" % n, name="page", align_bytes=64)
-        quarter = HALF // 2
-        for n, j0, width in ((0, 0, quarter), (1, 0, quarter), (2, 0, HALF), (0, quarter, quarter), (1, quarter, quarter)):
-            scatter(n, ysb[:, n, j0 : j0 + width], j0, width)
+        quantise_w1(1, 0, 2, [on_scalar, on_vector])
+        quantise_w1(0, 1, 1, [on_vector, on_vector])
+        quantise_w1(1, 1, 2, [on_vector, on_vector])
 
-        cols = upper
-        for b in range(PASSES):
-            for t in range(PACK):
-                if (b, t) not in early_planes:
-                    code_plane(b, t, False)
-            woven = keep.tile([P, HALF, PACK], BF16, tag="page3" if b else "woven0", name="woven", align_bytes=64)
-            for part in pieces:
-                nc.scalar.copy(
-                    out=woven[:, part, :].rearrange("p (c i) t -> p c t i", i=4),
-                    in_=planes[b][:, :, part].rearrange("p t (c i) -> p c t i", i=4),
-                )
-            nc.vector.quantize_mx(
-                out=hc[b][:, cols].bitcast(FP8X4), scales=hs[b][:, cols], in_=woven[:].rearrange("p j t -> p (j t)")
-            )
-
-        feats = keep.tile([P, N_TILES, S], F32, tag="planes0", name="feats", align_bytes=64)
+        feats = held([P, N_TILES, S], F32, "feats")
         for n in range(N_TILES):
             nc.sync.dma_start(out=feats[:, n, :], in_=x0[P * n : P * (n + 1), :])
 
-        pages[last] = keep.tile([P, S], F32, tag="page3", name="page", align_bytes=64)
-        scatter(last, ysb[:, last, :], 0, HALF)
+        hc = [held([P, S], U32, "hc%d" % b) for b in range(PASSES)]
+        hs = {}
 
-        for n in range(N_TILES):
-            y = psum.tile([P, HALF], F32, tag="z0", name="y")
-            for step in range(2 * PASSES):
-                y_pass(y[:], step, n, cols, step == 0, step == 2 * PASSES - 1)
-            y_sb = held([P, HALF], F32, "ylast%d" % n)
-            nc.scalar.activation(out=y_sb[:], in_=y[:], func=ACT.Abs)
-            scatter(n, y_sb[:], HALF, HALF)
-            nc.scalar.activation(out=feats[:, n, :], in_=feats[:, n, :], func=ACT.Abs)
-            parts = 4 if n == last else 1
+        def z_group(z, b, ts, cols):
+            for a in range(PASSES):
+                for i, t in enumerate(ts):
+                    nc.tensor.matmul_mx(
+                        out=z[:, i, :],
+                        lhsT=w1c[(a, b)][:, P * t : P * (t + 1)].bitcast(FP8X4),
+                        lhsT_scale=w1s[(a, b)][:, P * t : P * (t + 1)],
+                        rhs=v[a][:, cols].bitcast(FP8X4),
+                        rhs_scale=v_sc[4 * a :, cols],
+                        start=(a, i) == (0, 0),
+                        stop=(a, i) == (PASSES - 1, len(ts) - 1),
+                    )
+
+        def w3_passes(y, ns, cols):
+            for a in range(PASSES):
+                for i, n in enumerate(ns):
+                    ncols = slice(P * n, P * (n + 1))
+                    nc.tensor.matmul_mx(
+                        out=y[:, i, :],
+                        lhsT=w3[:, a, ncols].bitcast(FP8X4),
+                        lhsT_scale=w3_sc[:, a, ncols],
+                        rhs=v[a][:, cols].bitcast(FP8X4),
+                        rhs_scale=v_sc[4 * a :, cols],
+                        start=False,
+                        stop=False,
+                    )
+
+        def w4_passes(y, b, ns, cols):
+            starts = range(cols.start, cols.stop, PIECE)
+            for i, n in enumerate(ns):
+                for c0 in starts:
+                    nc.tensor.matmul_mx(
+                        out=y[:, i, c0 - cols.start : c0 - cols.start + PIECE],
+                        lhsT=w4[:, b, 2 * P * n : 2 * P * (n + 1)].bitcast(FP4X4),
+                        lhsT_scale=w4_sc[:, b, P * n : P * (n + 1)],
+                        rhs=hc[b][:, c0 : c0 + PIECE].bitcast(FP8X4),
+                        rhs_scale=hs[(b, cols.start)][:, c0 - cols.start : c0 - cols.start + PIECE],
+                        start=b == 0 and i == 0 and c0 == cols.start,
+                        stop=b == PASSES - 1 and i == len(ns) - 1 and c0 == starts[-1],
+                    )
+
+        def quantise_h(b, cols, woven, tag=None):
+            plane = held([P, cols.stop - cols.start], U8, "hs%d_%d" % (b, cols.start), tag=tag)
+            hs[(b, cols.start)] = plane
+            nc.vector.quantize_mx(
+                out=hc[b][:, cols].bitcast(FP8X4), scales=plane[:], in_=woven.rearrange("p j t -> p (j t)")
+            )
+
+        pages = [held([P, S], F32, "page%d" % n) for n in range(N_TILES)]
+
+        def scatter(n, values, cols):
+            nc.vector.tensor_tensor(
+                pages[n][:].indirect(places[:, cols.start // 16 : cols.stop // 16]), values, weight[:, cols], MULT
+            )
+
+        pieces = [slice(0, PIECE), slice(PIECE, 2 * PIECE)]
+        th_first = {}
+        for b in range(PASSES):
+            for i, cols in enumerate(pieces):
+                z = psum.tile([P, PACK, PIECE], F32, tag="bank%d" % (4 * b + i), name="z")
+                z_group(z, b, range(PACK), cols)
+                th_first[(b, i)] = held([P, PIECE, PACK], F32, "th_first%d%d" % (b, i))
+                nc.scalar.activation(
+                    out=th_first[(b, i)][:], in_=z[:].rearrange("p t j -> p j t"), func=ACT.Tanh, scale=-1.0
+                )
+        y_first = []
+        all_n = range(N_TILES)
+        for i, cols in enumerate(pieces):
+            y = psum.tile([P, N_TILES, PIECE], F32, tag="bank%d" % (6 + i), name="y")
+            for b in range(PASSES):
+                hb = held([P, PIECE, PACK], BF16, "hb%d%d" % (b, i), tag={(0, 0): "grouped11", (0, 1): "raw111"}.get((b, i)))
+                nc.vector.tensor_tensor(
+                    hb[:], th_first[(b, i)][:], gains[:, b : b + 1, :].to_broadcast([P, PIECE, PACK]), MULT
+                )
+                quantise_h(b, cols, hb[:])
+                w4_passes(y, b, all_n, cols)
+                if b == 0:
+                    w3_passes(y, all_n, cols)
+            y_first.append(y)
+
+        quarters = [slice(c0, c0 + QUARTER) for c0 in range(QUARTER, S, QUARTER)]
+        pairs = [(0, 1), (2, 3)]
+        y_banks = {}
+
+        def tanh_planes(g, b):
+            ths = []
+            for u, ts in enumerate(pairs):
+                z = psum.tile([P, 2, QUARTER], F32, tag="bank%d" % (2 * (b if g else 1) + u), name="z")
+                z_group(z, b, ts, quarters[g])
+                th = held([P, 2, QUARTER], F32, "th", tag="th%d" % u)
+                nc.scalar.activation(out=th[:], in_=z[:], func=ACT.Tanh, scale=-1.0)
+                ths.append(th)
+            return ths
+
+        def finish_h(g, b, ths):
+            cols = quarters[g]
+            planes = held([P, PACK, QUARTER], BF16, "planes%d%d" % (g, b))
+            for t in range(PACK):
+                nc.scalar.activation(
+                    out=planes[:, t, :], in_=ths[t // 2][:, t % 2, :], func=ACT.Copy, scale=gains[:, b, t : t + 1]
+                )
+            woven = held([P, QUARTER, PACK], BF16, "woven%d%d" % (g, b))
+            nc.scalar.copy(
+                out=woven[:].rearrange("p (c i) t -> p c t i", i=4),
+                in_=planes[:].rearrange("p t (c i) -> p c t i", i=4),
+            )
+            quantise_h(b, cols, woven[:], "th_first10" if (g, b) == (0, 0) else None)
+            for u, ns in enumerate(pairs):
+                if b == 0:
+                    y_banks[(g, u)] = psum.tile([P, 2, QUARTER], F32, tag="bank%d" % (4 + 2 * (g % 2) + u), name="y")
+                w4_passes(y_banks[(g, u)], b, ns, cols)
+                if b == 0:
+                    w3_passes(y_banks[(g, u)], ns, cols)
+
+        def place(values, bank, ns, cols):
+            nc.scalar.activation(out=values, in_=bank, func=ACT.Abs)
+            for i, n in enumerate(ns):
+                scatter(n, values[:, i, :], cols)
+
+        finish_h(0, 0, tanh_planes(0, 0))
+        ths = tanh_planes(0, 1)
+        place(held([P, N_TILES, PIECE], F32, "ys_first0", tag="th_first11")[:], y_first[0][:], all_n, pieces[0])
+        finish_h(0, 1, ths)
+        place(held([P, N_TILES, PIECE], F32, "ys_first1", tag="planes01")[:], y_first[1][:], all_n, pieces[1])
+        last = len(quarters) - 1
+        for g in range(1, last + 1):
+            before = quarters[g - 1]
+            ths = tanh_planes(g, 0)
+            place(held([P, 2, QUARTER], F32, "ys%d0" % g)[:], y_banks[(g - 1, 0)][:], pairs[0], before)
+            finish_h(g, 0, ths)
+            ths = tanh_planes(g, 1)
+            place(held([P, 1, QUARTER], F32, "ys%d1" % g)[:], y_banks[(g - 1, 1)][:, 0:1, :], [2], before)
+            finish_h(g, 1, ths)
+            width = QUARTER + (N_TILES * S if g == last else 0)
+            late = held([P, width], F32, "late%d" % g, tag="planes%d1" % g)
+            place(
+                late[:, :QUARTER].rearrange("p (o j) -> p o j", o=1), y_banks[(g - 1, 1)][:, 1:2, :], [3], before
+            )
+
+        sizes = late[:, QUARTER:].rearrange("p (n m) -> p n m", n=N_TILES)
+
+        def size_of_features(n):
+            nc.scalar.activation(out=sizes[:, n, :], in_=feats[:, n, :], func=ACT.Abs)
+
+        def weigh_and_store(n, parts):
             width = S // parts
             for u in range(parts):
-                res = held([P, width], F32, "res%d%d" % (n, u))
                 part = slice(u * width, (u + 1) * width)
-                nc.vector.tensor_tensor(res[:], pages[n][:, part], feats[:, n, part], MULT)
-                nc.sync.dma_start(out=out[P * n : P * (n + 1), part], in_=res[:])
+                nc.vector.tensor_tensor(feats[:, n, part], pages[n][:, part], sizes[:, n, part], MULT)
+                nc.sync.dma_start(out=out[P * n : P * (n + 1), part], in_=feats[:, n, part])
+
+        cols = quarters[last]
+        size_of_features(0)
+        place(held([P, 2, QUARTER], F32, "ys_last0")[:], y_banks[(last, 0)][:], pairs[0], cols)
+        weigh_and_store(0, 1)
+        place(held([P, 1, QUARTER], F32, "ys_last2")[:], y_banks[(last, 1)][:, 0:1, :], [2], cols)
+        for n in (1, 2):
+            size_of_features(n)
+            weigh_and_store(n, 1)
+        size_of_features(3)
+        place(held([P, 1, QUARTER], F32, "ys_last3")[:], y_banks[(last, 1)][:, 1:2, :], [3], cols)
+        weigh_and_store(3, 4)

@@ -24,6 +24,7 @@ N_TILES = N // P
 HALF = S // 2
 PIECE = 128
 QUARTER = 256
+W3_ROW = 8
 
 
 def tile_list_tape_restore_residuals_kernel(
@@ -72,19 +73,19 @@ def tile_list_tape_restore_residuals_kernel(
                 )
                 raw[(a, b)].append(t_raw)
 
-        def load_scales(sc, src):
-            for q in range(4):
-                nc.sync.dma_start(
-                    out=sc[32 * q : 32 * q + 4, :, :].bitcast(I32),
-                    in_=src[:, 4 * q : 4 * q + 4, :].rearrange("a r c -> r a c").bitcast(I32),
+        def load_scales(sc, first_row, src):
+            for r in range(4):
+                nc.gpsimd.dma_start(
+                    out=sc[first_row + r : P : 32, :, :].bitcast(I32),
+                    in_=src[:, r:16:4, :].rearrange("a q c -> q a c").bitcast(I32),
                 )
 
-        def load_tab_scales(a):
-            for q in range(4):
-                row = 32 * q + 4 * a
-                nc.sync.dma_start(
-                    out=tab_sc[row : row + 4, :].bitcast(I32), in_=tab_scales[a, 4 * q : 4 * q + 4, :].bitcast(I32)
-                )
+        def load_tab_scales(rows):
+            for r in rows:
+                for a in range(PASSES):
+                    nc.sync.dma_start(
+                        out=tab_sc[4 * a + r : P : 32, :].bitcast(I32), in_=tab_scales[a, r:16:4, :].bitcast(I32)
+                    )
 
         w3 = held([P, PASSES, N], U32, "w3")
         w4 = held([P, PASSES, 2 * N], U8, "w4")
@@ -92,15 +93,15 @@ def tile_list_tape_restore_residuals_kernel(
 
         nc.sync.dma_start(picks[:], offs)
         load_w1(0, 0, 1)
-        load_tab_scales(0)
+        load_tab_scales((0, 1))
         load_tab(0, 0, T // 2)
-        load_tab_scales(1)
+        load_tab_scales((2, 3))
         load_tab(0, T // 2, T)
         load_tab(1, 0, T)
-        load_scales(w4_sc, w4_scales)
+        load_scales(w4_sc, 0, w4_scales)
         nc.sync.dma_start(out=gains[:], in_=gain.rearrange("(b p t) -> p b t", b=PASSES, t=PACK))
         load_w1(1, 0, 2)
-        load_scales(w3_sc, w3_scales)
+        load_scales(w3_sc, W3_ROW, w3_scales)
         load_w1(0, 1, 2)
         load_w1(1, 1, 2)
         nc.sync.dma_start(out=w4[:].bitcast(I32), in_=w4_words.rearrange("a p c -> p a c").bitcast(I32))
@@ -168,7 +169,7 @@ def tile_list_tape_restore_residuals_kernel(
                     nc.tensor.matmul_mx(
                         out=y[:, i, :],
                         lhsT=w3[:, a, ncols].bitcast(FP8X4),
-                        lhsT_scale=w3_sc[:, a, ncols],
+                        lhsT_scale=w3_sc[W3_ROW:, a, ncols],
                         rhs=v[a][:, cols].bitcast(FP8X4),
                         rhs_scale=v_sc[4 * a :, cols],
                         start=False,

@@ -48,11 +48,6 @@ def tile_list_tape_restore_residuals_kernel(
         nc.vector.memset(w4_sc[:].bitcast(I32), 0)
         nc.vector.memset(w3_sc[:].bitcast(I32), 0)
 
-        warm_in = held([P, 1], F32, "warm_in")
-        warm_out = held([P, 1], F32, "warm_out")
-        nc.vector.memset(warm_in[:], 0.0)
-        nc.scalar.activation(out=warm_out[:], in_=warm_in[:], func=ACT.Tanh)
-
         def load_tab(a, c0, c1):
             nc.sync.dma_start(
                 out=tab[a][:, c0:c1], in_=tab_words[a].rearrange("p t i -> p (t i)").bitcast(I32)[:, c0:c1]
@@ -217,76 +212,115 @@ def tile_list_tape_restore_residuals_kernel(
         y_first = []
         all_n = range(N_TILES)
         for i, cols in enumerate(pieces):
-            y = psum.tile([P, N_TILES, PIECE], F32, tag="bank%d" % (6 + i), name="y")
+            splits = [(0, range(0, 1)), (6, range(1, N_TILES))] if i == 0 else [(7, all_n)]
+            y = [psum.tile([P, len(ns), PIECE], F32, tag="bank%d" % bank, name="y") for bank, ns in splits]
             for b in range(PASSES):
                 hb = held([P, PIECE, PACK], BF16, "hb%d%d" % (b, i), tag={(0, 0): "grouped11", (0, 1): "raw111"}.get((b, i)))
                 nc.vector.tensor_tensor(
                     hb[:], th_first[(b, i)][:], gains[:, b : b + 1, :].to_broadcast([P, PIECE, PACK]), MULT
                 )
                 quantise_h(b, cols, hb[:])
-                w4_passes(y, b, all_n, cols)
-                if b == 0:
-                    w3_passes(y, all_n, cols)
-            y_first.append(y)
+                for bank, (number, ns) in zip(y, splits):
+                    w4_passes(bank, b, ns, cols)
+                    if b == 0:
+                        w3_passes(bank, ns, cols)
+            y_first.extend(y)
 
-        quarters = [slice(c0, c0 + QUARTER) for c0 in range(QUARTER, S, QUARTER)]
-        pairs = [(0, 1), (2, 3)]
-        y_banks = {}
+        units = [slice(256, 512), slice(512, 768), slice(768, 896), slice(896, S)]
+        z_banks = [((2, 3), (4, 5)), ((0, 1), (2, 3)), ((0,), (1,)), ((0,), (3,))]
+        y_banks = [(4, 5), (6, 7), (2,), (4,)]
+        ys_psum = {}
 
-        def tanh_planes(g, b):
-            ths = []
-            for u, ts in enumerate(pairs):
-                z = psum.tile([P, 2, QUARTER], F32, tag="bank%d" % (2 * (b if g else 1) + u), name="z")
-                z_group(z, b, ts, quarters[g])
-                th = held([P, 2, QUARTER], F32, "th", tag="th%d" % u)
-                nc.scalar.activation(out=th[:], in_=z[:], func=ACT.Tanh, scale=-1.0)
-                ths.append(th)
-            return ths
+        def groups(g):
+            per_bank = PASS // (units[g].stop - units[g].start)
+            return [range(i, i + per_bank) for i in range(0, PACK, per_bank)]
 
-        def finish_h(g, b, ths):
-            cols = quarters[g]
-            planes = held([P, PACK, QUARTER], BF16, "planes%d%d" % (g, b))
+        ths, planes_of = {}, {}
+
+        def tanh_bank(g, b, u):
+            bank, ts = z_banks[g][b][u], groups(g)[u]
+            width = units[g].stop - units[g].start
+            z = psum.tile([P, len(ts), width], F32, tag="bank%d" % bank, name="z")
+            z_group(z, b, ts, units[g])
+            th = held([P, len(ts), width], F32, "th", tag="th%d" % (bank % 2))
+            nc.scalar.activation(out=th[:], in_=z[:], func=ACT.Tanh, scale=-1.0)
+            for i, t in enumerate(ts):
+                ths[(g, b, t)] = th[:, i, :]
+
+        def apply_gain(g, b):
+            planes = held([P, PACK, units[g].stop - units[g].start], BF16, "planes%d%d" % (g, b))
             for t in range(PACK):
                 nc.scalar.activation(
-                    out=planes[:, t, :], in_=ths[t // 2][:, t % 2, :], func=ACT.Copy, scale=gains[:, b, t : t + 1]
+                    out=planes[:, t, :], in_=ths[(g, b, t)], func=ACT.Copy, scale=gains[:, b, t : t + 1]
                 )
-            woven = held([P, QUARTER, PACK], BF16, "woven%d%d" % (g, b))
+            planes_of[(g, b)] = planes
+
+        def weave(g, b):
+            cols = units[g]
+            width = cols.stop - cols.start
+            first = (g, b) == (0, 0)
+            planes = planes_of[(g, b)]
+            woven = held([P, width, PACK], BF16, "woven%d%d" % (g, b), tag="grouped11" if first else None)
             nc.scalar.copy(
                 out=woven[:].rearrange("p (c i) t -> p c t i", i=4),
                 in_=planes[:].rearrange("p t (c i) -> p c t i", i=4),
             )
-            quantise_h(b, cols, woven[:], "th_first10" if (g, b) == (0, 0) else None)
-            for u, ns in enumerate(pairs):
-                if b == 0:
-                    y_banks[(g, u)] = psum.tile([P, 2, QUARTER], F32, tag="bank%d" % (4 + 2 * (g % 2) + u), name="y")
-                w4_passes(y_banks[(g, u)], b, ns, cols)
-                if b == 0:
-                    w3_passes(y_banks[(g, u)], ns, cols)
+            quantise_h(b, cols, woven[:], "hb10" if first else None)
+            if first:
+                return
+            for bank, ns in zip(y_banks[g], groups(g)):
+                if (g, ns[0]) not in ys_psum:
+                    y = psum.tile([P, len(ns), width], F32, tag="bank%d" % bank, name="y")
+                    ys_psum[(g, ns[0])] = y
+                    w4_passes(y, 0, ns, cols)
+                    w3_passes(y, ns, cols)
+                if b == 1:
+                    w4_passes(ys_psum[(g, ns[0])], 1, ns, cols)
 
         def place(values, bank, ns, cols):
             nc.scalar.activation(out=values, in_=bank, func=ACT.Abs)
             for i, n in enumerate(ns):
                 scatter(n, values[:, i, :], cols)
 
-        finish_h(0, 0, tanh_planes(0, 0))
-        ths = tanh_planes(0, 1)
-        place(held([P, N_TILES, PIECE], F32, "ys_first0", tag="th_first11")[:], y_first[0][:], all_n, pieces[0])
-        finish_h(0, 1, ths)
-        place(held([P, N_TILES, PIECE], F32, "ys_first1", tag="planes01")[:], y_first[1][:], all_n, pieces[1])
-        last = len(quarters) - 1
-        for g in range(1, last + 1):
-            before = quarters[g - 1]
-            ths = tanh_planes(g, 0)
-            place(held([P, 2, QUARTER], F32, "ys%d0" % g)[:], y_banks[(g - 1, 0)][:], pairs[0], before)
-            finish_h(g, 0, ths)
-            ths = tanh_planes(g, 1)
-            place(held([P, 1, QUARTER], F32, "ys%d1" % g)[:], y_banks[(g - 1, 1)][:, 0:1, :], [2], before)
-            finish_h(g, 1, ths)
-            width = QUARTER + (N_TILES * S if g == last else 0)
-            late = held([P, width], F32, "late%d" % g, tag="planes%d1" % g)
-            place(
-                late[:, :QUARTER].rearrange("p (o j) -> p o j", o=1), y_banks[(g - 1, 1)][:, 1:2, :], [3], before
-            )
+        def place_unit(g, n0, n1, values=None):
+            cols = units[g]
+            per_bank = len(groups(g)[0])
+            first = n0 // per_bank * per_bank
+            if values is None:
+                values = held([P, n1 - n0, cols.stop - cols.start], F32, "ys%d%d" % (g, n0))[:]
+            place(values, ys_psum[(g, first)][:, n0 - first : n1 - first, :], range(n0, n1), cols)
+
+        def first_rows(name, tag, y, n0, n1, rows, cols):
+            place(held([P, n1 - n0, PIECE], F32, name, tag=tag)[:], y[:, rows, :], range(n0, n1), cols)
+
+        last = len(units) - 1
+        steps = [(g, b) for g in range(last + 1) for b in range(PASSES)]
+        tanh_bank(0, 0, 0)
+        tanh_bank(0, 0, 1)
+        for (g, b), ahead in zip(steps, steps[1:] + [None]):
+            apply_gain(g, b)
+            if ahead and (g, b) != (0, 0):
+                tanh_bank(*ahead, 0)
+            weave(g, b)
+            if (g, b) == (0, 0):
+                first_rows("ys_first0", None, y_first[0], 0, 1, slice(0, 1), pieces[0])
+                first_rows("ys_first1", "th_first11", y_first[1], 1, 4, slice(0, 3), pieces[0])
+                tanh_bank(*ahead, 0)
+            if ahead and len(groups(ahead[0])) == 2:
+                tanh_bank(*ahead, 1)
+            wide = g > 0 and len(groups(g - 1)) == 2
+            if (g, b) == (0, 0):
+                first_rows("ys_first2", None, y_first[2], 0, 2, slice(0, 2), pieces[1])
+            elif g == 0:
+                first_rows("ys_first3", "planes01", y_first[2], 2, 4, slice(2, 4), pieces[1])
+            elif b == 0:
+                place_unit(g - 1, *((2, 3) if wide else (0, 2)))
+            else:
+                late = held([P, QUARTER + (N_TILES * S if g == last else 0)], F32, "late%d" % g, tag="planes%d1" % g)
+                n0 = 3 if wide else 2
+                place_unit(g - 1, n0, N_TILES, late[:, :QUARTER].rearrange("p (n j) -> p n j", n=N_TILES - n0))
+            if b == 1 and len(groups(g)) == 2:
+                place_unit(g, 0, 2)
 
         sizes = late[:, QUARTER:].rearrange("p (n m) -> p n m", n=N_TILES)
 
@@ -300,14 +334,13 @@ def tile_list_tape_restore_residuals_kernel(
                 nc.vector.tensor_tensor(feats[:, n, part], pages[n][:, part], sizes[:, n, part], MULT)
                 nc.sync.dma_start(out=out[P * n : P * (n + 1), part], in_=feats[:, n, part])
 
-        cols = quarters[last]
         size_of_features(0)
-        place(held([P, 2, QUARTER], F32, "ys_last0")[:], y_banks[(last, 0)][:], pairs[0], cols)
+        place_unit(last, 0, 2)
         weigh_and_store(0, 1)
-        place(held([P, 1, QUARTER], F32, "ys_last2")[:], y_banks[(last, 1)][:, 0:1, :], [2], cols)
+        place_unit(last, 2, 3)
         for n in (1, 2):
             size_of_features(n)
             weigh_and_store(n, 1)
         size_of_features(3)
-        place(held([P, 1, QUARTER], F32, "ys_last3")[:], y_banks[(last, 1)][:, 1:2, :], [3], cols)
+        place_unit(last, 3, 4)
         weigh_and_store(3, 4)

@@ -41,17 +41,18 @@ def tile_list_tape_restore_residuals_kernel(
         picks = keep.tile([P, S // 16], U16, name="picks")
         places = keep.tile([P, S // 16], U16, name="places")
         tab = [held([P, T], I32, "tab%d" % a) for a in range(PASSES)]
-        tab_sc = held([P, T], U8, "tab_sc")
+        tab_sc = [held([P, T], U8, "tab_sc%d" % a) for a in range(PASSES)]
+        v_sc = held([P, PASSES, S], U8, "v_sc")
         w3_sc = held([P, PASSES, N], U8, "w3_sc")
         w4_sc = held([P, PASSES, N], U8, "w4_sc")
-        nc.vector.memset(tab_sc[:].bitcast(I32), 0)
+        for a in range(PASSES):
+            nc.vector.memset(tab_sc[a][:].bitcast(I32), 0)
+        nc.vector.memset(v_sc[:].bitcast(I32), 0)
         nc.vector.memset(w4_sc[:].bitcast(I32), 0)
         nc.vector.memset(w3_sc[:].bitcast(I32), 0)
 
-        def load_tab(a, c0, c1):
-            nc.sync.dma_start(
-                out=tab[a][:, c0:c1], in_=tab_words[a].rearrange("p t i -> p (t i)").bitcast(I32)[:, c0:c1]
-            )
+        def load_tab(a):
+            nc.sync.dma_start(out=tab[a][:], in_=tab_words[a].rearrange("p t i -> p (t i)").bitcast(I32))
 
         gains = held([P, PASSES, PACK], F32, "gains")
         raw = {}
@@ -75,29 +76,26 @@ def tile_list_tape_restore_residuals_kernel(
                     in_=src[:, r:16:4, :].rearrange("a q c -> q a c").bitcast(I32),
                 )
 
-        def load_tab_scales(rows):
-            for r in rows:
-                for a in range(PASSES):
-                    nc.sync.dma_start(
-                        out=tab_sc[4 * a + r : P : 32, :].bitcast(I32), in_=tab_scales[a, r:16:4, :].bitcast(I32)
-                    )
-
         w3 = held([P, PASSES, N], U32, "w3")
         w4 = held([P, PASSES, 2 * N], U8, "w4")
         weight = held([P, S], F32, "weight")
 
         nc.sync.dma_start(picks[:], offs)
         load_w1(0, 0, 1)
-        load_tab_scales((0, 1))
-        load_tab(0, 0, T // 2)
-        load_tab_scales((2, 3))
-        load_tab(0, T // 2, T)
-        load_tab(1, 0, T)
+        for a in range(PASSES):
+            nc.sync.dma_start(out=tab_sc[a][0:P:8, :].bitcast(I32), in_=tab_scales[a].bitcast(I32))
+        load_tab(0)
+        load_tab(1)
+        picked_sc = held([P, PASSES, S], U8, "picked_sc")
+        for a in range(PASSES):
+            nc.vector.tensor_copy(picked_sc[:, a, :], tab_sc[a][:].indirect(picks[:]))
+        for r in range(4):
+            nc.sync.dma_start(out=v_sc[r:P:32, :, :].bitcast(I32), in_=picked_sc[8 * r : P : 32, :, :].bitcast(I32))
         load_scales(w4_sc, 0, w4_scales)
         nc.sync.dma_start(out=gains[:], in_=gain.rearrange("(b p t) -> p b t", b=PASSES, t=PACK))
         load_w1(1, 0, 2)
         load_scales(w3_sc, W3_ROW, w3_scales)
-        load_w1(0, 1, 2)
+        load_w1(0, 1, 1)
         load_w1(1, 1, 2)
         nc.sync.dma_start(out=w4[:].bitcast(I32), in_=w4_words.rearrange("a p c -> p a c").bitcast(I32))
         nc.sync.dma_start(out=w3[:].bitcast(I32), in_=w3_words.rearrange("a p c i -> p a (c i)").bitcast(I32))
@@ -105,7 +103,6 @@ def tile_list_tape_restore_residuals_kernel(
         nc.sync.dma_start(out=weight[:], in_=wgo)
 
         v = [held([P, S], U32, "v%d" % a) for a in range(PASSES)]
-        v_sc = held([P, S], U8, "v_sc")
         w1c, w1s = {}, {}
 
         def quantise_w1(a, b, calls, copies):
@@ -128,13 +125,12 @@ def tile_list_tape_restore_residuals_kernel(
                 )
 
         on_vector, on_scalar = nc.vector.tensor_copy, nc.scalar.copy
-        quantise_w1(0, 0, 1, [on_vector])
-        nc.vector.tensor_copy(v_sc[:], tab_sc[:].indirect(picks[:]))
+        quantise_w1(0, 0, 1, [on_scalar])
         nc.vector.tensor_copy(v[0][:], tab[0][:].bitcast(U32).indirect(picks[:]))
         nc.vector.tensor_copy(v[1][:, :HALF], tab[1][:].bitcast(U32).indirect(picks[:, : HALF // 16]))
         nc.vector.tensor_copy(v[1][:, HALF:], tab[1][:].bitcast(U32).indirect(picks[:, HALF // 16 :]))
         quantise_w1(1, 0, 2, [on_scalar, on_vector])
-        quantise_w1(0, 1, 1, [on_vector, on_vector])
+        quantise_w1(0, 1, 1, [on_vector])
         quantise_w1(1, 1, 2, [on_vector, on_vector])
 
         feats = held([P, N_TILES, S], F32, "feats")
@@ -152,7 +148,7 @@ def tile_list_tape_restore_residuals_kernel(
                         lhsT=w1c[(a, b)][:, P * t : P * (t + 1)].bitcast(FP8X4),
                         lhsT_scale=w1s[(a, b)][:, P * t : P * (t + 1)],
                         rhs=v[a][:, cols].bitcast(FP8X4),
-                        rhs_scale=v_sc[4 * a :, cols],
+                        rhs_scale=v_sc[:, a, cols],
                         start=(a, i) == (0, 0),
                         stop=(a, i) == (PASSES - 1, len(ts) - 1),
                     )
@@ -166,7 +162,7 @@ def tile_list_tape_restore_residuals_kernel(
                         lhsT=w3[:, a, ncols].bitcast(FP8X4),
                         lhsT_scale=w3_sc[W3_ROW:, a, ncols],
                         rhs=v[a][:, cols].bitcast(FP8X4),
-                        rhs_scale=v_sc[4 * a :, cols],
+                        rhs_scale=v_sc[:, a, cols],
                         start=False,
                         stop=False,
                     )

@@ -45,14 +45,16 @@ def tile_list_tape_restore_residuals_kernel(
         v_sc = held([P, PASSES, S], U8, "v_sc")
         w3_sc = held([P, PASSES, N], U8, "w3_sc")
         w4_sc = held([P, PASSES, N], U8, "w4_sc")
-        for a in range(PASSES):
-            nc.vector.memset(tab_sc[a][:].bitcast(I32), 0)
+        nc.vector.memset(tab_sc[0][:].bitcast(I32), 0)
+        nc.gpsimd.memset(tab_sc[1][:].bitcast(I32), 0)
         nc.vector.memset(v_sc[:].bitcast(I32), 0)
         nc.vector.memset(w4_sc[:].bitcast(I32), 0)
         nc.vector.memset(w3_sc[:].bitcast(I32), 0)
 
-        def load_tab(a):
-            nc.sync.dma_start(out=tab[a][:], in_=tab_words[a].rearrange("p t i -> p (t i)").bitcast(I32))
+        def load_tab(a, c0, c1):
+            nc.sync.dma_start(
+                out=tab[a][:, c0:c1], in_=tab_words[a].rearrange("p t i -> p (t i)").bitcast(I32)[:, c0:c1]
+            )
 
         gains = held([P, PASSES, PACK], F32, "gains")
         raw = {}
@@ -80,20 +82,21 @@ def tile_list_tape_restore_residuals_kernel(
         w4 = held([P, PASSES, 2 * N], U8, "w4")
         weight = held([P, S], F32, "weight")
 
-        nc.sync.dma_start(picks[:], offs)
         load_w1(0, 0, 1)
+        nc.sync.dma_start(picks[:], offs)
         for a in range(PASSES):
             nc.sync.dma_start(out=tab_sc[a][0:P:8, :].bitcast(I32), in_=tab_scales[a].bitcast(I32))
-        load_tab(0)
-        load_tab(1)
+        load_tab(0, 0, T)
+        nc.sync.dma_start(out=gains[:], in_=gain.rearrange("(b p t) -> p b t", b=PASSES, t=PACK))
+        load_w1(1, 0, 1)
+        load_tab(1, 0, T // 2)
         picked_sc = held([P, PASSES, S], U8, "picked_sc")
         for a in range(PASSES):
             nc.vector.tensor_copy(picked_sc[:, a, :], tab_sc[a][:].indirect(picks[:]))
         for r in range(4):
             nc.sync.dma_start(out=v_sc[r:P:32, :, :].bitcast(I32), in_=picked_sc[8 * r : P : 32, :, :].bitcast(I32))
+        load_tab(1, T // 2, T)
         load_scales(w4_sc, 0, w4_scales)
-        nc.sync.dma_start(out=gains[:], in_=gain.rearrange("(b p t) -> p b t", b=PASSES, t=PACK))
-        load_w1(1, 0, 2)
         load_scales(w3_sc, W3_ROW, w3_scales)
         load_w1(0, 1, 1)
         load_w1(1, 1, 2)
@@ -109,12 +112,14 @@ def tile_list_tape_restore_residuals_kernel(
             grouped = held([P, PACK, P, PACK], BF16, "grouped%d%d" % (a, b))
             w1c[(a, b)] = held([P, PASS], U32, "w1c%d%d" % (a, b))
             w1s[(a, b)] = held([P, PASS], U8, "w1s%d%d" % (a, b))
-            parts = len(raw[(a, b)])
-            for u, t_raw in enumerate(raw[(a, b)]):
-                m0, m1 = u * P // parts, (u + 1) * P // parts
-                copies[u](
+            per_load = P // len(raw[(a, b)])
+            for copy_rows, m0, m1 in copies:
+                first = m0 // per_load * per_load
+                copy_rows(
                     out=grouped[:, :, m0:m1, :].rearrange("p t m j -> p m t j"),
-                    in_=t_raw[:].rearrange("p j (m t) -> p m t j", t=PACK),
+                    in_=raw[(a, b)][m0 // per_load][:].rearrange("p j (m t) -> p m t j", t=PACK)[
+                        :, m0 - first : m1 - first, :, :
+                    ],
                 )
             tw = PACK // calls
             for u in range(calls):
@@ -125,15 +130,15 @@ def tile_list_tape_restore_residuals_kernel(
                 )
 
         on_vector, on_scalar = nc.vector.tensor_copy, nc.scalar.copy
-        quantise_w1(0, 0, 1, [on_scalar])
+        quantise_w1(0, 0, 1, [(on_scalar, 0, P)])
         nc.vector.tensor_copy(v[0][:], tab[0][:].bitcast(U32).indirect(picks[:]))
+        quantise_w1(1, 0, 1, [(on_scalar, 0, P)])
         nc.vector.tensor_copy(v[1][:, :HALF], tab[1][:].bitcast(U32).indirect(picks[:, : HALF // 16]))
         nc.vector.tensor_copy(v[1][:, HALF:], tab[1][:].bitcast(U32).indirect(picks[:, HALF // 16 :]))
-        quantise_w1(1, 0, 2, [on_scalar, on_vector])
-        quantise_w1(0, 1, 1, [on_vector])
-        quantise_w1(1, 1, 2, [on_vector, on_vector])
+        quantise_w1(0, 1, 1, [(on_vector, 0, P)])
+        quantise_w1(1, 1, 2, [(on_vector, 0, 64), (on_vector, 64, P)])
 
-        feats = held([P, N_TILES, S], F32, "feats")
+        feats = held([P, N_TILES, S], F32, "feats", tag="tab0")
         for n in range(N_TILES):
             nc.sync.dma_start(out=feats[:, n, :], in_=x0[P * n : P * (n + 1), :])
 
@@ -153,7 +158,7 @@ def tile_list_tape_restore_residuals_kernel(
                         stop=(a, i) == (PASSES - 1, len(ts) - 1),
                     )
 
-        def w3_passes(y, ns, cols):
+        def w3_passes(y, ns, cols, closes=False):
             for a in range(PASSES):
                 for i, n in enumerate(ns):
                     ncols = slice(P * n, P * (n + 1))
@@ -164,10 +169,10 @@ def tile_list_tape_restore_residuals_kernel(
                         rhs=v[a][:, cols].bitcast(FP8X4),
                         rhs_scale=v_sc[:, a, cols],
                         start=False,
-                        stop=False,
+                        stop=closes and (a, i) == (PASSES - 1, len(ns) - 1),
                     )
 
-        def w4_passes(y, b, ns, cols):
+        def w4_passes(y, b, ns, cols, opens=False, closes=False):
             starts = range(cols.start, cols.stop, PIECE)
             for i, n in enumerate(ns):
                 for c0 in starts:
@@ -176,14 +181,15 @@ def tile_list_tape_restore_residuals_kernel(
                         lhsT=w4[:, b, 2 * P * n : 2 * P * (n + 1)].bitcast(FP4X4),
                         lhsT_scale=w4_sc[:, b, P * n : P * (n + 1)],
                         rhs=hc[b][:, c0 : c0 + PIECE].bitcast(FP8X4),
-                        rhs_scale=hs[(b, cols.start)][:, c0 - cols.start : c0 - cols.start + PIECE],
-                        start=b == 0 and i == 0 and c0 == cols.start,
-                        stop=b == PASSES - 1 and i == len(ns) - 1 and c0 == starts[-1],
+                        rhs_scale=hs[(b, c0)],
+                        start=opens and i == 0 and c0 == cols.start,
+                        stop=closes and i == len(ns) - 1 and c0 == starts[-1],
                     )
 
         def quantise_h(b, cols, woven, tag=None):
             plane = held([P, cols.stop - cols.start], U8, "hs%d_%d" % (b, cols.start), tag=tag)
-            hs[(b, cols.start)] = plane
+            for c0 in range(cols.start, cols.stop, PIECE):
+                hs[(b, c0)] = plane[:, c0 - cols.start : c0 - cols.start + PIECE]
             nc.vector.quantize_mx(
                 out=hc[b][:, cols].bitcast(FP8X4), scales=plane[:], in_=woven.rearrange("p j t -> p (j t)")
             )
@@ -195,130 +201,162 @@ def tile_list_tape_restore_residuals_kernel(
                 pages[n][:].indirect(places[:, cols.start // 16 : cols.stop // 16]), values, weight[:, cols], MULT
             )
 
+        def bank(number, shape, name):
+            return psum.tile(shape, F32, tag="bank%d" % number, name=name)
+
         pieces = [slice(0, PIECE), slice(PIECE, 2 * PIECE)]
-        th_first = {}
-        for b in range(PASSES):
-            for i, cols in enumerate(pieces):
-                z = psum.tile([P, PACK, PIECE], F32, tag="bank%d" % (4 * b + i), name="z")
-                z_group(z, b, range(PACK), cols)
-                th_first[(b, i)] = held([P, PIECE, PACK], F32, "th_first%d%d" % (b, i))
-                nc.scalar.activation(
-                    out=th_first[(b, i)][:], in_=z[:].rearrange("p t j -> p j t"), func=ACT.Tanh, scale=-1.0
-                )
-        y_first = []
-        all_n = range(N_TILES)
-        for i, cols in enumerate(pieces):
-            splits = [(0, range(0, 1)), (6, range(1, N_TILES))] if i == 0 else [(7, all_n)]
-            y = [psum.tile([P, len(ns), PIECE], F32, tag="bank%d" % bank, name="y") for bank, ns in splits]
-            for b in range(PASSES):
-                hb = held([P, PIECE, PACK], BF16, "hb%d%d" % (b, i), tag={(0, 0): "grouped11", (0, 1): "raw111"}.get((b, i)))
-                nc.vector.tensor_tensor(
-                    hb[:], th_first[(b, i)][:], gains[:, b : b + 1, :].to_broadcast([P, PIECE, PACK]), MULT
-                )
-                quantise_h(b, cols, hb[:])
-                for bank, (number, ns) in zip(y, splits):
-                    w4_passes(bank, b, ns, cols)
-                    if b == 0:
-                        w3_passes(bank, ns, cols)
-            y_first.extend(y)
+        th_piece = {}
 
-        units = [slice(256, 512), slice(512, 768), slice(768, 896), slice(896, S)]
-        z_banks = [((2, 3), (4, 5)), ((0, 1), (2, 3)), ((0,), (1,)), ((0,), (3,))]
-        y_banks = [(4, 5), (6, 7), (2,), (4,)]
-        ys_psum = {}
+        def tanh_piece(i, b, number):
+            z = bank(number, [P, PACK, PIECE], "z")
+            z_group(z, b, range(PACK), pieces[i])
+            th_piece[(i, b)] = held([P, PIECE, PACK], F32, "thp%d%d" % (i, b))
+            nc.scalar.activation(
+                out=th_piece[(i, b)][:], in_=z[:].rearrange("p t j -> p j t"), func=ACT.Tanh, scale=-1.0
+            )
 
-        def groups(g):
-            per_bank = PASS // (units[g].stop - units[g].start)
-            return [range(i, i + per_bank) for i in range(0, PACK, per_bank)]
+        def gain_piece(i, b, hb):
+            nc.vector.tensor_tensor(
+                hb, th_piece[(i, b)][:], gains[:, b : b + 1, :].to_broadcast([P, PIECE, PACK]), MULT
+            )
 
+        units = {1: slice(256, 512), 2: slice(512, 768), 3: slice(768, 896), 4: slice(896, S)}
         ths, planes_of = {}, {}
 
-        def tanh_bank(g, b, u):
-            bank, ts = z_banks[g][b][u], groups(g)[u]
+        def tanh_bank(g, b, ts, number, tag=None):
             width = units[g].stop - units[g].start
-            z = psum.tile([P, len(ts), width], F32, tag="bank%d" % bank, name="z")
+            z = bank(number, [P, len(ts), width], "z")
             z_group(z, b, ts, units[g])
-            th = held([P, len(ts), width], F32, "th", tag="th%d" % (bank % 2))
+            th = held([P, len(ts), width], F32, "th%d%d%d" % (g, b, ts[0]), tag=tag)
             nc.scalar.activation(out=th[:], in_=z[:], func=ACT.Tanh, scale=-1.0)
             for i, t in enumerate(ts):
                 ths[(g, b, t)] = th[:, i, :]
 
-        def apply_gain(g, b):
-            planes = held([P, PACK, units[g].stop - units[g].start], BF16, "planes%d%d" % (g, b))
+        def apply_gain(g, b, tag=None):
+            planes = held([P, PACK, units[g].stop - units[g].start], BF16, "planes%d%d" % (g, b), tag=tag)
             for t in range(PACK):
                 nc.scalar.activation(
                     out=planes[:, t, :], in_=ths[(g, b, t)], func=ACT.Copy, scale=gains[:, b, t : t + 1]
                 )
             planes_of[(g, b)] = planes
 
-        def weave(g, b):
-            cols = units[g]
-            width = cols.stop - cols.start
-            first = (g, b) == (0, 0)
-            planes = planes_of[(g, b)]
-            woven = held([P, width, PACK], BF16, "woven%d%d" % (g, b), tag="grouped11" if first else None)
+        def weave(g, b, tag=None):
+            woven = held([P, units[g].stop - units[g].start, PACK], BF16, "woven%d%d" % (g, b), tag=tag)
             nc.scalar.copy(
                 out=woven[:].rearrange("p (c i) t -> p c t i", i=4),
-                in_=planes[:].rearrange("p t (c i) -> p c t i", i=4),
+                in_=planes_of[(g, b)][:].rearrange("p t (c i) -> p c t i", i=4),
             )
-            quantise_h(b, cols, woven[:], "hb10" if first else None)
-            if first:
-                return
-            for bank, ns in zip(y_banks[g], groups(g)):
-                if (g, ns[0]) not in ys_psum:
-                    y = psum.tile([P, len(ns), width], F32, tag="bank%d" % bank, name="y")
-                    ys_psum[(g, ns[0])] = y
-                    w4_passes(y, 0, ns, cols)
-                    w3_passes(y, ns, cols)
-                if b == 1:
-                    w4_passes(ys_psum[(g, ns[0])], 1, ns, cols)
+            quantise_h(b, units[g], woven[:])
 
-        def place(values, bank, ns, cols):
-            nc.scalar.activation(out=values, in_=bank, func=ACT.Abs)
+        def open_y(number, ns, cols):
+            y = bank(number, [P, len(ns), cols.stop - cols.start], "y")
+            w4_passes(y, 0, ns, cols, opens=True)
+            w3_passes(y, ns, cols)
+            return y
+
+        def close_y(y, ns, cols):
+            w4_passes(y, 1, ns, cols, closes=True)
+
+        def whole_y(number, ns, cols):
+            y = bank(number, [P, len(ns), cols.stop - cols.start], "y")
+            w4_passes(y, 1, ns, cols, opens=True)
+            w4_passes(y, 0, ns, cols)
+            w3_passes(y, ns, cols, closes=True)
+            return y
+
+        def evacuate(values, y):
+            nc.scalar.activation(out=values, in_=y, func=ACT.Abs)
+
+        def place(y, rows, ns, cols, tag=None, values=None):
+            if values is None:
+                values = held([P, len(ns), cols.stop - cols.start], F32, "ys%d_%d" % (cols.start, ns[0]), tag=tag)[:]
+            evacuate(values, y[:, rows, :])
             for i, n in enumerate(ns):
                 scatter(n, values[:, i, :], cols)
+            return values
 
-        def place_unit(g, n0, n1, values=None):
-            cols = units[g]
-            per_bank = len(groups(g)[0])
-            first = n0 // per_bank * per_bank
-            if values is None:
-                values = held([P, n1 - n0, cols.stop - cols.start], F32, "ys%d%d" % (g, n0))[:]
-            place(values, ys_psum[(g, first)][:, n0 - first : n1 - first, :], range(n0, n1), cols)
+        low, high, every = range(0, 2), range(2, 4), range(4)
+        both = slice(0, 2)
 
-        def first_rows(name, tag, y, n0, n1, rows, cols):
-            place(held([P, n1 - n0, PIECE], F32, name, tag=tag)[:], y[:, rows, :], range(n0, n1), cols)
+        tanh_piece(0, 0, 0)
+        tanh_piece(1, 0, 1)
+        tanh_bank(1, 0, low, 2, "th0")
+        tanh_bank(1, 0, high, 3, "th1")
+        apply_gain(1, 0)
+        tanh_bank(2, 0, low, 6, "th2")
+        tanh_bank(2, 0, high, 7, "th3")
+        tanh_piece(0, 1, 4)
+        tanh_piece(1, 1, 5)
 
-        last = len(units) - 1
-        steps = [(g, b) for g in range(last + 1) for b in range(PASSES)]
-        tanh_bank(0, 0, 0)
-        tanh_bank(0, 0, 1)
-        for (g, b), ahead in zip(steps, steps[1:] + [None]):
-            apply_gain(g, b)
-            if ahead and (g, b) != (0, 0):
-                tanh_bank(*ahead, 0)
-            weave(g, b)
-            if (g, b) == (0, 0):
-                first_rows("ys_first0", None, y_first[0], 0, 1, slice(0, 1), pieces[0])
-                first_rows("ys_first1", "th_first11", y_first[1], 1, 4, slice(0, 3), pieces[0])
-                tanh_bank(*ahead, 0)
-            if ahead and len(groups(ahead[0])) == 2:
-                tanh_bank(*ahead, 1)
-            wide = g > 0 and len(groups(g - 1)) == 2
-            if (g, b) == (0, 0):
-                first_rows("ys_first2", None, y_first[2], 0, 2, slice(0, 2), pieces[1])
-            elif g == 0:
-                first_rows("ys_first3", "planes01", y_first[2], 2, 4, slice(2, 4), pieces[1])
-            elif b == 0:
-                place_unit(g - 1, *((2, 3) if wide else (0, 2)))
-            else:
-                late = held([P, QUARTER + (N_TILES * S if g == last else 0)], F32, "late%d" % g, tag="planes%d1" % g)
-                n0 = 3 if wide else 2
-                place_unit(g - 1, n0, N_TILES, late[:, :QUARTER].rearrange("p (n j) -> p n j", n=N_TILES - n0))
-            if b == 1 and len(groups(g)) == 2:
-                place_unit(g, 0, 2)
+        hb0 = held([P, 2, PIECE, PACK], BF16, "hb0", tag="grouped11")
+        hb1 = [held([P, PIECE, PACK], BF16, "hb10")]
+        gain_piece(0, 0, hb0[:, 0, :, :])
+        gain_piece(1, 0, hb0[:, 1, :, :])
+        quantise_h(0, pieces[0], hb0[:, 0, :, :])
+        y_a0 = open_y(0, low, pieces[0])
+        gain_piece(0, 1, hb1[0][:])
+        quantise_h(0, pieces[1], hb0[:, 1, :, :])
+        quantise_h(1, pieces[0], hb1[0][:])
+        close_y(y_a0, low, pieces[0])
+        y_a1 = whole_y(1, high, pieces[0])
+        hb1.append(held([P, PIECE, PACK], BF16, "hb11", tag="hb10"))
+        gain_piece(1, 1, hb1[1][:])
+        first = place(y_a0, slice(0, 1), range(0, 1), pieces[0])
+        place(y_a0, slice(1, 2), range(1, 2), pieces[0])
+        quantise_h(1, pieces[1], hb1[1][:])
+        y_b = whole_y(6, every, pieces[1])
+        place(y_a1, both, high, pieces[0])
+        apply_gain(2, 0, tag="thp01")
+        tanh_bank(1, 1, low, 2, "th0")
+        tanh_bank(1, 1, high, 3, "th1")
+        weave(1, 0, tag="hb10")
+        y_1 = [open_y(4, low, units[1]), open_y(5, high, units[1])]
 
-        sizes = late[:, QUARTER:].rearrange("p (n m) -> p n m", n=N_TILES)
+        apply_gain(1, 1)
+        place(y_b, slice(0, 2), low, pieces[1], tag="th0")
+        weave(1, 1)
+        close_y(y_1[0], low, units[1])
+        close_y(y_1[1], high, units[1])
+        held_b = held([P, 2, PIECE], F32, "held_b", tag="planes11")
+        place(y_b, slice(2, 4), high, pieces[1], values=held_b[:])
+
+        second = place(y_1[0], both, low, units[1])
+        weave(2, 0)
+        y_2 = [open_y(2, low, units[2]), open_y(3, high, units[2])]
+        tanh_bank(2, 1, low, 0, "th2")
+        tanh_bank(2, 1, high, 1, "th3")
+        apply_gain(2, 1)
+        place(y_1[1], slice(0, 1), range(2, 3), units[1], tag="th2")
+        weave(2, 1)
+        close_y(y_2[0], low, units[2])
+        close_y(y_2[1], high, units[2])
+        place(y_1[1], slice(1, 2), range(3, 4), units[1], tag="planes21")
+
+        tanh_bank(3, 0, every, 6, "th3")
+        tanh_bank(3, 1, every, 0, "th0")
+        third = place(y_2[0], both, low, units[2])
+        apply_gain(3, 0)
+        weave(3, 0)
+        y_c = open_y(7, every, units[3])
+        apply_gain(3, 1)
+        place(y_2[1], slice(0, 1), range(2, 3), units[2], tag="th0")
+        weave(3, 1)
+        close_y(y_c, every, units[3])
+        tanh_bank(4, 0, every, 1, "th3")
+        tanh_bank(4, 1, every, 4, "th1")
+        place(y_2[1], slice(1, 2), range(3, 4), units[2], tag="planes31")
+        apply_gain(4, 0)
+        weave(4, 0)
+        y_d = open_y(5, every, units[4])
+        place(y_c, slice(0, 1), range(0, 1), units[3])
+        apply_gain(4, 1)
+        weave(4, 1)
+        close_y(y_d, every, units[4])
+
+        late = held([P, 3 * QUARTER + N_TILES * S], F32, "late", tag="planes41")
+        ends = late[:, : 3 * QUARTER].rearrange("p (n j) -> p n j", n=3)
+        sizes = late[:, 3 * QUARTER :].rearrange("p (n m) -> p n m", n=N_TILES)
+        last_quarter = slice(S - QUARTER, S)
 
         def size_of_features(n):
             nc.scalar.activation(out=sizes[:, n, :], in_=feats[:, n, :], func=ACT.Abs)
@@ -330,13 +368,18 @@ def tile_list_tape_restore_residuals_kernel(
                 nc.vector.tensor_tensor(feats[:, n, part], pages[n][:, part], sizes[:, n, part], MULT)
                 nc.sync.dma_start(out=out[P * n : P * (n + 1), part], in_=feats[:, n, part])
 
+        evacuate(ends[:, :, :PIECE], y_c[:, 1:4, :])
+        scatter(1, ends[:, 0, :PIECE], units[3])
+        scatter(2, ends[:, 1, :PIECE], units[3])
         size_of_features(0)
-        place_unit(last, 0, 2)
+        place(y_d, both, low, units[4])
         weigh_and_store(0, 1)
-        place_unit(last, 2, 3)
-        for n in (1, 2):
-            size_of_features(n)
-            weigh_and_store(n, 1)
+        size_of_features(1)
+        place(y_d, slice(2, 3), range(2, 3), units[4])
+        weigh_and_store(1, 1)
+        size_of_features(2)
+        weigh_and_store(2, 1)
         size_of_features(3)
-        place_unit(last, 3, 4)
+        evacuate(ends[:, 2, PIECE:], y_d[:, 3, :])
+        scatter(3, ends[:, 2, :], last_quarter)
         weigh_and_store(3, 4)

@@ -204,30 +204,35 @@ def tile_list_tape_restore_residuals_kernel(
         def bank(number, shape, name):
             return psum.tile(shape, F32, tag="bank%d" % number, name=name)
 
-        pieces = [slice(0, PIECE), slice(PIECE, 2 * PIECE)]
+        pieces = [slice(PIECE * i, PIECE * (i + 1)) for i in range(4)]
         th_piece = {}
 
-        def tanh_piece(i, b, number):
+        def tanh_piece(i, b, number, th=None):
             z = bank(number, [P, PACK, PIECE], "z")
             z_group(z, b, range(PACK), pieces[i])
-            th_piece[(i, b)] = held([P, PIECE, PACK], F32, "thp%d%d" % (i, b))
+            th_piece[(i, b)] = held([P, PIECE, PACK], F32, "thp%d%d" % (i, b))[:] if th is None else th
             nc.scalar.activation(
-                out=th_piece[(i, b)][:], in_=z[:].rearrange("p t j -> p j t"), func=ACT.Tanh, scale=-1.0
+                out=th_piece[(i, b)], in_=z[:].rearrange("p t j -> p j t"), func=ACT.Tanh, scale=-1.0
             )
+
+        def gain_on_vector(hb, th, b):
+            nc.vector.tensor_tensor(hb, th, gains[:, b : b + 1, :].to_broadcast(list(th.shape)), MULT)
 
         def gain_piece(i, b, hb):
-            nc.vector.tensor_tensor(
-                hb, th_piece[(i, b)][:], gains[:, b : b + 1, :].to_broadcast([P, PIECE, PACK]), MULT
-            )
+            gain_on_vector(hb, th_piece[(i, b)], b)
 
-        units = {1: slice(256, 512), 2: slice(512, 768), 3: slice(768, 896), 4: slice(896, S)}
+        units = {g: slice(QUARTER * g, QUARTER * (g + 1)) for g in range(1, 4)}
         ths, planes_of = {}, {}
 
-        def tanh_bank(g, b, ts, number, tag=None):
-            width = units[g].stop - units[g].start
-            z = bank(number, [P, len(ts), width], "z")
-            z_group(z, b, ts, units[g])
-            th = held([P, len(ts), width], F32, "th%d%d%d" % (g, b, ts[0]), tag=tag)
+        zs = {}
+
+        def z_bank(g, b, ts, number):
+            zs[(g, b, ts[0])] = bank(number, [P, len(ts), QUARTER], "z")
+            z_group(zs[(g, b, ts[0])], b, ts, units[g])
+
+        def tanh_bank(g, b, ts, tag=None):
+            z = zs[(g, b, ts[0])]
+            th = held([P, len(ts), QUARTER], F32, "th%d%d%d" % (g, b, ts[0]), tag=tag)
             nc.scalar.activation(out=th[:], in_=z[:], func=ACT.Tanh, scale=-1.0)
             for i, t in enumerate(ts):
                 ths[(g, b, t)] = th[:, i, :]
@@ -280,11 +285,14 @@ def tile_list_tape_restore_residuals_kernel(
 
         tanh_piece(0, 0, 0)
         tanh_piece(1, 0, 1)
-        tanh_bank(1, 0, low, 2, "th0")
-        tanh_bank(1, 0, high, 3, "th1")
-        apply_gain(1, 0)
-        tanh_bank(2, 0, low, 6, "th2")
-        tanh_bank(2, 0, high, 7, "th3")
+        th_second = held([P, QUARTER, PACK], F32, "th_second")
+        tanh_piece(2, 0, 2, th_second[:, :PIECE, :])
+        tanh_piece(3, 0, 3, th_second[:, PIECE:, :])
+        z_bank(2, 0, low, 6)
+        z_bank(2, 0, high, 7)
+        tanh_bank(2, 0, low, "th2")
+        tanh_bank(2, 0, high, "th3")
+        apply_gain(2, 0)
         tanh_piece(0, 1, 4)
         tanh_piece(1, 1, 5)
 
@@ -298,88 +306,103 @@ def tile_list_tape_restore_residuals_kernel(
         quantise_h(0, pieces[1], hb0[:, 1, :, :])
         quantise_h(1, pieces[0], hb1[0][:])
         close_y(y_a0, low, pieces[0])
-        y_a1 = whole_y(1, high, pieces[0])
+        y_a1 = whole_y(6, high, pieces[0])
+        z_bank(1, 1, low, 4)
+        z_bank(1, 1, high, 5)
         hb1.append(held([P, PIECE, PACK], BF16, "hb11", tag="hb10"))
         gain_piece(1, 1, hb1[1][:])
         first = place(y_a0, slice(0, 1), range(0, 1), pieces[0])
-        place(y_a0, slice(1, 2), range(1, 2), pieces[0])
         quantise_h(1, pieces[1], hb1[1][:])
-        y_b = whole_y(6, every, pieces[1])
+        place(y_a0, slice(1, 2), range(1, 2), pieces[0])
+        y_b = [whole_y(1, low, pieces[1]), whole_y(7, high, pieces[1])]
+        hb_second = held([P, QUARTER, PACK], BF16, "hb_second", tag="hb10")
+        gain_on_vector(hb_second[:], th_second[:], 0)
         place(y_a1, both, high, pieces[0])
-        apply_gain(2, 0, tag="thp01")
-        tanh_bank(1, 1, low, 2, "th0")
-        tanh_bank(1, 1, high, 3, "th1")
-        weave(1, 0, tag="hb10")
-        y_1 = [open_y(4, low, units[1]), open_y(5, high, units[1])]
+        quantise_h(0, units[1], hb_second[:])
+        z_bank(2, 1, low, 0)
+        z_bank(2, 1, high, 6)
+        y_1 = [open_y(2, low, units[1]), open_y(3, high, units[1])]
+        weave(2, 0, tag="thp01")
+        tanh_bank(1, 1, low, "th0")
+        tanh_bank(1, 1, high, "th1")
 
         apply_gain(1, 1)
-        place(y_b, slice(0, 2), low, pieces[1], tag="th0")
+        place(y_b[0], both, low, pieces[1], tag="th0")
         weave(1, 1)
         close_y(y_1[0], low, units[1])
         close_y(y_1[1], high, units[1])
-        held_b = held([P, 2, PIECE], F32, "held_b", tag="planes11")
-        place(y_b, slice(2, 4), high, pieces[1], values=held_b[:])
-
-        second = place(y_1[0], both, low, units[1])
-        weave(2, 0)
-        y_2 = [open_y(2, low, units[2]), open_y(3, high, units[2])]
-        tanh_bank(2, 1, low, 0, "th2")
-        tanh_bank(2, 1, high, 1, "th3")
+        place(y_b[1], both, high, pieces[1], tag="planes11")
+        tanh_bank(2, 1, low, "th2")
+        tanh_bank(2, 1, high, "th3")
+        z_bank(3, 0, low, 1)
+        z_bank(3, 0, high, 7)
+        z_bank(3, 1, low, 0)
+        z_bank(3, 1, high, 6)
+        y_2 = [open_y(4, low, units[2]), open_y(5, high, units[2])]
         apply_gain(2, 1)
-        place(y_1[1], slice(0, 1), range(2, 3), units[1], tag="th2")
+        second = place(y_1[0], slice(0, 1), range(0, 1), units[1], tag="th2")
         weave(2, 1)
         close_y(y_2[0], low, units[2])
         close_y(y_2[1], high, units[2])
-        place(y_1[1], slice(1, 2), range(3, 4), units[1], tag="planes21")
+        rest_1 = held([P, 2, QUARTER], F32, "rest_1", tag="planes21")
+        place(y_1[0], slice(1, 2), range(1, 2), units[1], values=rest_1[:, 0:1, :])
+        place(y_1[1], slice(0, 1), range(2, 3), units[1], values=rest_1[:, 1:2, :])
 
-        tanh_bank(3, 0, every, 6, "th3")
-        tanh_bank(3, 1, every, 0, "th0")
-        third = place(y_2[0], both, low, units[2])
+        tanh_bank(3, 0, low, "th3")
+        tanh_bank(3, 0, high, "th0")
         apply_gain(3, 0)
+        third = place(y_2[0], both, low, units[2], tag="th3")
         weave(3, 0)
-        y_c = open_y(7, every, units[3])
-        apply_gain(3, 1)
+        y_3 = [open_y(2, low, units[3]), open_y(7, high, units[3])]
+        tanh_bank(3, 1, low, "th2")
+        tanh_bank(3, 1, high, "planes30")
         place(y_2[1], slice(0, 1), range(2, 3), units[2], tag="th0")
+        apply_gain(3, 1)
         weave(3, 1)
-        close_y(y_c, every, units[3])
-        tanh_bank(4, 0, every, 1, "th3")
-        tanh_bank(4, 1, every, 4, "th1")
-        place(y_2[1], slice(1, 2), range(3, 4), units[2], tag="planes31")
-        apply_gain(4, 0)
-        weave(4, 0)
-        y_d = open_y(5, every, units[4])
-        place(y_c, slice(0, 1), range(0, 1), units[3])
-        apply_gain(4, 1)
-        weave(4, 1)
-        close_y(y_d, every, units[4])
+        close_y(y_3[0], low, units[3])
+        close_y(y_3[1], high, units[3])
 
-        late = held([P, 3 * QUARTER + N_TILES * S], F32, "late", tag="planes41")
-        ends = late[:, : 3 * QUARTER].rearrange("p (n j) -> p n j", n=3)
-        sizes = late[:, 3 * QUARTER :].rearrange("p (n m) -> p n m", n=N_TILES)
-        last_quarter = slice(S - QUARTER, S)
+        late = held([P, 2 * QUARTER + N_TILES * S], F32, "late", tag="planes31")
+        ends = late[:, : 2 * QUARTER].rearrange("p (n j) -> p n j", n=2)
+        sizes = late[:, 2 * QUARTER :].rearrange("p (n m) -> p n m", n=N_TILES)
 
         def size_of_features(n):
             nc.scalar.activation(out=sizes[:, n, :], in_=feats[:, n, :], func=ACT.Abs)
 
-        def weigh_and_store(n, parts):
-            width = S // parts
-            for u in range(parts):
-                part = slice(u * width, (u + 1) * width)
-                nc.vector.tensor_tensor(feats[:, n, part], pages[n][:, part], sizes[:, n, part], MULT)
-                nc.sync.dma_start(out=out[P * n : P * (n + 1), part], in_=feats[:, n, part])
+        def weigh_and_store(n, c0, c1, engine):
+            part = slice(c0, c1)
+            engine.tensor_tensor(feats[:, n, part], pages[n][:, part], sizes[:, n, part], MULT)
+            nc.sync.dma_start(out=out[P * n : P * (n + 1), part], in_=feats[:, n, part])
 
-        evacuate(ends[:, :, :PIECE], y_c[:, 1:4, :])
-        scatter(1, ends[:, 0, :PIECE], units[3])
-        scatter(2, ends[:, 1, :PIECE], units[3])
+        def scatter_copy(n, values, cols):
+            nc.vector.tensor_copy(pages[n][:].indirect(places[:, cols.start // 16 : cols.stop // 16]), values)
+
+        weighed = held([P, N_TILES + 1, QUARTER], F32, "weighed")
+        evacuate(ends[:, 1, :], y_2[1][:, 1, :])
+        nc.vector.tensor_tensor(weighed[:, 3, :], ends[:, 1, :], weight[:, units[2]], MULT)
+        place(y_1[1], slice(1, 2), range(3, 4), units[1], values=ends[:, 0:1, :])
         size_of_features(0)
-        place(y_d, both, low, units[4])
-        weigh_and_store(0, 1)
+        ys_3 = held([P, N_TILES, QUARTER], F32, "ys_3")
+        evacuate(ys_3[:, 0:2, :], y_3[0][:])
+        evacuate(ys_3[:, 2:4, :], y_3[1][:])
+        nc.vector.tensor_tensor(
+            weighed[:, 0:2, :],
+            ys_3[:, 0:2, :],
+            weight[:, units[3]].unsqueeze(1).to_broadcast([P, 2, QUARTER]),
+            MULT,
+        )
+        scatter_copy(0, weighed[:, 0, :], units[3])
+        nc.gpsimd.tensor_tensor(weighed[:, 2, :], ys_3[:, 2, :], weight[:, units[3]], MULT)
+        nc.gpsimd.tensor_tensor(weighed[:, 4, :], ys_3[:, 3, :], weight[:, units[3]], MULT)
         size_of_features(1)
-        place(y_d, slice(2, 3), range(2, 3), units[4])
-        weigh_and_store(1, 1)
+        weigh_and_store(0, 0, S, nc.gpsimd)
+        scatter_copy(1, weighed[:, 1, :], units[3])
         size_of_features(2)
-        weigh_and_store(2, 1)
+        weigh_and_store(1, 0, S, nc.gpsimd)
+        scatter_copy(2, weighed[:, 2, :], units[3])
+        weigh_and_store(2, 0, 3 * QUARTER, nc.gpsimd)
+        scatter_copy(3, weighed[:, 3:5, :].rearrange("p n j -> p (n j)"), slice(HALF, S))
         size_of_features(3)
-        evacuate(ends[:, 2, PIECE:], y_d[:, 3, :])
-        scatter(3, ends[:, 2, :], last_quarter)
-        weigh_and_store(3, 4)
+        weigh_and_store(2, 3 * QUARTER, S, nc.vector)
+        for c0 in range(0, S, QUARTER):
+            weigh_and_store(3, c0, c0 + QUARTER, nc.vector)

@@ -197,9 +197,7 @@ def tile_list_tape_restore_residuals_kernel(
         pages = [held([P, S], F32, "page%d" % n) for n in range(N_TILES)]
 
         def scatter(n, values, cols):
-            nc.vector.tensor_tensor(
-                pages[n][:].indirect(places[:, cols.start // 16 : cols.stop // 16]), values, weight[:, cols], MULT
-            )
+            nc.vector.tensor_copy(pages[n][:].indirect(places[:, cols.start // 16 : cols.stop // 16]), values)
 
         def bank(number, shape, name):
             return psum.tile(shape, F32, tag="bank%d" % number, name=name)
@@ -215,8 +213,8 @@ def tile_list_tape_restore_residuals_kernel(
                 out=th_piece[(i, b)], in_=z[:].rearrange("p t j -> p j t"), func=ACT.Tanh, scale=-1.0
             )
 
-        def gain_on_vector(hb, th, b):
-            nc.vector.tensor_tensor(hb, th, gains[:, b : b + 1, :].to_broadcast(list(th.shape)), MULT)
+        def gain_on_vector(hb, th, b, engine=nc.vector):
+            engine.tensor_tensor(hb, th, gains[:, b : b + 1, :].to_broadcast(list(th.shape)), MULT)
 
         def gain_piece(i, b, hb):
             gain_on_vector(hb, th_piece[(i, b)], b)
@@ -277,6 +275,8 @@ def tile_list_tape_restore_residuals_kernel(
                 values = held([P, len(ns), cols.stop - cols.start], F32, "ys%d_%d" % (cols.start, ns[0]), tag=tag)[:]
             evacuate(values, y[:, rows, :])
             for i, n in enumerate(ns):
+                nc.gpsimd.tensor_tensor(values[:, i, :], values[:, i, :], weight[:, cols], MULT)
+            for i, n in enumerate(ns):
                 scatter(n, values[:, i, :], cols)
             return values
 
@@ -311,13 +311,17 @@ def tile_list_tape_restore_residuals_kernel(
         z_bank(1, 1, high, 5)
         hb1.append(held([P, PIECE, PACK], BF16, "hb11", tag="hb10"))
         gain_piece(1, 1, hb1[1][:])
-        first = place(y_a0, slice(0, 1), range(0, 1), pieces[0])
+        first = held([P, 2, PIECE], F32, "first")
+        evacuate(first[:], y_a0[:])
+        nc.vector.tensor_tensor(first[:], first[:], weight[:, pieces[0]].unsqueeze(1).to_broadcast([P, 2, PIECE]), MULT)
         quantise_h(1, pieces[1], hb1[1][:])
-        place(y_a0, slice(1, 2), range(1, 2), pieces[0])
+        for n in low:
+            scatter(n, first[:, n, :], pieces[0])
         y_b = [whole_y(1, low, pieces[1]), whole_y(7, high, pieces[1])]
-        hb_second = held([P, QUARTER, PACK], BF16, "hb_second", tag="hb10")
-        gain_on_vector(hb_second[:], th_second[:], 0)
+        hb_second = held([P, QUARTER, PACK], BF16, "hb_second", tag="thp11")
         place(y_a1, both, high, pieces[0])
+        for c0 in (0, PIECE):
+            gain_on_vector(hb_second[:, c0 : c0 + PIECE, :], th_second[:, c0 : c0 + PIECE, :], 0, nc.gpsimd)
         quantise_h(0, units[1], hb_second[:])
         z_bank(2, 1, low, 0)
         z_bank(2, 1, high, 6)
@@ -327,11 +331,13 @@ def tile_list_tape_restore_residuals_kernel(
         tanh_bank(1, 1, high, "th1")
 
         apply_gain(1, 1)
-        place(y_b[0], both, low, pieces[1], tag="th0")
+        place(y_b[0], slice(0, 1), range(0, 1), pieces[1], tag="th0")
         weave(1, 1)
         close_y(y_1[0], low, units[1])
         close_y(y_1[1], high, units[1])
-        place(y_b[1], both, high, pieces[1], tag="planes11")
+        rest_b = held([P, 3, PIECE], F32, "rest_b", tag="planes11")
+        place(y_b[0], slice(1, 2), range(1, 2), pieces[1], values=rest_b[:, 0:1, :])
+        place(y_b[1], both, high, pieces[1], values=rest_b[:, 1:3, :])
         tanh_bank(2, 1, low, "th2")
         tanh_bank(2, 1, high, "th3")
         z_bank(3, 0, low, 1)
@@ -374,35 +380,20 @@ def tile_list_tape_restore_residuals_kernel(
             engine.tensor_tensor(feats[:, n, part], pages[n][:, part], sizes[:, n, part], MULT)
             nc.sync.dma_start(out=out[P * n : P * (n + 1), part], in_=feats[:, n, part])
 
-        def scatter_copy(n, values, cols):
-            nc.vector.tensor_copy(pages[n][:].indirect(places[:, cols.start // 16 : cols.stop // 16]), values)
-
-        weighed = held([P, N_TILES + 1, QUARTER], F32, "weighed")
-        evacuate(ends[:, 1, :], y_2[1][:, 1, :])
-        nc.vector.tensor_tensor(weighed[:, 3, :], ends[:, 1, :], weight[:, units[2]], MULT)
         place(y_1[1], slice(1, 2), range(3, 4), units[1], values=ends[:, 0:1, :])
+        place(y_2[1], slice(1, 2), range(3, 4), units[2], values=ends[:, 1:2, :])
         size_of_features(0)
         ys_3 = held([P, N_TILES, QUARTER], F32, "ys_3")
         evacuate(ys_3[:, 0:2, :], y_3[0][:])
         evacuate(ys_3[:, 2:4, :], y_3[1][:])
-        nc.vector.tensor_tensor(
-            weighed[:, 0:2, :],
-            ys_3[:, 0:2, :],
-            weight[:, units[3]].unsqueeze(1).to_broadcast([P, 2, QUARTER]),
-            MULT,
-        )
-        scatter_copy(0, weighed[:, 0, :], units[3])
-        nc.gpsimd.tensor_tensor(weighed[:, 2, :], ys_3[:, 2, :], weight[:, units[3]], MULT)
-        nc.gpsimd.tensor_tensor(weighed[:, 4, :], ys_3[:, 3, :], weight[:, units[3]], MULT)
-        size_of_features(1)
+        for n in every:
+            nc.gpsimd.tensor_tensor(ys_3[:, n, :], ys_3[:, n, :], weight[:, units[3]], MULT)
+        for n in range(1, N_TILES):
+            size_of_features(n)
+        for n in every:
+            scatter(n, ys_3[:, n, :], units[3])
         weigh_and_store(0, 0, S, nc.gpsimd)
-        scatter_copy(1, weighed[:, 1, :], units[3])
-        size_of_features(2)
         weigh_and_store(1, 0, S, nc.gpsimd)
-        scatter_copy(2, weighed[:, 2, :], units[3])
-        weigh_and_store(2, 0, 3 * QUARTER, nc.gpsimd)
-        scatter_copy(3, weighed[:, 3:5, :].rearrange("p n j -> p (n j)"), slice(HALF, S))
-        size_of_features(3)
-        weigh_and_store(2, 3 * QUARTER, S, nc.vector)
+        weigh_and_store(2, 0, S, nc.vector)
         for c0 in range(0, S, QUARTER):
             weigh_and_store(3, c0, c0 + QUARTER, nc.vector)

@@ -25,6 +25,7 @@ HALF = S // 2
 PIECE = 128
 QUARTER = 256
 W3_ROW = 8
+SIZE_AT = (0, 1, 0, 2)
 
 
 def tile_list_tape_restore_residuals_kernel(
@@ -197,6 +198,11 @@ def tile_list_tape_restore_residuals_kernel(
         pages = [held([P, S], F32, "page%d" % n) for n in range(N_TILES)]
 
         def scatter(n, values, cols):
+            nc.vector.tensor_tensor(
+                pages[n][:].indirect(places[:, cols.start // 16 : cols.stop // 16]), values, weight[:, cols], MULT
+            )
+
+        def scatter_copy(n, values, cols):
             nc.vector.tensor_copy(pages[n][:].indirect(places[:, cols.start // 16 : cols.stop // 16]), values)
 
         def bank(number, shape, name):
@@ -243,13 +249,13 @@ def tile_list_tape_restore_residuals_kernel(
                 )
             planes_of[(g, b)] = planes
 
-        def weave(g, b, tag=None):
+        def weave(g, b, tag=None, plane_tag=None):
             woven = held([P, units[g].stop - units[g].start, PACK], BF16, "woven%d%d" % (g, b), tag=tag)
             nc.scalar.copy(
                 out=woven[:].rearrange("p (c i) t -> p c t i", i=4),
                 in_=planes_of[(g, b)][:].rearrange("p t (c i) -> p c t i", i=4),
             )
-            quantise_h(b, units[g], woven[:])
+            quantise_h(b, units[g], woven[:], plane_tag)
 
         def open_y(number, ns, cols):
             y = bank(number, [P, len(ns), cols.stop - cols.start], "y")
@@ -274,8 +280,6 @@ def tile_list_tape_restore_residuals_kernel(
             if values is None:
                 values = held([P, len(ns), cols.stop - cols.start], F32, "ys%d_%d" % (cols.start, ns[0]), tag=tag)[:]
             evacuate(values, y[:, rows, :])
-            for i, n in enumerate(ns):
-                nc.gpsimd.tensor_tensor(values[:, i, :], values[:, i, :], weight[:, cols], MULT)
             for i, n in enumerate(ns):
                 scatter(n, values[:, i, :], cols)
             return values
@@ -316,17 +320,24 @@ def tile_list_tape_restore_residuals_kernel(
         nc.vector.tensor_tensor(first[:], first[:], weight[:, pieces[0]].unsqueeze(1).to_broadcast([P, 2, PIECE]), MULT)
         quantise_h(1, pieces[1], hb1[1][:])
         for n in low:
-            scatter(n, first[:, n, :], pieces[0])
+            scatter_copy(n, first[:, n, :], pieces[0])
         y_b = [whole_y(1, low, pieces[1]), whole_y(7, high, pieces[1])]
-        hb_second = held([P, QUARTER, PACK], BF16, "hb_second", tag="thp11")
-        place(y_a1, both, high, pieces[0])
+        raw_high = held([P, 2, PIECE], F32, "raw_high")
+        first_high = held([P, 2, PIECE], F32, "first_high")
+        evacuate(raw_high[:], y_a1[:])
+        nc.vector.tensor_tensor(
+            first_high[:], raw_high[:], weight[:, pieces[0]].unsqueeze(1).to_broadcast([P, 2, PIECE]), MULT
+        )
+        for n in high:
+            scatter_copy(n, first_high[:, n - 2, :], pieces[0])
+        hb_second = held([P, QUARTER, PACK], BF16, "hb_second", tag="raw_high")
         for c0 in (0, PIECE):
             gain_on_vector(hb_second[:, c0 : c0 + PIECE, :], th_second[:, c0 : c0 + PIECE, :], 0, nc.gpsimd)
         quantise_h(0, units[1], hb_second[:])
         z_bank(2, 1, low, 0)
         z_bank(2, 1, high, 6)
         y_1 = [open_y(2, low, units[1]), open_y(3, high, units[1])]
-        weave(2, 0, tag="thp01")
+        weave(2, 0, tag="thp01", plane_tag="th_second")
         tanh_bank(1, 1, low, "th0")
         tanh_bank(1, 1, high, "th1")
 
@@ -368,32 +379,39 @@ def tile_list_tape_restore_residuals_kernel(
         close_y(y_3[0], low, units[3])
         close_y(y_3[1], high, units[3])
 
-        late = held([P, 2 * QUARTER + N_TILES * S], F32, "late", tag="planes31")
+        late = held([P, 2 * QUARTER + 3 * S], F32, "late", tag="planes31")
         ends = late[:, : 2 * QUARTER].rearrange("p (n j) -> p n j", n=2)
-        sizes = late[:, 2 * QUARTER :].rearrange("p (n m) -> p n m", n=N_TILES)
+        sizes = late[:, 2 * QUARTER :].rearrange("p (n m) -> p n m", n=3)
 
         def size_of_features(n):
-            nc.scalar.activation(out=sizes[:, n, :], in_=feats[:, n, :], func=ACT.Abs)
+            nc.scalar.activation(out=sizes[:, SIZE_AT[n], :], in_=feats[:, n, :], func=ACT.Abs)
 
-        def weigh_and_store(n, c0, c1, engine):
-            part = slice(c0, c1)
-            engine.tensor_tensor(feats[:, n, part], pages[n][:, part], sizes[:, n, part], MULT)
-            nc.sync.dma_start(out=out[P * n : P * (n + 1), part], in_=feats[:, n, part])
+        def weigh_and_store(n, c0, c1, engine, product):
+            engine.tensor_tensor(product, pages[n][:, c0:c1], sizes[:, SIZE_AT[n], c0:c1], MULT)
+            nc.sync.dma_start(out=out[P * n : P * (n + 1), c0:c1], in_=product)
 
-        place(y_1[1], slice(1, 2), range(3, 4), units[1], values=ends[:, 0:1, :])
-        place(y_2[1], slice(1, 2), range(3, 4), units[2], values=ends[:, 1:2, :])
+        evacuate(ends[:, 0, :], y_1[1][:, 1, :])
+        evacuate(ends[:, 1, :], y_2[1][:, 1, :])
+        nc.vector.tensor_tensor(ends[:, 0, :], ends[:, 0, :], weight[:, units[1]], MULT)
+        weighed = held([P, QUARTER], F32, "weighed", tag="woven31")
+        nc.gpsimd.tensor_tensor(weighed[:], ends[:, 1, :], weight[:, units[2]], MULT)
+        scatter_copy(3, ends[:, 0, :], units[1])
+        scatter_copy(3, weighed[:], units[2])
         size_of_features(0)
         ys_3 = held([P, N_TILES, QUARTER], F32, "ys_3")
         evacuate(ys_3[:, 0:2, :], y_3[0][:])
         evacuate(ys_3[:, 2:4, :], y_3[1][:])
         for n in every:
             nc.gpsimd.tensor_tensor(ys_3[:, n, :], ys_3[:, n, :], weight[:, units[3]], MULT)
-        for n in range(1, N_TILES):
-            size_of_features(n)
+        size_of_features(1)
+        size_of_features(3)
         for n in every:
-            scatter(n, ys_3[:, n, :], units[3])
-        weigh_and_store(0, 0, S, nc.gpsimd)
-        weigh_and_store(1, 0, S, nc.gpsimd)
-        weigh_and_store(2, 0, S, nc.vector)
+            scatter_copy(n, ys_3[:, n, :], units[3])
+        for n, c0 in [(0, 0), (0, HALF), (1, 0)]:
+            weigh_and_store(n, c0, c0 + HALF, nc.gpsimd, feats[:, n, c0 : c0 + HALF])
+        size_of_features(2)
+        weigh_and_store(2, 0, HALF, nc.vector, feats[:, 2, :HALF])
+        weigh_and_store(1, HALF, S, nc.vector, sizes[:, 1, :HALF])
+        weigh_and_store(2, HALF, S, nc.vector, feats[:, 2, HALF:])
         for c0 in range(0, S, QUARTER):
-            weigh_and_store(3, c0, c0 + QUARTER, nc.vector)
+            weigh_and_store(3, c0, c0 + QUARTER, nc.vector, sizes[:, 0, c0 : c0 + QUARTER])

@@ -25,7 +25,6 @@ HALF = S // 2
 PIECE = 128
 QUARTER = 256
 W3_ROW = 8
-SIZE_AT = (0, 1, 0, 2)
 
 
 def tile_list_tape_restore_residuals_kernel(
@@ -159,7 +158,7 @@ def tile_list_tape_restore_residuals_kernel(
                         stop=(a, i) == (PASSES - 1, len(ts) - 1),
                     )
 
-        def w3_passes(y, ns, cols, closes=False):
+        def w3_passes(y, ns, cols, opens=False, closes=False):
             for a in range(PASSES):
                 for i, n in enumerate(ns):
                     ncols = slice(P * n, P * (n + 1))
@@ -169,7 +168,7 @@ def tile_list_tape_restore_residuals_kernel(
                         lhsT_scale=w3_sc[W3_ROW:, a, ncols],
                         rhs=v[a][:, cols].bitcast(FP8X4),
                         rhs_scale=v_sc[:, a, cols],
-                        start=False,
+                        start=opens and (a, i) == (0, 0),
                         stop=closes and (a, i) == (PASSES - 1, len(ns) - 1),
                     )
 
@@ -261,6 +260,11 @@ def tile_list_tape_restore_residuals_kernel(
             y = bank(number, [P, len(ns), cols.stop - cols.start], "y")
             w4_passes(y, 0, ns, cols, opens=True)
             w3_passes(y, ns, cols)
+            return y
+
+        def open_early(number, ns, cols):
+            y = bank(number, [P, len(ns), cols.stop - cols.start], "y")
+            w3_passes(y, ns, cols, opens=True)
             return y
 
         def close_y(y, ns, cols):
@@ -368,50 +372,53 @@ def tile_list_tape_restore_residuals_kernel(
         tanh_bank(3, 0, low, "th3")
         tanh_bank(3, 0, high, "th0")
         apply_gain(3, 0)
-        third = place(y_2[0], both, low, units[2], tag="th3")
+        place(y_2[0], slice(0, 1), range(0, 1), units[2], tag="th3")
+        y_3 = [open_early(2, low, units[3]), open_early(7, high, units[3])]
         weave(3, 0)
-        y_3 = [open_y(2, low, units[3]), open_y(7, high, units[3])]
+        w4_passes(y_3[0], 0, low, units[3])
+        w4_passes(y_3[1], 0, high, units[3])
+        place(y_2[0], slice(1, 2), range(1, 2), units[2], tag="planes30")
         tanh_bank(3, 1, low, "th2")
-        tanh_bank(3, 1, high, "planes30")
-        place(y_2[1], slice(0, 1), range(2, 3), units[2], tag="th0")
+        tanh_bank(3, 1, high, "th0")
         apply_gain(3, 1)
         weave(3, 1)
         close_y(y_3[0], low, units[3])
         close_y(y_3[1], high, units[3])
 
-        late = held([P, 2 * QUARTER + 3 * S], F32, "late", tag="planes31")
-        ends = late[:, : 2 * QUARTER].rearrange("p (n j) -> p n j", n=2)
-        sizes = late[:, 2 * QUARTER :].rearrange("p (n m) -> p n m", n=3)
+        late = held([P, 3 * QUARTER + N_TILES * S], F32, "late", tag="planes31")
+        ends = late[:, : 3 * QUARTER].rearrange("p (n j) -> p n j", n=3)
+        sizes = late[:, 3 * QUARTER :].rearrange("p (n m) -> p n m", n=N_TILES)
 
         def size_of_features(n):
-            nc.scalar.activation(out=sizes[:, SIZE_AT[n], :], in_=feats[:, n, :], func=ACT.Abs)
+            nc.scalar.activation(out=sizes[:, n, :], in_=feats[:, n, :], func=ACT.Abs)
 
         def weigh_and_store(n, c0, c1, engine, product):
-            engine.tensor_tensor(product, pages[n][:, c0:c1], sizes[:, SIZE_AT[n], c0:c1], MULT)
+            engine.tensor_tensor(product, pages[n][:, c0:c1], sizes[:, n, c0:c1], MULT)
             nc.sync.dma_start(out=out[P * n : P * (n + 1), c0:c1], in_=product)
 
-        evacuate(ends[:, 0, :], y_1[1][:, 1, :])
-        evacuate(ends[:, 1, :], y_2[1][:, 1, :])
-        nc.vector.tensor_tensor(ends[:, 0, :], ends[:, 0, :], weight[:, units[1]], MULT)
-        weighed = held([P, QUARTER], F32, "weighed", tag="woven31")
-        nc.gpsimd.tensor_tensor(weighed[:], ends[:, 1, :], weight[:, units[2]], MULT)
-        scatter_copy(3, ends[:, 0, :], units[1])
-        scatter_copy(3, weighed[:], units[2])
-        size_of_features(0)
+        evacuate(ends[:, 0, :], y_2[1][:, 0, :])
+        evacuate(ends[:, 1, :], y_1[1][:, 1, :])
+        evacuate(ends[:, 2, :], y_2[1][:, 1, :])
+        nc.vector.tensor_tensor(ends[:, 0, :], ends[:, 0, :], weight[:, units[2]], MULT)
+        weighed = held([P, 3, QUARTER], F32, "weighed", tag="woven31")
+        nc.gpsimd.tensor_tensor(weighed[:, 0, :], ends[:, 1, :], weight[:, units[1]], MULT)
+        scatter_copy(2, ends[:, 0, :], units[2])
+        scatter_copy(3, weighed[:, 0, :], units[1])
+        nc.gpsimd.tensor_tensor(weighed[:, 1, :], ends[:, 2, :], weight[:, units[2]], MULT)
         ys_3 = held([P, N_TILES, QUARTER], F32, "ys_3")
         evacuate(ys_3[:, 0:2, :], y_3[0][:])
         evacuate(ys_3[:, 2:4, :], y_3[1][:])
-        for n in every:
+        for n in range(3):
             nc.gpsimd.tensor_tensor(ys_3[:, n, :], ys_3[:, n, :], weight[:, units[3]], MULT)
-        size_of_features(1)
-        size_of_features(3)
+        nc.gpsimd.tensor_tensor(weighed[:, 2, :], ys_3[:, 3, :], weight[:, units[3]], MULT)
         for n in every:
+            size_of_features(n)
+        for n in range(3):
             scatter_copy(n, ys_3[:, n, :], units[3])
-        for n, c0 in [(0, 0), (0, HALF), (1, 0)]:
-            weigh_and_store(n, c0, c0 + HALF, nc.gpsimd, feats[:, n, c0 : c0 + HALF])
-        size_of_features(2)
-        weigh_and_store(2, 0, HALF, nc.vector, feats[:, 2, :HALF])
-        weigh_and_store(1, HALF, S, nc.vector, sizes[:, 1, :HALF])
-        weigh_and_store(2, HALF, S, nc.vector, feats[:, 2, HALF:])
+        scatter_copy(3, weighed[:, 1:3, :].rearrange("p n j -> p (n j)"), slice(HALF, S))
+        for n in low:
+            weigh_and_store(n, 0, S, nc.gpsimd, feats[:, n, :])
+        for c0 in (0, HALF):
+            weigh_and_store(2, c0, c0 + HALF, nc.vector, sizes[:, 1, c0 : c0 + HALF])
         for c0 in range(0, S, QUARTER):
-            weigh_and_store(3, c0, c0 + QUARTER, nc.vector, sizes[:, 0, c0 : c0 + QUARTER])
+            weigh_and_store(3, c0, c0 + QUARTER, nc.vector, sizes[:, 2, c0 : c0 + QUARTER])

@@ -207,12 +207,19 @@ def tile_list_tape_restore_residuals_kernel(
         def bank(number, shape, name):
             return psum.tile(shape, F32, tag="bank%d" % number, name=name)
 
-        pieces = [slice(PIECE * i, PIECE * (i + 1)) for i in range(4)]
+        pieces = [slice(PIECE * i, PIECE * (i + 1)) for i in range(6)]
         th_piece = {}
 
+        z_pieces = {}
+
+        def z_piece(i, b, number):
+            z_pieces[(i, b)] = bank(number, [P, PACK, PIECE], "z")
+            z_group(z_pieces[(i, b)], b, range(PACK), pieces[i])
+
         def tanh_piece(i, b, number, th=None):
-            z = bank(number, [P, PACK, PIECE], "z")
-            z_group(z, b, range(PACK), pieces[i])
+            if number is not None:
+                z_piece(i, b, number)
+            z = z_pieces[(i, b)]
             th_piece[(i, b)] = held([P, PIECE, PACK], F32, "thp%d%d" % (i, b))[:] if th is None else th
             nc.scalar.activation(
                 out=th_piece[(i, b)], in_=z[:].rearrange("p t j -> p j t"), func=ACT.Tanh, scale=-1.0
@@ -338,12 +345,14 @@ def tile_list_tape_restore_residuals_kernel(
         for c0 in (0, PIECE):
             gain_on_vector(hb_second[:, c0 : c0 + PIECE, :], th_second[:, c0 : c0 + PIECE, :], 0, nc.gpsimd)
         quantise_h(0, units[1], hb_second[:])
-        z_bank(2, 1, low, 0)
-        z_bank(2, 1, high, 6)
+        z_piece(4, 1, 0)
+        z_piece(5, 1, 6)
         y_1 = [open_y(2, low, units[1]), open_y(3, high, units[1])]
         weave(2, 0, tag="thp01", plane_tag="th_second")
         tanh_bank(1, 1, low, "th0")
         tanh_bank(1, 1, high, "th1")
+        z_bank(3, 0, low, 4)
+        z_bank(3, 0, high, 5)
 
         apply_gain(1, 1)
         place(y_b[0], slice(0, 1), range(0, 1), pieces[1], tag="th0")
@@ -351,43 +360,45 @@ def tile_list_tape_restore_residuals_kernel(
         close_y(y_1[0], low, units[1])
         close_y(y_1[1], high, units[1])
         rest_b = held([P, 3, PIECE], F32, "rest_b", tag="planes11")
-        place(y_b[0], slice(1, 2), range(1, 2), pieces[1], values=rest_b[:, 0:1, :])
-        place(y_b[1], both, high, pieces[1], values=rest_b[:, 1:3, :])
-        tanh_bank(2, 1, low, "th2")
-        tanh_bank(2, 1, high, "th3")
-        z_bank(3, 0, low, 1)
-        z_bank(3, 0, high, 7)
+        weighed_b = held([P, 3, PIECE], F32, "weighed_b")
+        evacuate(rest_b[:, 0, :], y_b[0][:, 1, :])
+        evacuate(rest_b[:, 1:3, :], y_b[1][:])
+        nc.vector.tensor_tensor(
+            weighed_b[:], rest_b[:], weight[:, pieces[1]].unsqueeze(1).to_broadcast([P, 3, PIECE]), MULT
+        )
+        for n in range(1, N_TILES):
+            scatter_copy(n, weighed_b[:, n - 1, :], pieces[1])
+        th_third = held([P, QUARTER, PACK], F32, "th_third", tag="th2")
+        tanh_piece(4, 1, None, th_third[:, :PIECE, :])
+        tanh_piece(5, 1, None, th_third[:, PIECE:, :])
+        hb_third = held([P, QUARTER, PACK], BF16, "hb_third", tag="planes11")
+        for c0 in (0, PIECE):
+            gain_on_vector(hb_third[:, c0 : c0 + PIECE, :], th_third[:, c0 : c0 + PIECE, :], 1, nc.gpsimd)
         z_bank(3, 1, low, 0)
         z_bank(3, 1, high, 6)
-        y_2 = [open_y(4, low, units[2]), open_y(5, high, units[2])]
-        apply_gain(2, 1)
-        second = place(y_1[0], slice(0, 1), range(0, 1), units[1], tag="th2")
-        weave(2, 1)
+        y_2 = [open_y(1, low, units[2]), open_y(7, high, units[2])]
+        quantise_h(1, units[2], hb_third[:])
         close_y(y_2[0], low, units[2])
         close_y(y_2[1], high, units[2])
-        rest_1 = held([P, 2, QUARTER], F32, "rest_1", tag="planes21")
-        place(y_1[0], slice(1, 2), range(1, 2), units[1], values=rest_1[:, 0:1, :])
-        place(y_1[1], slice(0, 1), range(2, 3), units[1], values=rest_1[:, 1:2, :])
-
         tanh_bank(3, 0, low, "th3")
         tanh_bank(3, 0, high, "th0")
+        place(y_1[0], slice(0, 1), range(0, 1), units[1])
         apply_gain(3, 0)
-        place(y_2[0], slice(0, 1), range(0, 1), units[2], tag="th3")
-        y_3 = [open_early(2, low, units[3]), open_early(7, high, units[3])]
+        place(y_1[0], slice(1, 2), range(1, 2), units[1])
+        y_3 = [open_early(2, low, units[3]), open_early(4, high, units[3])]
         weave(3, 0)
         w4_passes(y_3[0], 0, low, units[3])
         w4_passes(y_3[1], 0, high, units[3])
-        place(y_2[0], slice(1, 2), range(1, 2), units[2], tag="planes30")
-        tanh_bank(3, 1, low, "th2")
-        tanh_bank(3, 1, high, "th0")
+        rest_1 = held([P, 2, QUARTER], F32, "rest_1", tag="planes30")
+        place(y_1[1], slice(0, 1), range(2, 3), units[1], values=rest_1[:, 0:1, :])
+        tanh_bank(3, 1, low, "th0")
+        tanh_bank(3, 1, high, "th3")
+        place(y_2[0], slice(0, 1), range(0, 1), units[2], values=rest_1[:, 1:2, :])
         apply_gain(3, 1)
         weave(3, 1)
         close_y(y_3[0], low, units[3])
         close_y(y_3[1], high, units[3])
 
-        late = held([P, 3 * QUARTER + N_TILES * S], F32, "late", tag="planes31")
-        ends = late[:, : 3 * QUARTER].rearrange("p (n j) -> p n j", n=3)
-        sizes = late[:, 3 * QUARTER :].rearrange("p (n m) -> p n m", n=N_TILES)
 
         def size_of_features(n):
             nc.scalar.activation(out=sizes[:, n, :], in_=feats[:, n, :], func=ACT.Abs)
@@ -396,29 +407,32 @@ def tile_list_tape_restore_residuals_kernel(
             engine.tensor_tensor(product, pages[n][:, c0:c1], sizes[:, n, c0:c1], MULT)
             nc.sync.dma_start(out=out[P * n : P * (n + 1), c0:c1], in_=product)
 
-        evacuate(ends[:, 0, :], y_2[1][:, 0, :])
-        evacuate(ends[:, 1, :], y_1[1][:, 1, :])
-        evacuate(ends[:, 2, :], y_2[1][:, 1, :])
-        nc.vector.tensor_tensor(ends[:, 0, :], ends[:, 0, :], weight[:, units[2]], MULT)
-        weighed = held([P, 3, QUARTER], F32, "weighed", tag="woven31")
-        nc.gpsimd.tensor_tensor(weighed[:, 0, :], ends[:, 1, :], weight[:, units[1]], MULT)
-        scatter_copy(2, ends[:, 0, :], units[2])
-        scatter_copy(3, weighed[:, 0, :], units[1])
-        nc.gpsimd.tensor_tensor(weighed[:, 1, :], ends[:, 2, :], weight[:, units[2]], MULT)
+        bridge_raw = held([P, QUARTER], F32, "bridge_raw", tag="planes31")
+        bridge = held([P, QUARTER], F32, "bridge")
+        ends = held([P, 3, QUARTER], F32, "ends", tag="th3")
+        evacuate(bridge_raw[:], y_2[0][:, 1, :])
+        evacuate(ends[:, 0:2, :], y_2[1][:])
+        evacuate(ends[:, 2, :], y_1[1][:, 1, :])
+        nc.vector.tensor_tensor(bridge[:], bridge_raw[:], weight[:, units[2]], MULT)
+        weighed = held([P, 4, QUARTER], F32, "weighed", tag="planes31")
+        nc.gpsimd.tensor_tensor(weighed[:, 0, :], ends[:, 0, :], weight[:, units[2]], MULT)
+        scatter_copy(1, bridge[:], units[2])
+        scatter_copy(2, weighed[:, 0, :], units[2])
         ys_3 = held([P, N_TILES, QUARTER], F32, "ys_3")
         evacuate(ys_3[:, 0:2, :], y_3[0][:])
         evacuate(ys_3[:, 2:4, :], y_3[1][:])
         for n in range(3):
             nc.gpsimd.tensor_tensor(ys_3[:, n, :], ys_3[:, n, :], weight[:, units[3]], MULT)
-        nc.gpsimd.tensor_tensor(weighed[:, 2, :], ys_3[:, 3, :], weight[:, units[3]], MULT)
+        nc.gpsimd.tensor_tensor(weighed[:, 1, :], ends[:, 2, :], weight[:, units[1]], MULT)
+        nc.gpsimd.tensor_tensor(weighed[:, 2, :], ends[:, 1, :], weight[:, units[2]], MULT)
+        nc.gpsimd.tensor_tensor(weighed[:, 3, :], ys_3[:, 3, :], weight[:, units[3]], MULT)
+        sizes = held([P, N_TILES, S], F32, "sizes", tag="woven31")
         for n in every:
             size_of_features(n)
         for n in range(3):
             scatter_copy(n, ys_3[:, n, :], units[3])
-        scatter_copy(3, weighed[:, 1:3, :].rearrange("p n j -> p (n j)"), slice(HALF, S))
-        for n in low:
+        scatter_copy(3, weighed[:, 1:4, :].rearrange("p n j -> p (n j)"), slice(QUARTER, S))
+        for n in range(3):
             weigh_and_store(n, 0, S, nc.gpsimd, feats[:, n, :])
-        for c0 in (0, HALF):
-            weigh_and_store(2, c0, c0 + HALF, nc.vector, sizes[:, 1, c0 : c0 + HALF])
         for c0 in range(0, S, QUARTER):
             weigh_and_store(3, c0, c0 + QUARTER, nc.vector, sizes[:, 2, c0 : c0 + QUARTER])

@@ -116,8 +116,8 @@ def tile_list_tape_restore_residuals_kernel(
             for copy_rows, m0, m1 in copies:
                 first = m0 // per_load * per_load
                 copy_rows(
-                    out=grouped[:, :, m0:m1, :].rearrange("p t m j -> p m t j"),
-                    in_=raw[(a, b)][m0 // per_load][:].rearrange("p j (m t) -> p m t j", t=PACK)[
+                    out=grouped[:, :, m0:m1, :].rearrange("p t m j -> p m j t"),
+                    in_=raw[(a, b)][m0 // per_load][:].rearrange("p j (m t) -> p m j t", t=PACK)[
                         :, m0 - first : m1 - first, :, :
                     ],
                 )

@@ -24,7 +24,7 @@ N_TILES = N // P
 HALF = S // 2
 PIECE = 128
 QUARTER = 256
-W3_ROW = 8
+V_ROW = 8
 
 
 def tile_list_tape_restore_residuals_kernel(
@@ -59,17 +59,17 @@ def tile_list_tape_restore_residuals_kernel(
         gains = held([P, PASSES, PACK], F32, "gains")
         raw = {}
 
-        def load_w1(a, b, parts):
-            width = PASS // parts
-            raw[(a, b)] = []
-            for u in range(parts):
-                t_raw = held([P, PACK, width], F32, "raw%d%d%d" % (a, b, u))
-                c0 = PASS * b + width * u
+        def load_w1(a, b, *runs):
+            raw.setdefault((a, b), [])
+            for m0, m1 in runs:
+                width = PACK * (m1 - m0)
+                t_raw = held([P, PACK, width], F32, "raw%d%d_%d" % (a, b, m0))
+                c0 = PASS * b + PACK * m0
                 nc.sync.dma_start(
                     out=t_raw[:],
                     in_=w1[PASS * a : PASS * (a + 1), c0 : c0 + width].rearrange("(p j) c -> p j c", j=PACK),
                 )
-                raw[(a, b)].append(t_raw)
+                raw[(a, b)].append((m0, m1, t_raw))
 
         def load_scales(sc, first_row, src):
             for r in range(4):
@@ -82,24 +82,24 @@ def tile_list_tape_restore_residuals_kernel(
         w4 = held([P, PASSES, 2 * N], U8, "w4")
         weight = held([P, S], F32, "weight")
 
-        load_w1(0, 0, 1)
+        load_w1(0, 0, (0, P))
         nc.sync.dma_start(picks[:], offs)
         for a in range(PASSES):
-            nc.sync.dma_start(out=tab_sc[a][0:P:8, :].bitcast(I32), in_=tab_scales[a].bitcast(I32))
+            nc.sync.dma_start(out=tab_sc[a][4:P:8, :].bitcast(I32), in_=tab_scales[a].bitcast(I32))
         load_tab(0, 0, T)
         nc.sync.dma_start(out=gains[:], in_=gain.rearrange("(b p t) -> p b t", b=PASSES, t=PACK))
-        load_w1(1, 0, 1)
-        load_tab(1, 0, T // 2)
+        load_tab(1, 0, T)
+        load_w1(1, 0, (0, 64))
         picked_sc = held([P, PASSES, S], U8, "picked_sc")
         for a in range(PASSES):
             nc.vector.tensor_copy(picked_sc[:, a, :], tab_sc[a][:].indirect(picks[:]))
         for r in range(4):
-            nc.sync.dma_start(out=v_sc[r:P:32, :, :].bitcast(I32), in_=picked_sc[8 * r : P : 32, :, :].bitcast(I32))
-        load_tab(1, T // 2, T)
+            nc.sync.dma_start(out=v_sc[V_ROW + r : P : 32, :, :].bitcast(I32), in_=picked_sc[4 + 8 * r : P : 32, :, :].bitcast(I32))
+        load_w1(1, 0, (64, P))
         load_scales(w4_sc, 0, w4_scales)
-        load_scales(w3_sc, W3_ROW, w3_scales)
-        load_w1(0, 1, 1)
-        load_w1(1, 1, 2)
+        load_scales(w3_sc, 0, w3_scales)
+        load_w1(0, 1, (0, 64), (64, P))
+        load_w1(1, 1, (0, 64), (64, P))
         nc.sync.dma_start(out=w4[:].bitcast(I32), in_=w4_words.rearrange("a p c -> p a c").bitcast(I32))
         nc.sync.dma_start(out=w3[:].bitcast(I32), in_=w3_words.rearrange("a p c i -> p a (c i)").bitcast(I32))
         nc.sync.dma_start(places[:], offs2)
@@ -112,14 +112,10 @@ def tile_list_tape_restore_residuals_kernel(
             grouped = held([P, PACK, P, PACK], BF16, "grouped%d%d" % (a, b))
             w1c[(a, b)] = held([P, PASS], U32, "w1c%d%d" % (a, b))
             w1s[(a, b)] = held([P, PASS], U8, "w1s%d%d" % (a, b))
-            per_load = P // len(raw[(a, b)])
-            for copy_rows, m0, m1 in copies:
-                first = m0 // per_load * per_load
+            for copy_rows, (m0, m1, t_raw) in zip(copies, raw[(a, b)]):
                 copy_rows(
                     out=grouped[:, :, m0:m1, :].rearrange("p t m j -> p m j t"),
-                    in_=raw[(a, b)][m0 // per_load][:].rearrange("p j (m t) -> p m j t", t=PACK)[
-                        :, m0 - first : m1 - first, :, :
-                    ],
+                    in_=t_raw[:].rearrange("p j (m t) -> p m j t", t=PACK),
                 )
             tw = PACK // calls
             for u in range(calls):
@@ -130,13 +126,12 @@ def tile_list_tape_restore_residuals_kernel(
                 )
 
         on_vector, on_scalar = nc.vector.tensor_copy, nc.scalar.copy
-        quantise_w1(0, 0, 1, [(on_scalar, 0, P)])
-        nc.vector.tensor_copy(v[0][:], tab[0][:].bitcast(U32).indirect(picks[:]))
-        quantise_w1(1, 0, 1, [(on_scalar, 0, P)])
-        nc.vector.tensor_copy(v[1][:, :HALF], tab[1][:].bitcast(U32).indirect(picks[:, : HALF // 16]))
-        nc.vector.tensor_copy(v[1][:, HALF:], tab[1][:].bitcast(U32).indirect(picks[:, HALF // 16 :]))
-        quantise_w1(0, 1, 1, [(on_vector, 0, P)])
-        quantise_w1(1, 1, 2, [(on_vector, 0, 64), (on_vector, 64, P)])
+        quantise_w1(0, 0, 1, [on_scalar])
+        for a in range(PASSES):
+            nc.vector.tensor_copy(v[a][:], tab[a][:].bitcast(U32).indirect(picks[:]))
+        quantise_w1(1, 0, 2, [on_scalar, on_vector])
+        quantise_w1(0, 1, 1, [on_vector, on_vector])
+        quantise_w1(1, 1, 4, [on_vector, on_vector])
 
         feats = held([P, N_TILES, S], F32, "feats", tag="tab0")
         for n in range(N_TILES):
@@ -153,7 +148,7 @@ def tile_list_tape_restore_residuals_kernel(
                         lhsT=w1c[(a, b)][:, P * t : P * (t + 1)].bitcast(FP8X4),
                         lhsT_scale=w1s[(a, b)][:, P * t : P * (t + 1)],
                         rhs=v[a][:, cols].bitcast(FP8X4),
-                        rhs_scale=v_sc[:, a, cols],
+                        rhs_scale=v_sc[V_ROW:, a, cols],
                         start=(a, i) == (0, 0),
                         stop=(a, i) == (PASSES - 1, len(ts) - 1),
                     )
@@ -165,9 +160,9 @@ def tile_list_tape_restore_residuals_kernel(
                     nc.tensor.matmul_mx(
                         out=y[:, i, :],
                         lhsT=w3[:, a, ncols].bitcast(FP8X4),
-                        lhsT_scale=w3_sc[W3_ROW:, a, ncols],
+                        lhsT_scale=w3_sc[:, a, ncols],
                         rhs=v[a][:, cols].bitcast(FP8X4),
-                        rhs_scale=v_sc[:, a, cols],
+                        rhs_scale=v_sc[V_ROW:, a, cols],
                         start=opens and (a, i) == (0, 0),
                         stop=closes and (a, i) == (PASSES - 1, len(ns) - 1),
                     )
@@ -307,9 +302,18 @@ def tile_list_tape_restore_residuals_kernel(
         z_bank(2, 0, high, 7)
         tanh_bank(2, 0, low, "th2")
         tanh_bank(2, 0, high, "th3")
-        apply_gain(2, 0)
-        tanh_piece(0, 1, 4)
+        z_piece(0, 1, 4)
+        th_piece[(0, 1)] = held([P, PIECE, PACK], F32, "thp01")[:]
+        halves = (slice(0, PIECE // 2), slice(PIECE // 2, PIECE))
+        for half in halves:
+            nc.scalar.activation(
+                out=th_piece[(0, 1)][:, half, :],
+                in_=z_pieces[(0, 1)][:, :, half].rearrange("p t j -> p j t"),
+                func=ACT.Tanh,
+                scale=-1.0,
+            )
         tanh_piece(1, 1, 5)
+        apply_gain(2, 0)
 
         hb0 = held([P, 2, PIECE, PACK], BF16, "hb0", tag="grouped11")
         hb1 = [held([P, PIECE, PACK], BF16, "hb10")]
@@ -317,7 +321,8 @@ def tile_list_tape_restore_residuals_kernel(
         gain_piece(1, 0, hb0[:, 1, :, :])
         quantise_h(0, pieces[0], hb0[:, 0, :, :])
         y_a0 = open_y(0, low, pieces[0])
-        gain_piece(0, 1, hb1[0][:])
+        for half in halves:
+            gain_on_vector(hb1[0][:, half, :], th_piece[(0, 1)][:, half, :], 1)
         quantise_h(0, pieces[1], hb0[:, 1, :, :])
         quantise_h(1, pieces[0], hb1[0][:])
         close_y(y_a0, low, pieces[0])

@@ -69,7 +69,7 @@ def tile_list_tape_restore_residuals_kernel(
                     out=t_raw[:],
                     in_=w1[PASS * a : PASS * (a + 1), c0 : c0 + width].rearrange("(p j) c -> p j c", j=PACK),
                 )
-                raw[(a, b)].append((m0, m1, t_raw))
+                raw[(a, b)].append((m0, t_raw))
 
         def load_scales(sc, first_row, src):
             for r in range(4):
@@ -89,13 +89,12 @@ def tile_list_tape_restore_residuals_kernel(
         load_tab(0, 0, T)
         nc.sync.dma_start(out=gains[:], in_=gain.rearrange("(b p t) -> p b t", b=PASSES, t=PACK))
         load_tab(1, 0, T)
-        load_w1(1, 0, (0, 64))
         picked_sc = held([P, PASSES, S], U8, "picked_sc")
         for a in range(PASSES):
             nc.vector.tensor_copy(picked_sc[:, a, :], tab_sc[a][:].indirect(picks[:]))
         for r in range(4):
             nc.sync.dma_start(out=v_sc[V_ROW + r : P : 32, :, :].bitcast(I32), in_=picked_sc[4 + 8 * r : P : 32, :, :].bitcast(I32))
-        load_w1(1, 0, (64, P))
+        load_w1(1, 0, (0, 64), (64, P))
         load_scales(w4_sc, 0, w4_scales)
         load_scales(w3_sc, 0, w3_scales)
         load_w1(0, 1, (0, 64), (64, P))
@@ -112,10 +111,11 @@ def tile_list_tape_restore_residuals_kernel(
             grouped = held([P, PACK, P, PACK], BF16, "grouped%d%d" % (a, b))
             w1c[(a, b)] = held([P, PASS], U32, "w1c%d%d" % (a, b))
             w1s[(a, b)] = held([P, PASS], U8, "w1s%d%d" % (a, b))
-            for copy_rows, (m0, m1, t_raw) in zip(copies, raw[(a, b)]):
+            for copy_rows, part, m0, m1 in copies:
+                first, t_raw = raw[(a, b)][part]
                 copy_rows(
                     out=grouped[:, :, m0:m1, :].rearrange("p t m j -> p m j t"),
-                    in_=t_raw[:].rearrange("p j (m t) -> p m j t", t=PACK),
+                    in_=t_raw[:].rearrange("p j (m t) -> p m j t", t=PACK)[:, m0 - first : m1 - first, :, :],
                 )
             tw = PACK // calls
             for u in range(calls):
@@ -126,12 +126,12 @@ def tile_list_tape_restore_residuals_kernel(
                 )
 
         on_vector, on_scalar = nc.vector.tensor_copy, nc.scalar.copy
-        quantise_w1(0, 0, 1, [on_scalar])
+        quantise_w1(0, 0, 1, [(on_scalar, 0, 0, P)])
         for a in range(PASSES):
             nc.vector.tensor_copy(v[a][:], tab[a][:].bitcast(U32).indirect(picks[:]))
-        quantise_w1(1, 0, 2, [on_scalar, on_vector])
-        quantise_w1(0, 1, 1, [on_vector, on_vector])
-        quantise_w1(1, 1, 4, [on_vector, on_vector])
+        quantise_w1(1, 0, 4, [(on_scalar, 0, 0, 64), (on_vector, 1, 64, 104), (on_scalar, 1, 104, P)])
+        quantise_w1(0, 1, 1, [(on_vector, 0, 0, 64), (on_vector, 1, 64, P)])
+        quantise_w1(1, 1, 4, [(on_vector, 0, 0, 64), (on_vector, 1, 64, P)])
 
         feats = held([P, N_TILES, S], F32, "feats", tag="tab0")
         for n in range(N_TILES):
@@ -168,23 +168,20 @@ def tile_list_tape_restore_residuals_kernel(
                     )
 
         def w4_passes(y, b, ns, cols, opens=False, closes=False):
-            starts = range(cols.start, cols.stop, PIECE)
             for i, n in enumerate(ns):
-                for c0 in starts:
-                    nc.tensor.matmul_mx(
-                        out=y[:, i, c0 - cols.start : c0 - cols.start + PIECE],
-                        lhsT=w4[:, b, 2 * P * n : 2 * P * (n + 1)].bitcast(FP4X4),
-                        lhsT_scale=w4_sc[:, b, P * n : P * (n + 1)],
-                        rhs=hc[b][:, c0 : c0 + PIECE].bitcast(FP8X4),
-                        rhs_scale=hs[(b, c0)],
-                        start=opens and i == 0 and c0 == cols.start,
-                        stop=closes and i == len(ns) - 1 and c0 == starts[-1],
-                    )
+                nc.tensor.matmul_mx(
+                    out=y[:, i, :],
+                    lhsT=w4[:, b, 2 * P * n : 2 * P * (n + 1)].bitcast(FP4X4),
+                    lhsT_scale=w4_sc[:, b, P * n : P * (n + 1)],
+                    rhs=hc[b][:, cols].bitcast(FP8X4),
+                    rhs_scale=hs[(b, cols.start)],
+                    start=opens and i == 0,
+                    stop=closes and i == len(ns) - 1,
+                )
 
         def quantise_h(b, cols, woven, tag=None):
             plane = held([P, cols.stop - cols.start], U8, "hs%d_%d" % (b, cols.start), tag=tag)
-            for c0 in range(cols.start, cols.stop, PIECE):
-                hs[(b, c0)] = plane[:, c0 - cols.start : c0 - cols.start + PIECE]
+            hs[(b, cols.start)] = plane[:]
             nc.vector.quantize_mx(
                 out=hc[b][:, cols].bitcast(FP8X4), scales=plane[:], in_=woven.rearrange("p j t -> p (j t)")
             )
@@ -321,14 +318,15 @@ def tile_list_tape_restore_residuals_kernel(
         gain_piece(1, 0, hb0[:, 1, :, :])
         quantise_h(0, pieces[0], hb0[:, 0, :, :])
         y_a0 = open_y(0, low, pieces[0])
+        y_a1 = open_y(6, high, pieces[0])
         for half in halves:
             gain_on_vector(hb1[0][:, half, :], th_piece[(0, 1)][:, half, :], 1)
         quantise_h(0, pieces[1], hb0[:, 1, :, :])
         quantise_h(1, pieces[0], hb1[0][:])
         close_y(y_a0, low, pieces[0])
-        y_a1 = whole_y(6, high, pieces[0])
-        z_bank(1, 1, low, 4)
-        z_bank(1, 1, high, 5)
+        close_y(y_a1, high, pieces[0])
+        z_bank(1, 1, low, 2)
+        z_bank(1, 1, high, 3)
         hb1.append(held([P, PIECE, PACK], BF16, "hb11", tag="hb10"))
         gain_piece(1, 1, hb1[1][:])
         first = held([P, 2, PIECE], F32, "first")
@@ -337,7 +335,7 @@ def tile_list_tape_restore_residuals_kernel(
         quantise_h(1, pieces[1], hb1[1][:])
         for n in low:
             scatter_copy(n, first[:, n, :], pieces[0])
-        y_b = [whole_y(1, low, pieces[1]), whole_y(7, high, pieces[1])]
+        y_b = [whole_y(4, low, pieces[1]), whole_y(5, high, pieces[1])]
         raw_high = held([P, 2, PIECE], F32, "raw_high")
         first_high = held([P, 2, PIECE], F32, "first_high")
         evacuate(raw_high[:], y_a1[:])
@@ -352,27 +350,26 @@ def tile_list_tape_restore_residuals_kernel(
         quantise_h(0, units[1], hb_second[:])
         z_piece(4, 1, 0)
         z_piece(5, 1, 6)
-        y_1 = [open_y(2, low, units[1]), open_y(3, high, units[1])]
-        weave(2, 0, tag="thp01", plane_tag="th_second")
         tanh_bank(1, 1, low, "th0")
         tanh_bank(1, 1, high, "th1")
-        z_bank(3, 0, low, 4)
-        z_bank(3, 0, high, 5)
+        weave(2, 0, tag="thp11", plane_tag="th_second")
+        y_1 = [open_y(1, low, units[1]), open_y(7, high, units[1])]
+        z_bank(3, 0, low, 2)
+        z_bank(3, 0, high, 3)
 
         apply_gain(1, 1)
-        place(y_b[0], slice(0, 1), range(0, 1), pieces[1], tag="th0")
         weave(1, 1)
         close_y(y_1[0], low, units[1])
         close_y(y_1[1], high, units[1])
-        rest_b = held([P, 3, PIECE], F32, "rest_b", tag="planes11")
-        weighed_b = held([P, 3, PIECE], F32, "weighed_b")
-        evacuate(rest_b[:, 0, :], y_b[0][:, 1, :])
-        evacuate(rest_b[:, 1:3, :], y_b[1][:])
+        rest_b = held([P, N_TILES, PIECE], F32, "rest_b", tag="planes11")
+        weighed_b = held([P, N_TILES, PIECE], F32, "weighed_b")
+        evacuate(rest_b[:, 0:2, :], y_b[0][:])
+        evacuate(rest_b[:, 2:4, :], y_b[1][:])
         nc.vector.tensor_tensor(
-            weighed_b[:], rest_b[:], weight[:, pieces[1]].unsqueeze(1).to_broadcast([P, 3, PIECE]), MULT
+            weighed_b[:], rest_b[:], weight[:, pieces[1]].unsqueeze(1).to_broadcast([P, N_TILES, PIECE]), MULT
         )
-        for n in range(1, N_TILES):
-            scatter_copy(n, weighed_b[:, n - 1, :], pieces[1])
+        for n in every:
+            scatter_copy(n, weighed_b[:, n, :], pieces[1])
         th_third = held([P, QUARTER, PACK], F32, "th_third", tag="th2")
         tanh_piece(4, 1, None, th_third[:, :PIECE, :])
         tanh_piece(5, 1, None, th_third[:, PIECE:, :])
@@ -381,7 +378,7 @@ def tile_list_tape_restore_residuals_kernel(
             gain_on_vector(hb_third[:, c0 : c0 + PIECE, :], th_third[:, c0 : c0 + PIECE, :], 1, nc.gpsimd)
         z_bank(3, 1, low, 0)
         z_bank(3, 1, high, 6)
-        y_2 = [open_y(1, low, units[2]), open_y(7, high, units[2])]
+        y_2 = [open_y(4, low, units[2]), open_y(5, high, units[2])]
         quantise_h(1, units[2], hb_third[:])
         close_y(y_2[0], low, units[2])
         close_y(y_2[1], high, units[2])
@@ -390,7 +387,7 @@ def tile_list_tape_restore_residuals_kernel(
         place(y_1[0], slice(0, 1), range(0, 1), units[1])
         apply_gain(3, 0)
         place(y_1[0], slice(1, 2), range(1, 2), units[1])
-        y_3 = [open_early(2, low, units[3]), open_early(4, high, units[3])]
+        y_3 = [open_early(2, low, units[3]), open_early(3, high, units[3])]
         weave(3, 0)
         w4_passes(y_3[0], 0, low, units[3])
         w4_passes(y_3[1], 0, high, units[3])

@@ -352,7 +352,6 @@ def tile_list_tape_restore_residuals_kernel(
         z_piece(5, 1, 6)
         tanh_bank(1, 1, low, "th0")
         tanh_bank(1, 1, high, "th1")
-        weave(2, 0, tag="thp11", plane_tag="th_second")
         y_1 = [open_y(1, low, units[1]), open_y(7, high, units[1])]
         z_bank(3, 0, low, 2)
         z_bank(3, 0, high, 3)
@@ -361,25 +360,35 @@ def tile_list_tape_restore_residuals_kernel(
         weave(1, 1)
         close_y(y_1[0], low, units[1])
         close_y(y_1[1], high, units[1])
-        rest_b = held([P, N_TILES, PIECE], F32, "rest_b", tag="planes11")
-        weighed_b = held([P, N_TILES, PIECE], F32, "weighed_b")
+        after_weave = held([P, PASS + S], F32, "after_weave", tag="planes11")
+        rest_b = after_weave[:, :PASS].rearrange("p (n j) -> p n j", n=N_TILES)
+        th_third = after_weave[:, PASS:].rearrange("p (j t) -> p j t", t=PACK)
+        after_quantise = held([P, QUARTER + PASS], F32, "after_quantise", tag="woven11")
+        hb_third = after_quantise[:, QUARTER:].bitcast(BF16).rearrange("p (j t) -> p j t", t=PACK)
+        weighed_b = [
+            held([P, 2, PIECE], F32, "weighed_b")[:],
+            after_quantise[:, :QUARTER].rearrange("p (n j) -> p n j", n=2),
+        ]
         evacuate(rest_b[:, 0:2, :], y_b[0][:])
         evacuate(rest_b[:, 2:4, :], y_b[1][:])
-        nc.vector.tensor_tensor(
-            weighed_b[:], rest_b[:], weight[:, pieces[1]].unsqueeze(1).to_broadcast([P, N_TILES, PIECE]), MULT
-        )
-        for n in every:
-            scatter_copy(n, weighed_b[:, n, :], pieces[1])
-        th_third = held([P, QUARTER, PACK], F32, "th_third", tag="th2")
+        for engine, values, ns in zip((nc.vector, nc.gpsimd), weighed_b, (low, high)):
+            engine.tensor_tensor(
+                values,
+                rest_b[:, ns.start : ns.stop, :],
+                weight[:, pieces[1]].unsqueeze(1).to_broadcast([P, 2, PIECE]),
+                MULT,
+            )
+            for n in ns:
+                scatter_copy(n, values[:, n - ns.start, :], pieces[1])
         tanh_piece(4, 1, None, th_third[:, :PIECE, :])
         tanh_piece(5, 1, None, th_third[:, PIECE:, :])
-        hb_third = held([P, QUARTER, PACK], BF16, "hb_third", tag="planes11")
         for c0 in (0, PIECE):
             gain_on_vector(hb_third[:, c0 : c0 + PIECE, :], th_third[:, c0 : c0 + PIECE, :], 1, nc.gpsimd)
+        weave(2, 0, tag="th1")
         z_bank(3, 1, low, 0)
         z_bank(3, 1, high, 6)
         y_2 = [open_y(4, low, units[2]), open_y(5, high, units[2])]
-        quantise_h(1, units[2], hb_third[:])
+        quantise_h(1, units[2], hb_third)
         close_y(y_2[0], low, units[2])
         close_y(y_2[1], high, units[2])
         tanh_bank(3, 0, low, "th3")
@@ -387,15 +396,14 @@ def tile_list_tape_restore_residuals_kernel(
         place(y_1[0], slice(0, 1), range(0, 1), units[1])
         apply_gain(3, 0)
         place(y_1[0], slice(1, 2), range(1, 2), units[1])
+        place(y_1[1], slice(0, 1), range(2, 3), units[1])
         y_3 = [open_early(2, low, units[3]), open_early(3, high, units[3])]
         weave(3, 0)
         w4_passes(y_3[0], 0, low, units[3])
         w4_passes(y_3[1], 0, high, units[3])
-        rest_1 = held([P, 2, QUARTER], F32, "rest_1", tag="planes30")
-        place(y_1[1], slice(0, 1), range(2, 3), units[1], values=rest_1[:, 0:1, :])
         tanh_bank(3, 1, low, "th0")
         tanh_bank(3, 1, high, "th3")
-        place(y_2[0], slice(0, 1), range(0, 1), units[2], values=rest_1[:, 1:2, :])
+        place(y_2[0], slice(0, 1), range(0, 1), units[2], tag="planes30")
         apply_gain(3, 1)
         weave(3, 1)
         close_y(y_3[0], low, units[3])
@@ -409,14 +417,16 @@ def tile_list_tape_restore_residuals_kernel(
             engine.tensor_tensor(product, pages[n][:, c0:c1], sizes[:, n, c0:c1], MULT)
             nc.sync.dma_start(out=out[P * n : P * (n + 1), c0:c1], in_=product)
 
-        bridge_raw = held([P, QUARTER], F32, "bridge_raw", tag="planes31")
+        late = held([P, 4, QUARTER], F32, "late", tag="planes31")
+        bridge_raw, ends = late[:, 0, :], late[:, 1:4, :]
         bridge = held([P, QUARTER], F32, "bridge")
-        ends = held([P, 3, QUARTER], F32, "ends", tag="th3")
-        evacuate(bridge_raw[:], y_2[0][:, 1, :])
+        evacuate(bridge_raw, y_2[0][:, 1, :])
         evacuate(ends[:, 0:2, :], y_2[1][:])
         evacuate(ends[:, 2, :], y_1[1][:, 1, :])
-        nc.vector.tensor_tensor(bridge[:], bridge_raw[:], weight[:, units[2]], MULT)
-        weighed = held([P, 4, QUARTER], F32, "weighed", tag="planes31")
+        nc.vector.tensor_tensor(bridge[:], bridge_raw, weight[:, units[2]], MULT)
+        last = held([P, (N_TILES + 1) * S], F32, "last", tag="woven31")
+        weighed = last[:, :S].rearrange("p (n j) -> p n j", n=4)
+        sizes = last[:, S:].rearrange("p (n m) -> p n m", n=N_TILES)
         nc.gpsimd.tensor_tensor(weighed[:, 0, :], ends[:, 0, :], weight[:, units[2]], MULT)
         scatter_copy(1, bridge[:], units[2])
         scatter_copy(2, weighed[:, 0, :], units[2])
@@ -428,12 +438,11 @@ def tile_list_tape_restore_residuals_kernel(
         nc.gpsimd.tensor_tensor(weighed[:, 1, :], ends[:, 2, :], weight[:, units[1]], MULT)
         nc.gpsimd.tensor_tensor(weighed[:, 2, :], ends[:, 1, :], weight[:, units[2]], MULT)
         nc.gpsimd.tensor_tensor(weighed[:, 3, :], ys_3[:, 3, :], weight[:, units[3]], MULT)
-        sizes = held([P, N_TILES, S], F32, "sizes", tag="woven31")
         for n in every:
             size_of_features(n)
         for n in range(3):
             scatter_copy(n, ys_3[:, n, :], units[3])
-        scatter_copy(3, weighed[:, 1:4, :].rearrange("p n j -> p (n j)"), slice(QUARTER, S))
+        scatter_copy(3, last[:, QUARTER:S], slice(QUARTER, S))
         for n in range(3):
             weigh_and_store(n, 0, S, nc.gpsimd, feats[:, n, :])
         for c0 in range(0, S, QUARTER):

@@ -87,7 +87,6 @@ def tile_list_tape_restore_residuals_kernel(
         for a in range(PASSES):
             nc.sync.dma_start(out=tab_sc[a][4:P:8, :].bitcast(I32), in_=tab_scales[a].bitcast(I32))
         load_tab(0, 0, T)
-        nc.sync.dma_start(out=gains[:], in_=gain.rearrange("(b p t) -> p b t", b=PASSES, t=PACK))
         load_tab(1, 0, T)
         picked_sc = held([P, PASSES, S], U8, "picked_sc")
         for a in range(PASSES):
@@ -99,6 +98,7 @@ def tile_list_tape_restore_residuals_kernel(
         load_scales(w3_sc, 0, w3_scales)
         load_w1(0, 1, (0, 64), (64, P))
         load_w1(1, 1, (0, 64), (64, P))
+        nc.sync.dma_start(out=gains[:], in_=gain.rearrange("(b p t) -> p b t", b=PASSES, t=PACK))
         nc.sync.dma_start(out=w4[:].bitcast(I32), in_=w4_words.rearrange("a p c -> p a c").bitcast(I32))
         nc.sync.dma_start(out=w3[:].bitcast(I32), in_=w3_words.rearrange("a p c i -> p a (c i)").bitcast(I32))
         nc.sync.dma_start(places[:], offs2)

@@ -21,7 +21,6 @@ PACK = 4
 PASS = P * PACK
 PASSES = 2
 N_TILES = N // P
-HALF = S // 2
 PIECE = 128
 QUARTER = 256
 V_ROW = 8
@@ -38,6 +37,9 @@ def tile_list_tape_restore_residuals_kernel(
         def held(shape, dtype, name, tag=None):
             return keep.tile(shape, dtype, name=name, tag=tag or name, align_bytes=64)
 
+        def bank(number, shape, name):
+            return psum.tile(shape, F32, tag="bank%d" % number, name=name)
+
         picks = keep.tile([P, S // 16], U16, name="picks")
         places = keep.tile([P, S // 16], U16, name="places")
         tab = [held([P, T], I32, "tab%d" % a) for a in range(PASSES)]
@@ -51,87 +53,75 @@ def tile_list_tape_restore_residuals_kernel(
         nc.vector.memset(w4_sc[:].bitcast(I32), 0)
         nc.vector.memset(w3_sc[:].bitcast(I32), 0)
 
-        def load_tab(a, c0, c1):
-            nc.sync.dma_start(
-                out=tab[a][:, c0:c1], in_=tab_words[a].rearrange("p t i -> p (t i)").bitcast(I32)[:, c0:c1]
-            )
-
+        raw = [held([P, PACK, H], F32, "raw%d" % a) for a in range(PASSES)]
         gains = held([P, PASSES, PACK], F32, "gains")
-        raw = {}
-
-        def load_w1(a, b, *runs):
-            raw.setdefault((a, b), [])
-            for m0, m1 in runs:
-                width = PACK * (m1 - m0)
-                t_raw = held([P, PACK, width], F32, "raw%d%d_%d" % (a, b, m0))
-                c0 = PASS * b + PACK * m0
-                nc.sync.dma_start(
-                    out=t_raw[:],
-                    in_=w1[PASS * a : PASS * (a + 1), c0 : c0 + width].rearrange("(p j) c -> p j c", j=PACK),
-                )
-                raw[(a, b)].append((m0, t_raw))
-
-        def load_scales(sc, first_row, src):
-            for r in range(4):
-                nc.gpsimd.dma_start(
-                    out=sc[first_row + r : P : 32, :, :].bitcast(I32),
-                    in_=src[:, r:16:4, :].rearrange("a q c -> q a c").bitcast(I32),
-                )
-
         w3 = held([P, PASSES, N], U32, "w3")
         w4 = held([P, PASSES, 2 * N], U8, "w4")
         weight = held([P, S], F32, "weight")
+        picked_sc = held([P, PASSES, S], U8, "picked_sc")
 
-        load_w1(0, 0, (0, P))
+        def load_w1(a):
+            nc.sync.dma_start(out=raw[a][:], in_=w1[PASS * a : PASS * (a + 1), :].rearrange("(p j) c -> p j c", j=PACK))
+
+        def load_tab(a):
+            nc.sync.dma_start(out=tab[a][:], in_=tab_words[a].rearrange("p t i -> p (t i)").bitcast(I32))
+
+        def load_scales(sc, src):
+            for r in range(4):
+                nc.gpsimd.dma_start(
+                    out=sc[r:P:32, :, :].bitcast(I32), in_=src[:, r:16:4, :].rearrange("a q c -> q a c").bitcast(I32)
+                )
+
+        load_w1(0)
         nc.sync.dma_start(picks[:], offs)
         for a in range(PASSES):
             nc.sync.dma_start(out=tab_sc[a][4:P:8, :].bitcast(I32), in_=tab_scales[a].bitcast(I32))
-        load_tab(0, 0, T)
-        load_tab(1, 0, T)
-        picked_sc = held([P, PASSES, S], U8, "picked_sc")
+        load_w1(1)
+        load_tab(0)
         for a in range(PASSES):
             nc.vector.tensor_copy(picked_sc[:, a, :], tab_sc[a][:].indirect(picks[:]))
         for r in range(4):
-            nc.sync.dma_start(out=v_sc[V_ROW + r : P : 32, :, :].bitcast(I32), in_=picked_sc[4 + 8 * r : P : 32, :, :].bitcast(I32))
-        load_w1(1, 0, (0, 64), (64, P))
-        load_scales(w4_sc, 0, w4_scales)
-        load_scales(w3_sc, 0, w3_scales)
-        load_w1(0, 1, (0, 64), (64, P))
-        load_w1(1, 1, (0, 64), (64, P))
+            nc.sync.dma_start(
+                out=v_sc[V_ROW + r : P : 32, :, :].bitcast(I32), in_=picked_sc[4 + 8 * r : P : 32, :, :].bitcast(I32)
+            )
+        load_tab(1)
+        load_scales(w4_sc, w4_scales)
+        load_scales(w3_sc, w3_scales)
         nc.sync.dma_start(out=gains[:], in_=gain.rearrange("(b p t) -> p b t", b=PASSES, t=PACK))
         nc.sync.dma_start(out=w4[:].bitcast(I32), in_=w4_words.rearrange("a p c -> p a c").bitcast(I32))
         nc.sync.dma_start(out=w3[:].bitcast(I32), in_=w3_words.rearrange("a p c i -> p a (c i)").bitcast(I32))
         nc.sync.dma_start(places[:], offs2)
         nc.sync.dma_start(out=weight[:], in_=wgo)
 
-        v = [held([P, S], U32, "v%d" % a) for a in range(PASSES)]
         w1c, w1s = {}, {}
 
-        def quantise_w1(a, b, calls, copies):
+        def quantise_w1(a, b, copy_rows):
             grouped = held([P, PACK, P, PACK], BF16, "grouped%d%d" % (a, b))
             w1c[(a, b)] = held([P, PASS], U32, "w1c%d%d" % (a, b))
             w1s[(a, b)] = held([P, PASS], U8, "w1s%d%d" % (a, b))
-            for copy_rows, part, m0, m1 in copies:
-                first, t_raw = raw[(a, b)][part]
-                copy_rows(
-                    out=grouped[:, :, m0:m1, :].rearrange("p t m j -> p m j t"),
-                    in_=t_raw[:].rearrange("p j (m t) -> p m j t", t=PACK)[:, m0 - first : m1 - first, :, :],
-                )
-            tw = PACK // calls
-            for u in range(calls):
-                nc.vector.quantize_mx(
-                    out=w1c[(a, b)][:, u * tw * P : (u + 1) * tw * P].bitcast(FP8X4),
-                    scales=w1s[(a, b)][:, u * tw * P : (u + 1) * tw * P],
-                    in_=grouped[:, u * tw : (u + 1) * tw, :, :].rearrange("p t m j -> p (t m j)"),
-                )
+            copy_rows(
+                out=grouped[:].rearrange("p t m j -> p m j t"),
+                in_=raw[a][:, :, PASS * b : PASS * (b + 1)].rearrange("p j (m t) -> p m j t", t=PACK),
+            )
+            nc.vector.quantize_mx(
+                out=w1c[(a, b)][:].bitcast(FP8X4), scales=w1s[(a, b)][:], in_=grouped[:].rearrange("p t m j -> p (t m j)")
+            )
 
-        on_vector, on_scalar = nc.vector.tensor_copy, nc.scalar.copy
-        quantise_w1(0, 0, 1, [(on_scalar, 0, 0, P)])
-        for a in range(PASSES):
-            nc.vector.tensor_copy(v[a][:], tab[a][:].bitcast(U32).indirect(picks[:]))
-        quantise_w1(1, 0, 4, [(on_scalar, 0, 0, 64), (on_vector, 1, 64, 104), (on_scalar, 1, 104, P)])
-        quantise_w1(0, 1, 1, [(on_vector, 0, 0, 64), (on_vector, 1, 64, P)])
-        quantise_w1(1, 1, 4, [(on_vector, 0, 0, 64), (on_vector, 1, 64, P)])
+        quantise_w1(0, 0, nc.scalar.copy)
+        quantise_w1(0, 1, nc.scalar.copy)
+        quantise_w1(1, 0, nc.scalar.copy)
+        quantise_w1(1, 1, nc.vector.tensor_copy)
+
+        v = [held([P, S], U32, "v%d" % a) for a in range(PASSES)]
+
+        def gather(a, c0, c1):
+            nc.vector.tensor_copy(v[a][:, c0:c1], tab[a][:].bitcast(U32).indirect(picks[:, c0 // 16 : c1 // 16]))
+
+        gather(0, 0, S // 2)
+        gather(0, S // 2, S)
+        gather(1, 0, QUARTER)
+        gather(1, QUARTER, 2 * QUARTER)
+        gather(1, 2 * QUARTER, S)
 
         feats = held([P, N_TILES, S], F32, "feats", tag="tab0")
         for n in range(N_TILES):
@@ -139,8 +129,16 @@ def tile_list_tape_restore_residuals_kernel(
 
         hc = [held([P, S], U32, "hc%d" % b) for b in range(PASSES)]
         hs = {}
+        pages = [held([P, S], F32, "page%d" % n) for n in range(N_TILES)]
+        low, high = range(0, 2), range(2, 4)
+        pieces = [slice(PIECE * i, PIECE * (i + 1)) for i in range(S // PIECE)]
+        quarters = [slice(QUARTER * g, QUARTER * (g + 1)) for g in range(S // QUARTER)]
 
-        def z_group(z, b, ts, cols):
+        def width(cols):
+            return cols.stop - cols.start
+
+        def z_product(number, b, ts, cols):
+            z = bank(number, [P, len(ts), width(cols)], "z")
             for a in range(PASSES):
                 for i, t in enumerate(ts):
                     nc.tensor.matmul_mx(
@@ -152,6 +150,7 @@ def tile_list_tape_restore_residuals_kernel(
                         start=(a, i) == (0, 0),
                         stop=(a, i) == (PASSES - 1, len(ts) - 1),
                     )
+            return z
 
         def w3_passes(y, ns, cols, opens=False, closes=False):
             for a in range(PASSES):
@@ -179,271 +178,220 @@ def tile_list_tape_restore_residuals_kernel(
                     stop=closes and i == len(ns) - 1,
                 )
 
-        def quantise_h(b, cols, woven, tag=None):
-            plane = held([P, cols.stop - cols.start], U8, "hs%d_%d" % (b, cols.start), tag=tag)
-            hs[(b, cols.start)] = plane[:]
-            nc.vector.quantize_mx(
-                out=hc[b][:, cols].bitcast(FP8X4), scales=plane[:], in_=woven.rearrange("p j t -> p (j t)")
-            )
-
-        pages = [held([P, S], F32, "page%d" % n) for n in range(N_TILES)]
-
-        def scatter(n, values, cols):
-            nc.vector.tensor_tensor(
-                pages[n][:].indirect(places[:, cols.start // 16 : cols.stop // 16]), values, weight[:, cols], MULT
-            )
-
-        def scatter_copy(n, values, cols):
-            nc.vector.tensor_copy(pages[n][:].indirect(places[:, cols.start // 16 : cols.stop // 16]), values)
-
-        def bank(number, shape, name):
-            return psum.tile(shape, F32, tag="bank%d" % number, name=name)
-
-        pieces = [slice(PIECE * i, PIECE * (i + 1)) for i in range(6)]
-        th_piece = {}
-
-        z_pieces = {}
-
-        def z_piece(i, b, number):
-            z_pieces[(i, b)] = bank(number, [P, PACK, PIECE], "z")
-            z_group(z_pieces[(i, b)], b, range(PACK), pieces[i])
-
-        def tanh_piece(i, b, number, th=None):
-            if number is not None:
-                z_piece(i, b, number)
-            z = z_pieces[(i, b)]
-            th_piece[(i, b)] = held([P, PIECE, PACK], F32, "thp%d%d" % (i, b))[:] if th is None else th
-            nc.scalar.activation(
-                out=th_piece[(i, b)], in_=z[:].rearrange("p t j -> p j t"), func=ACT.Tanh, scale=-1.0
-            )
-
-        def gain_on_vector(hb, th, b, engine=nc.vector):
-            engine.tensor_tensor(hb, th, gains[:, b : b + 1, :].to_broadcast(list(th.shape)), MULT)
-
-        def gain_piece(i, b, hb):
-            gain_on_vector(hb, th_piece[(i, b)], b)
-
-        units = {g: slice(QUARTER * g, QUARTER * (g + 1)) for g in range(1, 4)}
-        ths, planes_of = {}, {}
-
-        zs = {}
-
-        def z_bank(g, b, ts, number):
-            zs[(g, b, ts[0])] = bank(number, [P, len(ts), QUARTER], "z")
-            z_group(zs[(g, b, ts[0])], b, ts, units[g])
-
-        def tanh_bank(g, b, ts, tag=None):
-            z = zs[(g, b, ts[0])]
-            th = held([P, len(ts), QUARTER], F32, "th%d%d%d" % (g, b, ts[0]), tag=tag)
-            nc.scalar.activation(out=th[:], in_=z[:], func=ACT.Tanh, scale=-1.0)
-            for i, t in enumerate(ts):
-                ths[(g, b, t)] = th[:, i, :]
-
-        def apply_gain(g, b, tag=None):
-            planes = held([P, PACK, units[g].stop - units[g].start], BF16, "planes%d%d" % (g, b), tag=tag)
-            for t in range(PACK):
-                nc.scalar.activation(
-                    out=planes[:, t, :], in_=ths[(g, b, t)], func=ACT.Copy, scale=gains[:, b, t : t + 1]
-                )
-            planes_of[(g, b)] = planes
-
-        def weave(g, b, tag=None, plane_tag=None):
-            woven = held([P, units[g].stop - units[g].start, PACK], BF16, "woven%d%d" % (g, b), tag=tag)
-            nc.scalar.copy(
-                out=woven[:].rearrange("p (c i) t -> p c t i", i=4),
-                in_=planes_of[(g, b)][:].rearrange("p t (c i) -> p c t i", i=4),
-            )
-            quantise_h(b, units[g], woven[:], plane_tag)
-
         def open_y(number, ns, cols):
-            y = bank(number, [P, len(ns), cols.stop - cols.start], "y")
-            w4_passes(y, 0, ns, cols, opens=True)
-            w3_passes(y, ns, cols)
-            return y
-
-        def open_early(number, ns, cols):
-            y = bank(number, [P, len(ns), cols.stop - cols.start], "y")
+            y = bank(number, [P, len(ns), width(cols)], "y")
             w3_passes(y, ns, cols, opens=True)
             return y
 
-        def close_y(y, ns, cols):
-            w4_passes(y, 1, ns, cols, closes=True)
-
         def whole_y(number, ns, cols):
-            y = bank(number, [P, len(ns), cols.stop - cols.start], "y")
+            y = bank(number, [P, len(ns), width(cols)], "y")
             w4_passes(y, 1, ns, cols, opens=True)
             w4_passes(y, 0, ns, cols)
             w3_passes(y, ns, cols, closes=True)
             return y
 
+        def tanh_woven(th, z):
+            nc.scalar.activation(out=th, in_=z[:].rearrange("p t j -> p j t"), func=ACT.Tanh, scale=-1.0)
+
+        def tanh_planes(th, z):
+            nc.scalar.activation(out=th, in_=z[:], func=ACT.Tanh, scale=-1.0)
+
+        def gain_woven(engine, hb, th, b):
+            engine.tensor_tensor(hb, th, gains[:, b : b + 1, :].to_broadcast(list(th.shape)), MULT)
+
+        def gain_planes(planes, th_low, th_high, b):
+            for t in range(PACK):
+                th = (th_low, th_high)[t // 2]
+                nc.scalar.activation(out=planes[:, t, :], in_=th[:, t % 2, :], func=ACT.Copy, scale=gains[:, b, t : t + 1])
+
+        def weave(woven, planes):
+            nc.scalar.copy(
+                out=woven.rearrange("p (c i) t -> p c t i", i=4), in_=planes.rearrange("p t (c i) -> p c t i", i=4)
+            )
+
+        def quantise_h(b, cols, woven):
+            plane = held([P, width(cols)], U8, "hs%d_%d" % (b, cols.start))
+            hs[(b, cols.start)] = plane[:]
+            nc.vector.quantize_mx(
+                out=hc[b][:, cols].bitcast(FP8X4), scales=plane[:], in_=woven.rearrange("p j t -> p (j t)")
+            )
+
         def evacuate(values, y):
             nc.scalar.activation(out=values, in_=y, func=ACT.Abs)
 
-        def place(y, rows, ns, cols, tag=None, values=None):
-            if values is None:
-                values = held([P, len(ns), cols.stop - cols.start], F32, "ys%d_%d" % (cols.start, ns[0]), tag=tag)[:]
-            evacuate(values, y[:, rows, :])
-            for i, n in enumerate(ns):
-                scatter(n, values[:, i, :], cols)
-            return values
+        def weigh(engine, weighed, values, cols):
+            factor = weight[:, cols]
+            if len(values.shape) == 3:
+                factor = factor.unsqueeze(1).to_broadcast(list(values.shape))
+            engine.tensor_tensor(weighed, values, factor, MULT)
 
-        low, high, every = range(0, 2), range(2, 4), range(4)
-        both = slice(0, 2)
+        def window(n, cols):
+            return pages[n][:].indirect(places[:, cols.start // 16 : cols.stop // 16])
 
-        tanh_piece(0, 0, 0)
-        tanh_piece(1, 0, 1)
-        th_second = held([P, QUARTER, PACK], F32, "th_second")
-        tanh_piece(2, 0, 2, th_second[:, :PIECE, :])
-        tanh_piece(3, 0, 3, th_second[:, PIECE:, :])
-        z_bank(2, 0, low, 6)
-        z_bank(2, 0, high, 7)
-        tanh_bank(2, 0, low, "th2")
-        tanh_bank(2, 0, high, "th3")
-        z_piece(0, 1, 4)
-        th_piece[(0, 1)] = held([P, PIECE, PACK], F32, "thp01")[:]
-        halves = (slice(0, PIECE // 2), slice(PIECE // 2, PIECE))
-        for half in halves:
-            nc.scalar.activation(
-                out=th_piece[(0, 1)][:, half, :],
-                in_=z_pieces[(0, 1)][:, :, half].rearrange("p t j -> p j t"),
-                func=ACT.Tanh,
-                scale=-1.0,
-            )
-        tanh_piece(1, 1, 5)
-        apply_gain(2, 0)
+        def scatter_weighing(n, values, cols):
+            nc.vector.tensor_tensor(window(n, cols), values, weight[:, cols], MULT)
 
-        hb0 = held([P, 2, PIECE, PACK], BF16, "hb0", tag="grouped11")
-        hb1 = [held([P, PIECE, PACK], BF16, "hb10")]
-        gain_piece(0, 0, hb0[:, 0, :, :])
-        gain_piece(1, 0, hb0[:, 1, :, :])
-        quantise_h(0, pieces[0], hb0[:, 0, :, :])
-        y_a0 = open_y(0, low, pieces[0])
-        y_a1 = open_y(6, high, pieces[0])
-        for half in halves:
-            gain_on_vector(hb1[0][:, half, :], th_piece[(0, 1)][:, half, :], 1)
-        quantise_h(0, pieces[1], hb0[:, 1, :, :])
-        quantise_h(1, pieces[0], hb1[0][:])
-        close_y(y_a0, low, pieces[0])
-        close_y(y_a1, high, pieces[0])
-        z_bank(1, 1, low, 2)
-        z_bank(1, 1, high, 3)
-        hb1.append(held([P, PIECE, PACK], BF16, "hb11", tag="hb10"))
-        gain_piece(1, 1, hb1[1][:])
-        first = held([P, 2, PIECE], F32, "first")
-        evacuate(first[:], y_a0[:])
-        nc.vector.tensor_tensor(first[:], first[:], weight[:, pieces[0]].unsqueeze(1).to_broadcast([P, 2, PIECE]), MULT)
-        quantise_h(1, pieces[1], hb1[1][:])
+        def scatter_copy(n, values, cols):
+            nc.vector.tensor_copy(window(n, cols), values)
+
+        th_first, hb_first = {}, {}
+        for i in range(2):
+            for b in range(PASSES):
+                th_first[(i, b)] = held([P, PIECE, PACK], F32, "th_first%d%d" % (i, b))
+                tanh_woven(th_first[(i, b)][:], z_product(2 * i + b, b, range(PACK), pieces[i]))
+        th_c0 = held([P, QUARTER, PACK], F32, "th_c0")
+        z_c0 = [z_product(4 + i, 0, range(PACK), pieces[2 + i]) for i in range(2)]
+        y_a = [open_y(6, low, pieces[0]), open_y(7, high, pieces[0])]
+        for b in range(PASSES):
+            hb_first[(0, b)] = held([P, PIECE, PACK], BF16, "hb_first0%d" % b)
+            gain_woven(nc.vector, hb_first[(0, b)][:], th_first[(0, b)][:], b)
+        for b in range(PASSES):
+            quantise_h(b, pieces[0], hb_first[(0, b)][:])
+            for y, ns in zip(y_a, (low, high)):
+                w4_passes(y, b, ns, pieces[0], closes=b == 1)
+        z_c1 = [z_product(i, 1, ts, quarters[1]) for i, ts in enumerate((low, high))]
+        raw_a = held([P, 2, PIECE], F32, "raw_a")
+        evacuate(raw_a[:], y_a[1][:])
+        for i in range(2):
+            tanh_woven(th_c0[:, pieces[i], :], z_c0[i])
+        for b in range(PASSES):
+            hb_first[(1, b)] = held([P, PIECE, PACK], BF16, "hb_first1%d" % b)
+            gain_woven(nc.vector, hb_first[(1, b)][:], th_first[(1, b)][:], b)
+        quantise_h(0, pieces[1], hb_first[(1, 0)][:])
+        weighed_a = held([P, 2, PIECE], F32, "weighed_a")
+        weigh(nc.vector, weighed_a[:], y_a[0][:], pieces[0])
+        quantise_h(1, pieces[1], hb_first[(1, 1)][:])
+        y_b = [whole_y(2, low, pieces[1]), whole_y(3, high, pieces[1])]
+
+        after_b = held([P, QUARTER + PASS], F32, "after_b", tag="hb_first11")
+        weighed_a_high = after_b[:, :QUARTER].rearrange("p (n j) -> p n j", n=2)
+        hb_c0 = after_b[:, QUARTER:].bitcast(BF16).rearrange("p (j t) -> p j t", t=PACK)
+        weigh(nc.gpsimd, weighed_a_high, raw_a[:], pieces[0])
+        for i in range(2):
+            gain_woven(nc.gpsimd, hb_c0[:, pieces[i], :], th_c0[:, pieces[i], :], 0)
         for n in low:
-            scatter_copy(n, first[:, n, :], pieces[0])
-        y_b = [whole_y(4, low, pieces[1]), whole_y(5, high, pieces[1])]
-        raw_high = held([P, 2, PIECE], F32, "raw_high")
-        first_high = held([P, 2, PIECE], F32, "first_high")
-        evacuate(raw_high[:], y_a1[:])
-        nc.vector.tensor_tensor(
-            first_high[:], raw_high[:], weight[:, pieces[0]].unsqueeze(1).to_broadcast([P, 2, PIECE]), MULT
-        )
+            scatter_copy(n, weighed_a[:, n, :], pieces[0])
         for n in high:
-            scatter_copy(n, first_high[:, n - 2, :], pieces[0])
-        hb_second = held([P, QUARTER, PACK], BF16, "hb_second", tag="raw_high")
-        for c0 in (0, PIECE):
-            gain_on_vector(hb_second[:, c0 : c0 + PIECE, :], th_second[:, c0 : c0 + PIECE, :], 0, nc.gpsimd)
-        quantise_h(0, units[1], hb_second[:])
-        z_piece(4, 1, 0)
-        z_piece(5, 1, 6)
-        tanh_bank(1, 1, low, "th0")
-        tanh_bank(1, 1, high, "th1")
-        y_1 = [open_y(1, low, units[1]), open_y(7, high, units[1])]
-        z_bank(3, 0, low, 2)
-        z_bank(3, 0, high, 3)
+            scatter_copy(n, weighed_a_high[:, n - 2, :], pieces[0])
 
-        apply_gain(1, 1)
-        weave(1, 1)
-        close_y(y_1[0], low, units[1])
-        close_y(y_1[1], high, units[1])
-        after_weave = held([P, PASS + S], F32, "after_weave", tag="planes11")
-        rest_b = after_weave[:, :PASS].rearrange("p (n j) -> p n j", n=N_TILES)
-        th_third = after_weave[:, PASS:].rearrange("p (j t) -> p j t", t=PACK)
-        after_quantise = held([P, QUARTER + PASS], F32, "after_quantise", tag="woven11")
-        hb_third = after_quantise[:, QUARTER:].bitcast(BF16).rearrange("p (j t) -> p j t", t=PACK)
-        weighed_b = [
-            held([P, 2, PIECE], F32, "weighed_b")[:],
-            after_quantise[:, :QUARTER].rearrange("p (n j) -> p n j", n=2),
-        ]
-        evacuate(rest_b[:, 0:2, :], y_b[0][:])
-        evacuate(rest_b[:, 2:4, :], y_b[1][:])
-        for engine, values, ns in zip((nc.vector, nc.gpsimd), weighed_b, (low, high)):
-            engine.tensor_tensor(
-                values,
-                rest_b[:, ns.start : ns.stop, :],
-                weight[:, pieces[1]].unsqueeze(1).to_broadcast([P, 2, PIECE]),
-                MULT,
-            )
-            for n in ns:
-                scatter_copy(n, values[:, n - ns.start, :], pieces[1])
-        tanh_piece(4, 1, None, th_third[:, :PIECE, :])
-        tanh_piece(5, 1, None, th_third[:, PIECE:, :])
-        for c0 in (0, PIECE):
-            gain_on_vector(hb_third[:, c0 : c0 + PIECE, :], th_third[:, c0 : c0 + PIECE, :], 1, nc.gpsimd)
-        weave(2, 0, tag="th1")
-        z_bank(3, 1, low, 0)
-        z_bank(3, 1, high, 6)
-        y_2 = [open_y(4, low, units[2]), open_y(5, high, units[2])]
-        quantise_h(1, units[2], hb_third)
-        close_y(y_2[0], low, units[2])
-        close_y(y_2[1], high, units[2])
-        tanh_bank(3, 0, low, "th3")
-        tanh_bank(3, 0, high, "th0")
-        place(y_1[0], slice(0, 1), range(0, 1), units[1])
-        apply_gain(3, 0)
-        place(y_1[0], slice(1, 2), range(1, 2), units[1])
-        place(y_1[1], slice(0, 1), range(2, 3), units[1])
-        y_3 = [open_early(2, low, units[3]), open_early(3, high, units[3])]
-        weave(3, 0)
-        w4_passes(y_3[0], 0, low, units[3])
-        w4_passes(y_3[1], 0, high, units[3])
-        tanh_bank(3, 1, low, "th0")
-        tanh_bank(3, 1, high, "th3")
-        place(y_2[0], slice(0, 1), range(0, 1), units[2], tag="planes30")
-        apply_gain(3, 1)
-        weave(3, 1)
-        close_y(y_3[0], low, units[3])
-        close_y(y_3[1], high, units[3])
+        z_d1 = [z_product(4 + i, 1, range(PACK), pieces[4 + i]) for i in range(2)]
+        th_pair = [held([P, 2, QUARTER], F32, "th_c1_%d" % i, tag="th_pair%d" % i) for i in range(2)]
+        for th, z in zip(th_pair, z_c1):
+            tanh_planes(th[:], z)
+        z_d0 = [z_product(i, 0, ts, quarters[2]) for i, ts in enumerate((low, high))]
+        y_c = [open_y(6, low, quarters[1]), open_y(7, high, quarters[1])]
+        planes_c1 = held([P, PACK, QUARTER], BF16, "planes_c1")
+        gain_planes(planes_c1, th_pair[0], th_pair[1], 1)
+        woven_c1 = held([P, QUARTER, PACK], BF16, "woven_c1")
+        weave(woven_c1[:], planes_c1[:])
+        quantise_h(0, quarters[1], hb_c0)
+        quantise_h(1, quarters[1], woven_c1[:])
+        for b in range(PASSES):
+            for y, ns in zip(y_c, (low, high)):
+                w4_passes(y, b, ns, quarters[1], closes=b == 1)
 
+        after_weave = held([P, PASS + S], F32, "after_weave", tag="planes_c1")
+        raw_b = after_weave[:, :PASS].rearrange("p (n j) -> p n j", n=N_TILES)
+        th_d1 = after_weave[:, PASS:].rearrange("p (j t) -> p j t", t=PACK)
+        after_c = held([P, 2 * QUARTER + PASS], F32, "after_c", tag="woven_c1")
+        weighed_b = after_c[:, :QUARTER].rearrange("p (n j) -> p n j", n=2)
+        weighed_b_high = after_c[:, QUARTER : 2 * QUARTER].rearrange("p (n j) -> p n j", n=2)
+        hb_d1 = after_c[:, 2 * QUARTER :].bitcast(BF16).rearrange("p (j t) -> p j t", t=PACK)
+        evacuate(raw_b[:, 2:4, :], y_b[1][:])
+        weigh(nc.vector, weighed_b, y_b[0][:], pieces[1])
+        weigh(nc.gpsimd, weighed_b_high, raw_b[:, 2:4, :], pieces[1])
+        for n in low:
+            scatter_copy(n, weighed_b[:, n, :], pieces[1])
+        for n in high:
+            scatter_copy(n, weighed_b_high[:, n - 2, :], pieces[1])
+        for i in range(2):
+            tanh_woven(th_d1[:, pieces[i], :], z_d1[i])
+        for i in range(2):
+            gain_woven(nc.gpsimd, hb_d1[:, pieces[i], :], th_d1[:, pieces[i], :], 1)
+        z_e0 = [z_product(2 + i, 0, ts, quarters[3]) for i, ts in enumerate((low, high))]
+        z_e1 = [z_product(4 + i, 1, ts, quarters[3]) for i, ts in enumerate((low, high))]
+        th_pair = [held([P, 2, QUARTER], F32, "th_d0_%d" % i, tag="th_pair%d" % i) for i in range(2)]
+        for th, z in zip(th_pair, z_d0):
+            tanh_planes(th[:], z)
+        y_d = [open_y(0, low, quarters[2]), open_y(1, high, quarters[2])]
 
-        def size_of_features(n):
+        def place(n, y_rows, cols, tag=None):
+            values = held([P, width(cols)], F32, "values%d_%d" % (n, cols.start), tag=tag)
+            evacuate(values[:], y_rows)
+            scatter_weighing(n, values[:], cols)
+
+        place(0, y_c[0][:, 0, :], quarters[1])
+        planes_d0 = held([P, PACK, QUARTER], BF16, "planes_d0")
+        gain_planes(planes_d0, th_pair[0], th_pair[1], 0)
+        woven_d0 = held([P, QUARTER, PACK], BF16, "woven_d0")
+        weave(woven_d0[:], planes_d0[:])
+        quantise_h(1, quarters[2], hb_d1)
+        quantise_h(0, quarters[2], woven_d0[:])
+        for b in (1, 0):
+            for y, ns in zip(y_d, (low, high)):
+                w4_passes(y, b, ns, quarters[2], closes=b == 0)
+        after_d = held([P, 2, QUARTER], F32, "after_d", tag="planes_d0")
+        evacuate(after_d[:, 0, :], y_c[0][:, 1, :])
+        evacuate(after_d[:, 1, :], y_c[1][:, 0, :])
+        scatter_weighing(1, after_d[:, 0, :], quarters[1])
+        scatter_weighing(2, after_d[:, 1, :], quarters[1])
+
+        th_pair = [held([P, 2, QUARTER], F32, "th_e0_%d" % i, tag="th_pair%d" % i) for i in range(2)]
+        for th, z in zip(th_pair, z_e0):
+            tanh_planes(th[:], z)
+        place(0, y_d[0][:, 0, :], quarters[2])
+        planes_e0 = held([P, PACK, QUARTER], BF16, "planes_e0")
+        gain_planes(planes_e0, th_pair[0], th_pair[1], 0)
+        woven_e0 = held([P, QUARTER, PACK], BF16, "woven_e0")
+        weave(woven_e0[:], planes_e0[:])
+        quantise_h(0, quarters[3], woven_e0[:])
+        place(1, y_d[0][:, 1, :], quarters[2], tag="planes_e0")
+        th_pair = [held([P, 2, QUARTER], F32, "th_e1_%d" % i, tag="th_pair%d" % i) for i in range(2)]
+        for th, z in zip(th_pair, z_e1):
+            tanh_planes(th[:], z)
+        rows_e = (range(0, 1), range(1, 3), range(3, 4))
+        y_e = [open_y(number, ns, quarters[3]) for number, ns in zip((2, 3, 4), rows_e)]
+        for y, ns in zip(y_e, rows_e):
+            w4_passes(y, 0, ns, quarters[3])
+        planes_e1 = held([P, PACK, QUARTER], BF16, "planes_e1")
+        gain_planes(planes_e1, th_pair[0], th_pair[1], 1)
+        woven_e1 = held([P, QUARTER, PACK], BF16, "woven_e1")
+        weave(woven_e1[:], planes_e1[:])
+        quantise_h(1, quarters[3], woven_e1[:])
+        for y, ns in zip(y_e, rows_e):
+            w4_passes(y, 1, ns, quarters[3], closes=True)
+
+        late = held([P, 3, QUARTER], F32, "late", tag="planes_e1")
+        evacuate(late[:, 0, :], y_d[1][:, 0, :])
+        evacuate(late[:, 1, :], y_c[1][:, 1, :])
+        evacuate(late[:, 2, :], y_d[1][:, 1, :])
+        bridge = held([P, QUARTER], F32, "bridge")
+        weigh(nc.vector, bridge[:], late[:, 0, :], quarters[2])
+        scatter_copy(2, bridge[:], quarters[2])
+        last = held([P, 3 * QUARTER], F32, "last", tag="woven_e1")
+        values_e = held([P, N_TILES, QUARTER], F32, "values_e")
+        evacuate(values_e[:, 0, :], y_e[0][:, 0, :])
+        evacuate(values_e[:, 1:3, :], y_e[1][:])
+        evacuate(values_e[:, 3, :], y_e[2][:, 0, :])
+        for n in range(3):
+            weigh(nc.gpsimd, values_e[:, n, :], values_e[:, n, :], quarters[3])
+        weigh(nc.gpsimd, last[:, : 2 * QUARTER], late[:, 1:3, :].rearrange("p g j -> p (g j)"), slice(QUARTER, 3 * QUARTER))
+        weigh(nc.gpsimd, last[:, 2 * QUARTER :], values_e[:, 3, :], quarters[3])
+        sizes = held([P, N_TILES, S], F32, "sizes", tag="planes_e1")
+        for n in high:
             nc.scalar.activation(out=sizes[:, n, :], in_=feats[:, n, :], func=ACT.Abs)
+        for n in range(3):
+            scatter_copy(n, values_e[:, n, :], quarters[3])
+        scatter_copy(3, last[:, : 3 * QUARTER], slice(QUARTER, S))
 
         def weigh_and_store(n, c0, c1, engine, product):
             engine.tensor_tensor(product, pages[n][:, c0:c1], sizes[:, n, c0:c1], MULT)
             nc.sync.dma_start(out=out[P * n : P * (n + 1), c0:c1], in_=product)
 
-        late = held([P, 4, QUARTER], F32, "late", tag="planes31")
-        bridge_raw, ends = late[:, 0, :], late[:, 1:4, :]
-        bridge = held([P, QUARTER], F32, "bridge")
-        evacuate(bridge_raw, y_2[0][:, 1, :])
-        evacuate(ends[:, 0:2, :], y_2[1][:])
-        evacuate(ends[:, 2, :], y_1[1][:, 1, :])
-        nc.vector.tensor_tensor(bridge[:], bridge_raw, weight[:, units[2]], MULT)
-        last = held([P, (N_TILES + 1) * S], F32, "last", tag="woven31")
-        weighed = last[:, :S].rearrange("p (n j) -> p n j", n=4)
-        sizes = last[:, S:].rearrange("p (n m) -> p n m", n=N_TILES)
-        nc.gpsimd.tensor_tensor(weighed[:, 0, :], ends[:, 0, :], weight[:, units[2]], MULT)
-        scatter_copy(1, bridge[:], units[2])
-        scatter_copy(2, weighed[:, 0, :], units[2])
-        ys_3 = held([P, N_TILES, QUARTER], F32, "ys_3")
-        evacuate(ys_3[:, 0:2, :], y_3[0][:])
-        evacuate(ys_3[:, 2:4, :], y_3[1][:])
-        for n in range(3):
-            nc.gpsimd.tensor_tensor(ys_3[:, n, :], ys_3[:, n, :], weight[:, units[3]], MULT)
-        nc.gpsimd.tensor_tensor(weighed[:, 1, :], ends[:, 2, :], weight[:, units[1]], MULT)
-        nc.gpsimd.tensor_tensor(weighed[:, 2, :], ends[:, 1, :], weight[:, units[2]], MULT)
-        nc.gpsimd.tensor_tensor(weighed[:, 3, :], ys_3[:, 3, :], weight[:, units[3]], MULT)
-        for n in every:
-            size_of_features(n)
-        for n in range(3):
-            scatter_copy(n, ys_3[:, n, :], units[3])
-        scatter_copy(3, last[:, QUARTER:S], slice(QUARTER, S))
-        for n in range(3):
-            weigh_and_store(n, 0, S, nc.gpsimd, feats[:, n, :])
+        for n in low:
+            nc.gpsimd.tensor_tensor(feats[:, n, :], pages[n][:], feats[:, n, :], MULT)
+            nc.scalar.activation(out=sizes[:, n, :], in_=feats[:, n, :], func=ACT.Abs)
+            nc.sync.dma_start(out=out[P * n : P * (n + 1), :], in_=sizes[:, n, :])
+        weigh_and_store(2, 0, S, nc.gpsimd, feats[:, 2, :])
         for c0 in range(0, S, QUARTER):
             weigh_and_store(3, c0, c0 + QUARTER, nc.vector, sizes[:, 2, c0 : c0 + QUARTER])

@@ -53,15 +53,18 @@ def tile_list_tape_restore_residuals_kernel(
         nc.vector.memset(w4_sc[:].bitcast(I32), 0)
         nc.vector.memset(w3_sc[:].bitcast(I32), 0)
 
-        raw = [held([P, PACK, H], F32, "raw%d" % a) for a in range(PASSES)]
+        raw = {}
         gains = held([P, PASSES, PACK], F32, "gains")
         w3 = held([P, PASSES, N], U32, "w3")
         w4 = held([P, PASSES, 2 * N], U8, "w4")
         weight = held([P, S], F32, "weight")
         picked_sc = held([P, PASSES, S], U8, "picked_sc")
 
-        def load_w1(a):
-            nc.sync.dma_start(out=raw[a][:], in_=w1[PASS * a : PASS * (a + 1), :].rearrange("(p j) c -> p j c", j=PACK))
+        def load_w1(a, c0, c1):
+            raw[(a, c0)] = held([P, PACK, c1 - c0], F32, "raw%d_%d" % (a, c0))
+            nc.sync.dma_start(
+                out=raw[(a, c0)][:], in_=w1[PASS * a : PASS * (a + 1), c0:c1].rearrange("(p j) c -> p j c", j=PACK)
+            )
 
         def load_tab(a):
             nc.sync.dma_start(out=tab[a][:], in_=tab_words[a].rearrange("p t i -> p (t i)").bitcast(I32))
@@ -72,11 +75,11 @@ def tile_list_tape_restore_residuals_kernel(
                     out=sc[r:P:32, :, :].bitcast(I32), in_=src[:, r:16:4, :].rearrange("a q c -> q a c").bitcast(I32)
                 )
 
-        load_w1(0)
+        load_w1(1, 0, PASS)
         nc.sync.dma_start(picks[:], offs)
         for a in range(PASSES):
             nc.sync.dma_start(out=tab_sc[a][4:P:8, :].bitcast(I32), in_=tab_scales[a].bitcast(I32))
-        load_w1(1)
+        load_w1(0, 0, H)
         load_tab(0)
         for a in range(PASSES):
             nc.vector.tensor_copy(picked_sc[:, a, :], tab_sc[a][:].indirect(picks[:]))
@@ -85,6 +88,8 @@ def tile_list_tape_restore_residuals_kernel(
                 out=v_sc[V_ROW + r : P : 32, :, :].bitcast(I32), in_=picked_sc[4 + 8 * r : P : 32, :, :].bitcast(I32)
             )
         load_tab(1)
+        load_w1(1, PASS, PASS + QUARTER)
+        load_w1(1, PASS + QUARTER, H)
         load_scales(w4_sc, w4_scales)
         load_scales(w3_sc, w3_scales)
         nc.sync.dma_start(out=gains[:], in_=gain.rearrange("(b p t) -> p b t", b=PASSES, t=PACK))
@@ -95,22 +100,29 @@ def tile_list_tape_restore_residuals_kernel(
 
         w1c, w1s = {}, {}
 
-        def quantise_w1(a, b, copy_rows):
+        def quantise_w1(a, b, calls, copies):
             grouped = held([P, PACK, P, PACK], BF16, "grouped%d%d" % (a, b))
             w1c[(a, b)] = held([P, PASS], U32, "w1c%d%d" % (a, b))
             w1s[(a, b)] = held([P, PASS], U8, "w1s%d%d" % (a, b))
-            copy_rows(
-                out=grouped[:].rearrange("p t m j -> p m j t"),
-                in_=raw[a][:, :, PASS * b : PASS * (b + 1)].rearrange("p j (m t) -> p m j t", t=PACK),
-            )
-            nc.vector.quantize_mx(
-                out=w1c[(a, b)][:].bitcast(FP8X4), scales=w1s[(a, b)][:], in_=grouped[:].rearrange("p t m j -> p (t m j)")
-            )
+            m0 = 0
+            for copy_rows, rows in copies:
+                m1 = m0 + rows.shape[2] // PACK
+                copy_rows(
+                    out=grouped[:, :, m0:m1, :].rearrange("p t m j -> p m j t"),
+                    in_=rows.rearrange("p j (m t) -> p m j t", t=PACK),
+                )
+                m0 = m1
+            tw = PACK // calls
+            for u in range(calls):
+                nc.vector.quantize_mx(
+                    out=w1c[(a, b)][:, u * tw * P : (u + 1) * tw * P].bitcast(FP8X4),
+                    scales=w1s[(a, b)][:, u * tw * P : (u + 1) * tw * P],
+                    in_=grouped[:, u * tw : (u + 1) * tw, :, :].rearrange("p t m j -> p (t m j)"),
+                )
 
-        quantise_w1(0, 0, nc.scalar.copy)
-        quantise_w1(0, 1, nc.scalar.copy)
-        quantise_w1(1, 0, nc.scalar.copy)
-        quantise_w1(1, 1, nc.vector.tensor_copy)
+        quantise_w1(1, 0, 1, [(nc.scalar.copy, raw[(1, 0)][:])])
+        quantise_w1(0, 0, 1, [(nc.scalar.copy, raw[(0, 0)][:, :, :PASS])])
+        quantise_w1(0, 1, 1, [(nc.scalar.copy, raw[(0, 0)][:, :, PASS:])])
 
         v = [held([P, S], U32, "v%d" % a) for a in range(PASSES)]
 
@@ -122,6 +134,9 @@ def tile_list_tape_restore_residuals_kernel(
         gather(1, 0, QUARTER)
         gather(1, QUARTER, 2 * QUARTER)
         gather(1, 2 * QUARTER, S)
+        quantise_w1(
+            1, 1, PACK, [(nc.scalar.copy, raw[(1, PASS)][:]), (nc.vector.tensor_copy, raw[(1, PASS + QUARTER)][:])]
+        )
 
         feats = held([P, N_TILES, S], F32, "feats", tag="tab0")
         for n in range(N_TILES):
@@ -129,7 +144,7 @@ def tile_list_tape_restore_residuals_kernel(
 
         hc = [held([P, S], U32, "hc%d" % b) for b in range(PASSES)]
         hs = {}
-        pages = [held([P, S], F32, "page%d" % n) for n in range(N_TILES)]
+        pages = [held([P, S], F32, "page%d" % n) for n in range(N_TILES - 1)]
         low, high = range(0, 2), range(2, 4)
         pieces = [slice(PIECE * i, PIECE * (i + 1)) for i in range(S // PIECE)]
         quarters = [slice(QUARTER * g, QUARTER * (g + 1)) for g in range(S // QUARTER)]
@@ -191,7 +206,7 @@ def tile_list_tape_restore_residuals_kernel(
             return y
 
         def tanh_woven(th, z):
-            nc.scalar.activation(out=th, in_=z[:].rearrange("p t j -> p j t"), func=ACT.Tanh, scale=-1.0)
+            nc.scalar.activation(out=th, in_=z[:, :, :].rearrange("p t j -> p j t"), func=ACT.Tanh, scale=-1.0)
 
         def tanh_planes(th, z):
             nc.scalar.activation(out=th, in_=z[:], func=ACT.Tanh, scale=-1.0)
@@ -209,12 +224,11 @@ def tile_list_tape_restore_residuals_kernel(
                 out=woven.rearrange("p (c i) t -> p c t i", i=4), in_=planes.rearrange("p t (c i) -> p c t i", i=4)
             )
 
-        def quantise_h(b, cols, woven):
-            plane = held([P, width(cols)], U8, "hs%d_%d" % (b, cols.start))
-            hs[(b, cols.start)] = plane[:]
-            nc.vector.quantize_mx(
-                out=hc[b][:, cols].bitcast(FP8X4), scales=plane[:], in_=woven.rearrange("p j t -> p (j t)")
-            )
+        def quantise_h(b, cols, woven, plane=None):
+            if plane is None:
+                plane = held([P, width(cols)], U8, "hs%d_%d" % (b, cols.start))[:]
+            hs[(b, cols.start)] = plane
+            nc.vector.quantize_mx(out=hc[b][:, cols].bitcast(FP8X4), scales=plane, in_=woven.rearrange("p j t -> p (j t)"))
 
         def evacuate(values, y):
             nc.scalar.activation(out=values, in_=y, func=ACT.Abs)
@@ -234,114 +248,126 @@ def tile_list_tape_restore_residuals_kernel(
         def scatter_copy(n, values, cols):
             nc.vector.tensor_copy(window(n, cols), values)
 
-        th_first, hb_first = {}, {}
+        th_first = {}
+        th_early = held([P, 2 * QUARTER, PACK], F32, "th_early", tag="raw1_%d" % PASS)
         for i in range(2):
-            for b in range(PASSES):
-                th_first[(i, b)] = held([P, PIECE, PACK], F32, "th_first%d%d" % (i, b))
-                tanh_woven(th_first[(i, b)][:], z_product(2 * i + b, b, range(PACK), pieces[i]))
-        th_c0 = held([P, QUARTER, PACK], F32, "th_c0")
-        z_c0 = [z_product(4 + i, 0, range(PACK), pieces[2 + i]) for i in range(2)]
-        y_a = [open_y(6, low, pieces[0]), open_y(7, high, pieces[0])]
-        for b in range(PASSES):
-            hb_first[(0, b)] = held([P, PIECE, PACK], BF16, "hb_first0%d" % b)
-            gain_woven(nc.vector, hb_first[(0, b)][:], th_first[(0, b)][:], b)
-        for b in range(PASSES):
-            quantise_h(b, pieces[0], hb_first[(0, b)][:])
-            for y, ns in zip(y_a, (low, high)):
-                w4_passes(y, b, ns, pieces[0], closes=b == 1)
+            th_first[(i, 1)] = held([P, PIECE, PACK], F32, "th_first%d" % i)
+            th_first[(i, 0)] = th_early[:, pieces[i], :]
+            tanh_woven(th_first[(i, 0)], z_product(i, 0, range(PACK), pieces[i]))
+        th_c0 = th_early[:, quarters[1], :]
+        for i in range(2):
+            tanh_woven(th_c0[:, pieces[i], :], z_product(2 + i, 0, range(PACK), pieces[2 + i]))
+        halves = (slice(0, PIECE // 2), slice(PIECE // 2, PIECE))
+        z_a1 = z_product(4, 1, range(PACK), pieces[0])
+        for half in halves:
+            tanh_woven(th_first[(0, 1)][:, half, :], z_a1[:, :, half])
+        tanh_woven(th_first[(1, 1)][:], z_product(5, 1, range(PACK), pieces[1]))
+        y_a0 = open_y(6, range(0, 1), pieces[0])
+        y_ab = bank(2, [P, 3, PIECE], "y")
+        w3_passes(y_ab[:, 0:1, :], range(1, 2), pieces[0], opens=True)
+        y_a_high = open_y(7, high, pieces[0])
+        hb_0 = held([P, 2, PIECE, PACK], BF16, "hb_0", tag="grouped11")
+        hb_a1 = held([P, PIECE, PACK], BF16, "hb_a1")
+        for i in range(2):
+            gain_woven(nc.vector, hb_0[:, i, :, :], th_first[(i, 0)], 0)
+        quantise_h(0, pieces[0], hb_0[:, 0, :, :])
+        rows_a = ((y_a0, range(0, 1)), (y_ab[:, 0:1, :], range(1, 2)), (y_a_high, high))
+        for y, ns in rows_a:
+            w4_passes(y, 0, ns, pieces[0])
+        for half in halves:
+            gain_woven(nc.vector, hb_a1[:, half, :], th_first[(0, 1)][:, half, :], 1)
+        quantise_h(0, pieces[1], hb_0[:, 1, :, :])
+        quantise_h(1, pieces[0], hb_a1[:])
+        for y, ns in rows_a:
+            w4_passes(y, 1, ns, pieces[0], closes=ns.start != 1)
+        w3_passes(y_ab[:, 1:3, :], (1, 0), pieces[1])
+        w4_passes(y_ab[:, 1:3, :], 0, (1, 0), pieces[1])
         z_c1 = [z_product(i, 1, ts, quarters[1]) for i, ts in enumerate((low, high))]
-        raw_a = held([P, 2, PIECE], F32, "raw_a")
-        evacuate(raw_a[:], y_a[1][:])
-        for i in range(2):
-            tanh_woven(th_c0[:, pieces[i], :], z_c0[i])
-        for b in range(PASSES):
-            hb_first[(1, b)] = held([P, PIECE, PACK], BF16, "hb_first1%d" % b)
-            gain_woven(nc.vector, hb_first[(1, b)][:], th_first[(1, b)][:], b)
-        quantise_h(0, pieces[1], hb_first[(1, 0)][:])
-        weighed_a = held([P, 2, PIECE], F32, "weighed_a")
-        weigh(nc.vector, weighed_a[:], y_a[0][:], pieces[0])
-        quantise_h(1, pieces[1], hb_first[(1, 1)][:])
-        y_b = [whole_y(2, low, pieces[1]), whole_y(3, high, pieces[1])]
+        values_high = held([P, 2, QUARTER], F32, "values_high")
+        evacuate(values_high[:, :, pieces[0]], y_a_high[:])
+        hb_b1 = held([P, PIECE, PACK], BF16, "hb_b1", tag="hb_a1")
+        gain_woven(nc.vector, hb_b1[:], th_first[(1, 1)][:], 1)
+        weighed_a0 = held([P, PIECE], F32, "weighed_a0")
+        weigh(nc.vector, weighed_a0[:], y_a0[:, 0, :], pieces[0])
+        quantise_h(1, pieces[1], hb_b1[:])
+        w4_passes(y_ab[:, 1:3, :], 1, (1, 0), pieces[1], closes=True)
+        y_b_high = whole_y(4, high, pieces[1])
 
-        after_b = held([P, QUARTER + PASS], F32, "after_b", tag="hb_first11")
-        weighed_a_high = after_b[:, :QUARTER].rearrange("p (n j) -> p n j", n=2)
-        hb_c0 = after_b[:, QUARTER:].bitcast(BF16).rearrange("p (j t) -> p j t", t=PACK)
-        weigh(nc.gpsimd, weighed_a_high, raw_a[:], pieces[0])
-        for i in range(2):
-            gain_woven(nc.gpsimd, hb_c0[:, pieces[i], :], th_c0[:, pieces[i], :], 0)
-        for n in low:
-            scatter_copy(n, weighed_a[:, n, :], pieces[0])
-        for n in high:
-            scatter_copy(n, weighed_a_high[:, n - 2, :], pieces[0])
+        hb_c0 = held([P, QUARTER, PACK], BF16, "hb_c0", tag="hb_a1")
+        gain_woven(nc.gpsimd, hb_c0[:], th_c0, 0)
+        scatter_copy(0, weighed_a0[:], pieces[0])
+        weighed_ab1 = held([P, QUARTER], F32, "weighed_ab1")
+        weighed_b0 = held([P, PIECE], F32, "weighed_b0")
+        weigh(nc.vector, weighed_ab1[:], y_ab[:, 0:2, :].rearrange("p i j -> p (i j)"), quarters[0])
+        weigh(nc.vector, weighed_b0[:], y_ab[:, 2, :], pieces[1])
+        scatter_copy(1, weighed_ab1[:], quarters[0])
+        scatter_copy(0, weighed_b0[:], pieces[1])
 
-        z_d1 = [z_product(4 + i, 1, range(PACK), pieces[4 + i]) for i in range(2)]
+        z_d1 = [z_product(6 + i, 1, range(PACK), pieces[4 + i]) for i in range(2)]
         th_pair = [held([P, 2, QUARTER], F32, "th_c1_%d" % i, tag="th_pair%d" % i) for i in range(2)]
         for th, z in zip(th_pair, z_c1):
             tanh_planes(th[:], z)
+        evacuate(values_high[:, :, pieces[1]], y_b_high[:])
+        for i in range(2):
+            weigh(nc.gpsimd, values_high[:, i, :], values_high[:, i, :], quarters[0])
+        scatter_copy(2, values_high[:, 0, :], quarters[0])
         z_d0 = [z_product(i, 0, ts, quarters[2]) for i, ts in enumerate((low, high))]
-        y_c = [open_y(6, low, quarters[1]), open_y(7, high, quarters[1])]
+        y_c = [open_y(2, low, quarters[1]), open_y(4, high, quarters[1])]
         planes_c1 = held([P, PACK, QUARTER], BF16, "planes_c1")
         gain_planes(planes_c1, th_pair[0], th_pair[1], 1)
         woven_c1 = held([P, QUARTER, PACK], BF16, "woven_c1")
         weave(woven_c1[:], planes_c1[:])
-        quantise_h(0, quarters[1], hb_c0)
-        quantise_h(1, quarters[1], woven_c1[:])
-        for b in range(PASSES):
-            for y, ns in zip(y_c, (low, high)):
-                w4_passes(y, b, ns, quarters[1], closes=b == 1)
-
-        after_weave = held([P, PASS + S], F32, "after_weave", tag="planes_c1")
-        raw_b = after_weave[:, :PASS].rearrange("p (n j) -> p n j", n=N_TILES)
-        th_d1 = after_weave[:, PASS:].rearrange("p (j t) -> p j t", t=PACK)
-        after_c = held([P, 2 * QUARTER + PASS], F32, "after_c", tag="woven_c1")
-        weighed_b = after_c[:, :QUARTER].rearrange("p (n j) -> p n j", n=2)
-        weighed_b_high = after_c[:, QUARTER : 2 * QUARTER].rearrange("p (n j) -> p n j", n=2)
-        hb_d1 = after_c[:, 2 * QUARTER :].bitcast(BF16).rearrange("p (j t) -> p j t", t=PACK)
-        evacuate(raw_b[:, 2:4, :], y_b[1][:])
-        weigh(nc.vector, weighed_b, y_b[0][:], pieces[1])
-        weigh(nc.gpsimd, weighed_b_high, raw_b[:, 2:4, :], pieces[1])
-        for n in low:
-            scatter_copy(n, weighed_b[:, n, :], pieces[1])
-        for n in high:
-            scatter_copy(n, weighed_b_high[:, n - 2, :], pieces[1])
-        for i in range(2):
-            tanh_woven(th_d1[:, pieces[i], :], z_d1[i])
-        for i in range(2):
-            gain_woven(nc.gpsimd, hb_d1[:, pieces[i], :], th_d1[:, pieces[i], :], 1)
-        z_e0 = [z_product(2 + i, 0, ts, quarters[3]) for i, ts in enumerate((low, high))]
-        z_e1 = [z_product(4 + i, 1, ts, quarters[3]) for i, ts in enumerate((low, high))]
+        th_d1 = [held([P, PIECE, PACK], F32, "th_d1_%d" % i) for i in range(2)]
+        tanh_woven(th_d1[0][:], z_d1[0])
         th_pair = [held([P, 2, QUARTER], F32, "th_d0_%d" % i, tag="th_pair%d" % i) for i in range(2)]
         for th, z in zip(th_pair, z_d0):
             tanh_planes(th[:], z)
+        tanh_woven(th_d1[1][:], z_d1[1])
         y_d = [open_y(0, low, quarters[2]), open_y(1, high, quarters[2])]
+        z_e0 = [z_product(6 + i, 0, ts, quarters[3]) for i, ts in enumerate((low, high))]
+        hb_d1 = [held([P, PIECE, PACK], BF16, "hb_d1_0")]
+        gain_woven(nc.gpsimd, hb_d1[0][:], th_d1[0][:], 1)
+        scales_c = held([P, PASSES, QUARTER], U8, "scales_c", tag="th_d1_0")
+        quantise_h(0, quarters[1], hb_c0[:], scales_c[:, 0, :])
+        quantise_h(1, quarters[1], woven_c1[:], scales_c[:, 1, :])
+        for y, ns in zip(y_c, (low, high)):
+            for b in range(PASSES):
+                w4_passes(y, b, ns, quarters[1], closes=b == 1)
+
+        pages.append(held([P, S], F32, "page3", tag="woven_c1"))
+        hb_d1.append(held([P, PIECE, PACK], BF16, "hb_d1_1", tag="hb_a1"))
+        gain_woven(nc.gpsimd, hb_d1[1][:], th_d1[1][:], 1)
+        scatter_copy(3, values_high[:, 1, :], quarters[0])
 
         def place(n, y_rows, cols, tag=None):
             values = held([P, width(cols)], F32, "values%d_%d" % (n, cols.start), tag=tag)
             evacuate(values[:], y_rows)
             scatter_weighing(n, values[:], cols)
 
-        place(0, y_c[0][:, 0, :], quarters[1])
         planes_d0 = held([P, PACK, QUARTER], BF16, "planes_d0")
         gain_planes(planes_d0, th_pair[0], th_pair[1], 0)
         woven_d0 = held([P, QUARTER, PACK], BF16, "woven_d0")
         weave(woven_d0[:], planes_d0[:])
-        quantise_h(1, quarters[2], hb_d1)
         quantise_h(0, quarters[2], woven_d0[:])
-        for b in (1, 0):
-            for y, ns in zip(y_d, (low, high)):
-                w4_passes(y, b, ns, quarters[2], closes=b == 0)
-        after_d = held([P, 2, QUARTER], F32, "after_d", tag="planes_d0")
-        evacuate(after_d[:, 0, :], y_c[0][:, 1, :])
-        evacuate(after_d[:, 1, :], y_c[1][:, 0, :])
-        scatter_weighing(1, after_d[:, 0, :], quarters[1])
-        scatter_weighing(2, after_d[:, 1, :], quarters[1])
+        scales_d1 = held([P, QUARTER], U8, "scales_d1")
+        for i in range(2):
+            quantise_h(1, pieces[4 + i], hb_d1[i][:], scales_d1[:, pieces[i]])
+        hs[(1, quarters[2].start)] = scales_d1[:]
+        for y, ns in zip(y_d, (low, high)):
+            for b in range(PASSES):
+                w4_passes(y, b, ns, quarters[2], closes=b == 1)
+        values_c = held([P, 3, QUARTER], F32, "values_c", tag="th_d1_1")
+        for n in range(3):
+            evacuate(values_c[:, n, :], y_c[n // 2][:, n % 2, :])
+            scatter_weighing(n, values_c[:, n, :], quarters[1])
 
         th_pair = [held([P, 2, QUARTER], F32, "th_e0_%d" % i, tag="th_pair%d" % i) for i in range(2)]
         for th, z in zip(th_pair, z_e0):
             tanh_planes(th[:], z)
-        place(0, y_d[0][:, 0, :], quarters[2])
+        z_e1 = [z_product(6 + i, 1, ts, quarters[3]) for i, ts in enumerate((low, high))]
         planes_e0 = held([P, PACK, QUARTER], BF16, "planes_e0")
         gain_planes(planes_e0, th_pair[0], th_pair[1], 0)
+        place(0, y_d[0][:, 0, :], quarters[2])
         woven_e0 = held([P, QUARTER, PACK], BF16, "woven_e0")
         weave(woven_e0[:], planes_e0[:])
         quantise_h(0, quarters[3], woven_e0[:])
@@ -350,7 +376,7 @@ def tile_list_tape_restore_residuals_kernel(
         for th, z in zip(th_pair, z_e1):
             tanh_planes(th[:], z)
         rows_e = (range(0, 1), range(1, 3), range(3, 4))
-        y_e = [open_y(number, ns, quarters[3]) for number, ns in zip((2, 3, 4), rows_e)]
+        y_e = [open_y(number, ns, quarters[3]) for number, ns in zip((2, 6, 7), rows_e)]
         for y, ns in zip(y_e, rows_e):
             w4_passes(y, 0, ns, quarters[3])
         planes_e1 = held([P, PACK, QUARTER], BF16, "planes_e1")

@@ -43,12 +43,12 @@ def tile_list_tape_restore_residuals_kernel(
         picks = keep.tile([P, S // 16], U16, name="picks")
         places = keep.tile([P, S // 16], U16, name="places")
         tab = [held([P, T], I32, "tab%d" % a) for a in range(PASSES)]
-        tab_sc = [held([P, T], U8, "tab_sc%d" % a) for a in range(PASSES)]
+        tab_sc = held([P, PASSES, T], U8, "tab_sc")
         v_sc = held([P, PASSES, S], U8, "v_sc")
         w3_sc = held([P, PASSES, N], U8, "w3_sc")
         w4_sc = held([P, PASSES, N], U8, "w4_sc")
-        nc.vector.memset(tab_sc[0][:].bitcast(I32), 0)
-        nc.gpsimd.memset(tab_sc[1][:].bitcast(I32), 0)
+        nc.vector.memset(tab_sc[:, 0, :].bitcast(I32), 0)
+        nc.gpsimd.memset(tab_sc[:, 1, :].bitcast(I32), 0)
         nc.vector.memset(v_sc[:].bitcast(I32), 0)
         nc.vector.memset(w4_sc[:].bitcast(I32), 0)
         nc.vector.memset(w3_sc[:].bitcast(I32), 0)
@@ -77,12 +77,11 @@ def tile_list_tape_restore_residuals_kernel(
 
         load_w1(1, 0, PASS)
         nc.sync.dma_start(picks[:], offs)
-        for a in range(PASSES):
-            nc.sync.dma_start(out=tab_sc[a][4:P:8, :].bitcast(I32), in_=tab_scales[a].bitcast(I32))
+        nc.sync.dma_start(out=tab_sc[4:P:8, :, :].bitcast(I32), in_=tab_scales.rearrange("a q t -> q a t").bitcast(I32))
         load_w1(0, 0, H)
         load_tab(0)
         for a in range(PASSES):
-            nc.vector.tensor_copy(picked_sc[:, a, :], tab_sc[a][:].indirect(picks[:]))
+            nc.vector.tensor_copy(picked_sc[:, a, :], tab_sc[:, a, :].indirect(picks[:]))
         for r in range(4):
             nc.sync.dma_start(
                 out=v_sc[V_ROW + r : P : 32, :, :].bitcast(I32), in_=picked_sc[4 + 8 * r : P : 32, :, :].bitcast(I32)
@@ -112,17 +111,17 @@ def tile_list_tape_restore_residuals_kernel(
                     in_=rows.rearrange("p j (m t) -> p m j t", t=PACK),
                 )
                 m0 = m1
-            tw = PACK // calls
-            for u in range(calls):
+            flat = grouped[:].rearrange("p t m j -> p (t m j)")
+            for c0, c1 in calls:
                 nc.vector.quantize_mx(
-                    out=w1c[(a, b)][:, u * tw * P : (u + 1) * tw * P].bitcast(FP8X4),
-                    scales=w1s[(a, b)][:, u * tw * P : (u + 1) * tw * P],
-                    in_=grouped[:, u * tw : (u + 1) * tw, :, :].rearrange("p t m j -> p (t m j)"),
+                    out=w1c[(a, b)][:, c0:c1].bitcast(FP8X4),
+                    scales=w1s[(a, b)][:, c0:c1],
+                    in_=flat[:, PACK * c0 : PACK * c1],
                 )
 
-        quantise_w1(1, 0, 1, [(nc.scalar.copy, raw[(1, 0)][:])])
-        quantise_w1(0, 0, 1, [(nc.scalar.copy, raw[(0, 0)][:, :, :PASS])])
-        quantise_w1(0, 1, 1, [(nc.scalar.copy, raw[(0, 0)][:, :, PASS:])])
+        quantise_w1(1, 0, [(0, PASS)], [(nc.scalar.copy, raw[(1, 0)][:])])
+        quantise_w1(0, 0, [(0, PASS)], [(nc.scalar.copy, raw[(0, 0)][:, :, :PASS])])
+        quantise_w1(0, 1, [(0, PASS)], [(nc.scalar.copy, raw[(0, 0)][:, :, PASS:])])
 
         v = [held([P, S], U32, "v%d" % a) for a in range(PASSES)]
 
@@ -135,7 +134,10 @@ def tile_list_tape_restore_residuals_kernel(
         gather(1, QUARTER, 2 * QUARTER)
         gather(1, 2 * QUARTER, S)
         quantise_w1(
-            1, 1, PACK, [(nc.scalar.copy, raw[(1, PASS)][:]), (nc.vector.tensor_copy, raw[(1, PASS + QUARTER)][:])]
+            1,
+            1,
+            [(P * t + m0, P * t + m0 + P // 2) for m0 in (0, P // 2) for t in range(PACK)],
+            [(nc.scalar.copy, raw[(1, PASS)][:]), (nc.vector.tensor_copy, raw[(1, PASS + QUARTER)][:])],
         )
 
         feats = held([P, N_TILES, S], F32, "feats", tag="tab0")
@@ -285,7 +287,7 @@ def tile_list_tape_restore_residuals_kernel(
         z_c1 = [z_product(i, 1, ts, quarters[1]) for i, ts in enumerate((low, high))]
         values_high = held([P, 2, QUARTER], F32, "values_high")
         evacuate(values_high[:, :, pieces[0]], y_a_high[:])
-        hb_b1 = held([P, PIECE, PACK], BF16, "hb_b1", tag="hb_a1")
+        hb_b1 = held([P, PIECE, PACK], BF16, "hb_b1", tag="grouped11")
         gain_woven(nc.vector, hb_b1[:], th_first[(1, 1)][:], 1)
         weighed_a0 = held([P, PIECE], F32, "weighed_a0")
         weigh(nc.vector, weighed_a0[:], y_a0[:, 0, :], pieces[0])
@@ -293,7 +295,7 @@ def tile_list_tape_restore_residuals_kernel(
         w4_passes(y_ab[:, 1:3, :], 1, (1, 0), pieces[1], closes=True)
         y_b_high = whole_y(4, high, pieces[1])
 
-        hb_c0 = held([P, QUARTER, PACK], BF16, "hb_c0", tag="hb_a1")
+        hb_c0 = held([P, QUARTER, PACK], BF16, "hb_c0", tag="grouped11")
         gain_woven(nc.gpsimd, hb_c0[:], th_c0, 0)
         scatter_copy(0, weighed_a0[:], pieces[0])
         weighed_ab1 = held([P, QUARTER], F32, "weighed_ab1")
@@ -335,7 +337,7 @@ def tile_list_tape_restore_residuals_kernel(
                 w4_passes(y, b, ns, quarters[1], closes=b == 1)
 
         pages.append(held([P, S], F32, "page3", tag="woven_c1"))
-        hb_d1.append(held([P, PIECE, PACK], BF16, "hb_d1_1", tag="hb_a1"))
+        hb_d1.append(held([P, PIECE, PACK], BF16, "hb_d1_1", tag="grouped11"))
         gain_woven(nc.gpsimd, hb_d1[1][:], th_d1[1][:], 1)
         scatter_copy(3, values_high[:, 1, :], quarters[0])
 
@@ -371,7 +373,8 @@ def tile_list_tape_restore_residuals_kernel(
         woven_e0 = held([P, QUARTER, PACK], BF16, "woven_e0")
         weave(woven_e0[:], planes_e0[:])
         quantise_h(0, quarters[3], woven_e0[:])
-        place(1, y_d[0][:, 1, :], quarters[2], tag="planes_e0")
+        place(2, y_d[1][:, 0, :], quarters[2], tag="planes_e0")
+
         th_pair = [held([P, 2, QUARTER], F32, "th_e1_%d" % i, tag="th_pair%d" % i) for i in range(2)]
         for th, z in zip(th_pair, z_e1):
             tanh_planes(th[:], z)
@@ -387,28 +390,26 @@ def tile_list_tape_restore_residuals_kernel(
         for y, ns in zip(y_e, rows_e):
             w4_passes(y, 1, ns, quarters[3], closes=True)
 
-        late = held([P, 3, QUARTER], F32, "late", tag="planes_e1")
-        evacuate(late[:, 0, :], y_d[1][:, 0, :])
-        evacuate(late[:, 1, :], y_c[1][:, 1, :])
-        evacuate(late[:, 2, :], y_d[1][:, 1, :])
-        bridge = held([P, QUARTER], F32, "bridge")
-        weigh(nc.vector, bridge[:], late[:, 0, :], quarters[2])
-        scatter_copy(2, bridge[:], quarters[2])
-        last = held([P, 3 * QUARTER], F32, "last", tag="woven_e1")
-        values_e = held([P, N_TILES, QUARTER], F32, "values_e")
+        last = held([P, S], F32, "last", tag="woven_e1")
+        values_3 = held([P, 4, QUARTER], F32, "values_3", tag="planes_e1")
+        weigh(nc.vector, values_3[:, 3, :], y_d[0][:, 1, :], quarters[2])
+        scatter_copy(1, values_3[:, 3, :], quarters[2])
+        values_e = held([P, 3, QUARTER], F32, "values_e")
+        evacuate(values_3[:, 0, :], y_c[1][:, 1, :])
+        weigh(nc.gpsimd, last[:, quarters[1]], values_3[:, 0, :], quarters[1])
+        evacuate(values_3[:, 1, :], y_d[1][:, 1, :])
         evacuate(values_e[:, 0, :], y_e[0][:, 0, :])
         evacuate(values_e[:, 1:3, :], y_e[1][:])
-        evacuate(values_e[:, 3, :], y_e[2][:, 0, :])
-        for n in range(3):
-            weigh(nc.gpsimd, values_e[:, n, :], values_e[:, n, :], quarters[3])
-        weigh(nc.gpsimd, last[:, : 2 * QUARTER], late[:, 1:3, :].rearrange("p g j -> p (g j)"), slice(QUARTER, 3 * QUARTER))
-        weigh(nc.gpsimd, last[:, 2 * QUARTER :], values_e[:, 3, :], quarters[3])
+        evacuate(values_3[:, 2, :], y_e[2][:, 0, :])
+        weigh(nc.gpsimd, values_e[:, 0, :], values_e[:, 0, :], quarters[3])
+        weigh(nc.gpsimd, values_e[:, 1:3, :], values_e[:, 1:3, :], quarters[3])
+        weigh(nc.gpsimd, last[:, 2 * QUARTER :], values_3[:, 1:3, :].rearrange("p g j -> p (g j)"), slice(2 * QUARTER, S))
         sizes = held([P, N_TILES, S], F32, "sizes", tag="planes_e1")
         for n in high:
             nc.scalar.activation(out=sizes[:, n, :], in_=feats[:, n, :], func=ACT.Abs)
         for n in range(3):
             scatter_copy(n, values_e[:, n, :], quarters[3])
-        scatter_copy(3, last[:, : 3 * QUARTER], slice(QUARTER, S))
+        scatter_copy(3, last[:, QUARTER:], slice(QUARTER, S))
 
         def weigh_and_store(n, c0, c1, engine, product):
             engine.tensor_tensor(product, pages[n][:, c0:c1], sizes[:, n, c0:c1], MULT)
@@ -417,7 +418,8 @@ def tile_list_tape_restore_residuals_kernel(
         for n in low:
             nc.gpsimd.tensor_tensor(feats[:, n, :], pages[n][:], feats[:, n, :], MULT)
             nc.scalar.activation(out=sizes[:, n, :], in_=feats[:, n, :], func=ACT.Abs)
-            nc.sync.dma_start(out=out[P * n : P * (n + 1), :], in_=sizes[:, n, :])
-        weigh_and_store(2, 0, S, nc.gpsimd, feats[:, 2, :])
+            nc.scalar.dma_start(out=out[P * n : P * (n + 1), :], in_=sizes[:, n, :])
+        for c0 in (0, S // 2):
+            weigh_and_store(2, c0, c0 + S // 2, nc.gpsimd, feats[:, 2, c0 : c0 + S // 2])
         for c0 in range(0, S, QUARTER):
             weigh_and_store(3, c0, c0 + QUARTER, nc.vector, sizes[:, 2, c0 : c0 + QUARTER])

@@ -341,11 +341,6 @@ def tile_list_tape_restore_residuals_kernel(
         gain_woven(nc.gpsimd, hb_d1[1][:], th_d1[1][:], 1)
         scatter_copy(3, values_high[:, 1, :], quarters[0])
 
-        def place(n, y_rows, cols, tag=None):
-            values = held([P, width(cols)], F32, "values%d_%d" % (n, cols.start), tag=tag)
-            evacuate(values[:], y_rows)
-            scatter_weighing(n, values[:], cols)
-
         planes_d0 = held([P, PACK, QUARTER], BF16, "planes_d0")
         gain_planes(planes_d0, th_pair[0], th_pair[1], 0)
         woven_d0 = held([P, QUARTER, PACK], BF16, "woven_d0")
@@ -358,52 +353,71 @@ def tile_list_tape_restore_residuals_kernel(
         for y, ns in zip(y_d, (low, high)):
             for b in range(PASSES):
                 w4_passes(y, b, ns, quarters[2], closes=b == 1)
-        values_c = held([P, 3, QUARTER], F32, "values_c", tag="th_d1_1")
-        for n in range(3):
-            evacuate(values_c[:, n, :], y_c[n // 2][:, n % 2, :])
-            scatter_weighing(n, values_c[:, n, :], quarters[1])
+        values_c = held([P, 2, QUARTER], F32, "values_c", tag="th_d1_1")
+        for i in range(2):
+            evacuate(values_c[:, i, :], y_c[i][:, 0, :])
+            scatter_weighing(2 * i, values_c[:, i, :], quarters[1])
 
         th_pair = [held([P, 2, QUARTER], F32, "th_e0_%d" % i, tag="th_pair%d" % i) for i in range(2)]
         for th, z in zip(th_pair, z_e0):
             tanh_planes(th[:], z)
-        z_e1 = [z_product(6 + i, 1, ts, quarters[3]) for i, ts in enumerate((low, high))]
+        z_e1 = [z_product(6 + i, 1, range(PACK), pieces[6 + i]) for i in range(2)]
         planes_e0 = held([P, PACK, QUARTER], BF16, "planes_e0")
         gain_planes(planes_e0, th_pair[0], th_pair[1], 0)
-        place(0, y_d[0][:, 0, :], quarters[2])
         woven_e0 = held([P, QUARTER, PACK], BF16, "woven_e0")
         weave(woven_e0[:], planes_e0[:])
+        after_weave = held([P, 5, QUARTER], F32, "after_weave", tag="planes_e0")
+        weigh(nc.vector, after_weave[:, 2, :], y_c[0][:, 1, :], quarters[1])
         quantise_h(0, quarters[3], woven_e0[:])
-        place(2, y_d[1][:, 0, :], quarters[2], tag="planes_e0")
+        scatter_copy(1, after_weave[:, 2, :], quarters[1])
 
-        th_pair = [held([P, 2, QUARTER], F32, "th_e1_%d" % i, tag="th_pair%d" % i) for i in range(2)]
-        for th, z in zip(th_pair, z_e1):
-            tanh_planes(th[:], z)
+        evacuate(after_weave[:, 0:2, :], y_d[0][:])
+        after_e0 = held([P, 3 * QUARTER], F32, "after_e0", tag="woven_e0")
+        woven_e1 = after_e0[:, QUARTER:].bitcast(BF16).rearrange("p (j t) -> p j t", t=PACK)
+        weigh(nc.gpsimd, after_e0[:, :QUARTER], after_weave[:, 0, :], quarters[2])
+        scatter_copy(0, after_e0[:, :QUARTER], quarters[2])
+        th_e1 = after_weave[:, 3:5, :].rearrange("p i (j t) -> p (i j) t", t=PACK)
+        th_e1_rest = held([P, PACK, PIECE], F32, "th_e1_rest", tag="th_pair1")
+        tanh_woven(th_e1, z_e1[0])
+        tanh_planes(th_e1_rest[:], z_e1[1])
+        gain_woven(nc.gpsimd, woven_e1[:, :PIECE, :], th_e1, 1)
         rows_e = (range(0, 1), range(1, 3), range(3, 4))
         y_e = [open_y(number, ns, quarters[3]) for number, ns in zip((2, 6, 7), rows_e)]
         for y, ns in zip(y_e, rows_e):
             w4_passes(y, 0, ns, quarters[3])
-        planes_e1 = held([P, PACK, QUARTER], BF16, "planes_e1")
-        gain_planes(planes_e1, th_pair[0], th_pair[1], 1)
-        woven_e1 = held([P, QUARTER, PACK], BF16, "woven_e1")
-        weave(woven_e1[:], planes_e1[:])
-        quantise_h(1, quarters[3], woven_e1[:])
+        planes_e1 = held([P, PACK, PIECE], BF16, "planes_e1")
+        gain_planes(planes_e1, th_e1_rest[:, 0:2, :], th_e1_rest[:, 2:4, :], 1)
+        woven_rest = held([P, PIECE, PACK], BF16, "woven_rest")
+        weave(woven_rest[:], planes_e1[:])
+        values_late = held([P, 5, QUARTER], F32, "values_late", tag="planes_e1")
+        weigh(nc.gpsimd, values_late[:, 4, :], after_weave[:, 1, :], quarters[2])
+        scales_e1 = held([P, QUARTER], U8, "scales_e1")
+        quantise_h(1, pieces[7], woven_rest[:], scales_e1[:, pieces[1]])
+        quantise_h(1, pieces[6], woven_e1[:, :PIECE, :], scales_e1[:, pieces[0]])
+        hs[(1, quarters[3].start)] = scales_e1[:]
         for y, ns in zip(y_e, rows_e):
             w4_passes(y, 1, ns, quarters[3], closes=True)
 
-        last = held([P, S], F32, "last", tag="woven_e1")
-        values_3 = held([P, 4, QUARTER], F32, "values_3", tag="planes_e1")
-        weigh(nc.vector, values_3[:, 3, :], y_d[0][:, 1, :], quarters[2])
-        scatter_copy(1, values_3[:, 3, :], quarters[2])
+        last = held([P, S], F32, "last", tag="woven_e0")
+        scatter_copy(1, values_late[:, 4, :], quarters[2])
+        evacuate(values_late[:, 3, :], y_d[1][:, 0, :])
+        weigh(nc.gpsimd, last[:, quarters[0]], values_late[:, 3, :], quarters[2])
+        scatter_copy(2, last[:, quarters[0]], quarters[2])
         values_e = held([P, 3, QUARTER], F32, "values_e")
-        evacuate(values_3[:, 0, :], y_c[1][:, 1, :])
-        weigh(nc.gpsimd, last[:, quarters[1]], values_3[:, 0, :], quarters[1])
-        evacuate(values_3[:, 1, :], y_d[1][:, 1, :])
+        evacuate(values_late[:, 0, :], y_c[1][:, 1, :])
+        evacuate(values_late[:, 1, :], y_d[1][:, 1, :])
         evacuate(values_e[:, 0, :], y_e[0][:, 0, :])
         evacuate(values_e[:, 1:3, :], y_e[1][:])
-        evacuate(values_3[:, 2, :], y_e[2][:, 0, :])
+        evacuate(values_late[:, 2, :], y_e[2][:, 0, :])
+        weigh(
+            nc.gpsimd,
+            last[:, QUARTER : 3 * QUARTER],
+            values_late[:, 0:2, :].rearrange("p g j -> p (g j)"),
+            slice(QUARTER, 3 * QUARTER),
+        )
         weigh(nc.gpsimd, values_e[:, 0, :], values_e[:, 0, :], quarters[3])
         weigh(nc.gpsimd, values_e[:, 1:3, :], values_e[:, 1:3, :], quarters[3])
-        weigh(nc.gpsimd, last[:, 2 * QUARTER :], values_3[:, 1:3, :].rearrange("p g j -> p (g j)"), slice(2 * QUARTER, S))
+        weigh(nc.gpsimd, last[:, quarters[3]], values_late[:, 2, :], quarters[3])
         sizes = held([P, N_TILES, S], F32, "sizes", tag="planes_e1")
         for n in high:
             nc.scalar.activation(out=sizes[:, n, :], in_=feats[:, n, :], func=ACT.Abs)
@@ -416,9 +430,9 @@ def tile_list_tape_restore_residuals_kernel(
             nc.sync.dma_start(out=out[P * n : P * (n + 1), c0:c1], in_=product)
 
         for n in low:
-            nc.gpsimd.tensor_tensor(feats[:, n, :], pages[n][:], feats[:, n, :], MULT)
-            nc.scalar.activation(out=sizes[:, n, :], in_=feats[:, n, :], func=ACT.Abs)
-            nc.scalar.dma_start(out=out[P * n : P * (n + 1), :], in_=sizes[:, n, :])
+            nc.gpsimd.tensor_tensor(sizes[:, n, :], pages[n][:], feats[:, n, :], MULT)
+            nc.scalar.activation(out=feats[:, n, :], in_=sizes[:, n, :], func=ACT.Abs)
+            nc.scalar.dma_start(out=out[P * n : P * (n + 1), :], in_=feats[:, n, :])
         for c0 in (0, S // 2):
             weigh_and_store(2, c0, c0 + S // 2, nc.gpsimd, feats[:, 2, c0 : c0 + S // 2])
         for c0 in range(0, S, QUARTER):

@@ -92,8 +92,8 @@ def tile_list_tape_restore_residuals_kernel(
         load_scales(w4_sc, w4_scales)
         load_scales(w3_sc, w3_scales)
         nc.sync.dma_start(out=gains[:], in_=gain.rearrange("(b p t) -> p b t", b=PASSES, t=PACK))
-        nc.sync.dma_start(out=w4[:].bitcast(I32), in_=w4_words.rearrange("a p c -> p a c").bitcast(I32))
         nc.sync.dma_start(out=w3[:].bitcast(I32), in_=w3_words.rearrange("a p c i -> p a (c i)").bitcast(I32))
+        nc.sync.dma_start(out=w4[:].bitcast(I32), in_=w4_words.rearrange("a p c -> p a c").bitcast(I32))
         nc.sync.dma_start(places[:], offs2)
         nc.sync.dma_start(out=weight[:], in_=wgo)
 
@@ -265,7 +265,7 @@ def tile_list_tape_restore_residuals_kernel(
             tanh_woven(th_first[(0, 1)][:, half, :], z_a1[:, :, half])
         tanh_woven(th_first[(1, 1)][:], z_product(5, 1, range(PACK), pieces[1]))
         y_a0 = open_y(6, range(0, 1), pieces[0])
-        y_ab = bank(2, [P, 3, PIECE], "y")
+        y_ab = bank(2, [P, 2, PIECE], "y")
         w3_passes(y_ab[:, 0:1, :], range(1, 2), pieces[0], opens=True)
         y_a_high = open_y(7, high, pieces[0])
         hb_0 = held([P, 2, PIECE, PACK], BF16, "hb_0", tag="grouped11")
@@ -278,30 +278,35 @@ def tile_list_tape_restore_residuals_kernel(
             w4_passes(y, 0, ns, pieces[0])
         for half in halves:
             gain_woven(nc.vector, hb_a1[:, half, :], th_first[(0, 1)][:, half, :], 1)
-        quantise_h(0, pieces[1], hb_0[:, 1, :, :])
         quantise_h(1, pieces[0], hb_a1[:])
+        scales_b0 = held([P, PIECE], U8, "scales_b0", tag="th_first0")
+        quantise_h(0, pieces[1], hb_0[:, 1, :, :], scales_b0[:])
         for y, ns in rows_a:
             w4_passes(y, 1, ns, pieces[0], closes=ns.start != 1)
-        w3_passes(y_ab[:, 1:3, :], (1, 0), pieces[1])
-        w4_passes(y_ab[:, 1:3, :], 0, (1, 0), pieces[1])
+        y_b0 = open_y(3, range(0, 1), pieces[1])
+        rows_b = ((y_ab[:, 1:2, :], range(1, 2)), (y_b0, range(0, 1)))
+        w3_passes(y_ab[:, 1:2, :], range(1, 2), pieces[1])
+        for y, ns in rows_b:
+            w4_passes(y, 0, ns, pieces[1])
         z_c1 = [z_product(i, 1, ts, quarters[1]) for i, ts in enumerate((low, high))]
         values_high = held([P, 2, QUARTER], F32, "values_high")
         evacuate(values_high[:, :, pieces[0]], y_a_high[:])
-        hb_b1 = held([P, PIECE, PACK], BF16, "hb_b1", tag="grouped11")
+        hb_b1 = held([P, PIECE, PACK], BF16, "hb_b1", tag="hb_a1")
         gain_woven(nc.vector, hb_b1[:], th_first[(1, 1)][:], 1)
         weighed_a0 = held([P, PIECE], F32, "weighed_a0")
         weigh(nc.vector, weighed_a0[:], y_a0[:, 0, :], pieces[0])
         quantise_h(1, pieces[1], hb_b1[:])
-        w4_passes(y_ab[:, 1:3, :], 1, (1, 0), pieces[1], closes=True)
+        for y, ns in rows_b:
+            w4_passes(y, 1, ns, pieces[1], closes=True)
         y_b_high = whole_y(4, high, pieces[1])
 
-        hb_c0 = held([P, QUARTER, PACK], BF16, "hb_c0", tag="grouped11")
+        hb_c0 = held([P, QUARTER, PACK], BF16, "hb_c0", tag="hb_a1")
         gain_woven(nc.gpsimd, hb_c0[:], th_c0, 0)
         scatter_copy(0, weighed_a0[:], pieces[0])
         weighed_ab1 = held([P, QUARTER], F32, "weighed_ab1")
         weighed_b0 = held([P, PIECE], F32, "weighed_b0")
-        weigh(nc.vector, weighed_ab1[:], y_ab[:, 0:2, :].rearrange("p i j -> p (i j)"), quarters[0])
-        weigh(nc.vector, weighed_b0[:], y_ab[:, 2, :], pieces[1])
+        weigh(nc.vector, weighed_ab1[:], y_ab[:].rearrange("p i j -> p (i j)"), quarters[0])
+        weigh(nc.vector, weighed_b0[:], y_b0[:, 0, :], pieces[1])
         scatter_copy(1, weighed_ab1[:], quarters[0])
         scatter_copy(0, weighed_b0[:], pieces[1])
 
@@ -310,11 +315,11 @@ def tile_list_tape_restore_residuals_kernel(
         for th, z in zip(th_pair, z_c1):
             tanh_planes(th[:], z)
         evacuate(values_high[:, :, pieces[1]], y_b_high[:])
-        for i in range(2):
-            weigh(nc.gpsimd, values_high[:, i, :], values_high[:, i, :], quarters[0])
+        weigh(nc.gpsimd, values_high[:], values_high[:], quarters[0])
         scatter_copy(2, values_high[:, 0, :], quarters[0])
         z_d0 = [z_product(i, 0, ts, quarters[2]) for i, ts in enumerate((low, high))]
-        y_c = [open_y(2, low, quarters[1]), open_y(4, high, quarters[1])]
+        rows_c = (range(0, 1), range(1, 2), high)
+        y_c = [open_y(number, ns, quarters[1]) for number, ns in zip((5, 2, 4), rows_c)]
         planes_c1 = held([P, PACK, QUARTER], BF16, "planes_c1")
         gain_planes(planes_c1, th_pair[0], th_pair[1], 1)
         woven_c1 = held([P, QUARTER, PACK], BF16, "woven_c1")
@@ -332,15 +337,18 @@ def tile_list_tape_restore_residuals_kernel(
         scales_c = held([P, PASSES, QUARTER], U8, "scales_c", tag="th_d1_0")
         quantise_h(0, quarters[1], hb_c0[:], scales_c[:, 0, :])
         quantise_h(1, quarters[1], woven_c1[:], scales_c[:, 1, :])
-        for y, ns in zip(y_c, (low, high)):
-            for b in range(PASSES):
-                w4_passes(y, b, ns, quarters[1], closes=b == 1)
+        for y, ns, order in zip(y_c, rows_c, ((0, 1), (1, 0), (1, 0))):
+            for b in order:
+                w4_passes(y, b, ns, quarters[1], closes=b == order[1])
 
         pages.append(held([P, S], F32, "page3", tag="woven_c1"))
-        hb_d1.append(held([P, PIECE, PACK], BF16, "hb_d1_1", tag="grouped11"))
+        hb_d1.append(held([P, PIECE, PACK], BF16, "hb_d1_1", tag="hb_a1"))
         gain_woven(nc.gpsimd, hb_d1[1][:], th_d1[1][:], 1)
         scatter_copy(3, values_high[:, 1, :], quarters[0])
 
+        values_c0 = held([P, QUARTER], F32, "values_c0")
+        evacuate(values_c0[:], y_c[0][:, 0, :])
+        scatter_weighing(0, values_c0[:], quarters[1])
         planes_d0 = held([P, PACK, QUARTER], BF16, "planes_d0")
         gain_planes(planes_d0, th_pair[0], th_pair[1], 0)
         woven_d0 = held([P, QUARTER, PACK], BF16, "woven_d0")
@@ -353,10 +361,9 @@ def tile_list_tape_restore_residuals_kernel(
         for y, ns in zip(y_d, (low, high)):
             for b in range(PASSES):
                 w4_passes(y, b, ns, quarters[2], closes=b == 1)
-        values_c = held([P, 2, QUARTER], F32, "values_c", tag="th_d1_1")
-        for i in range(2):
-            evacuate(values_c[:, i, :], y_c[i][:, 0, :])
-            scatter_weighing(2 * i, values_c[:, i, :], quarters[1])
+        values_c2 = held([P, QUARTER], F32, "values_c2", tag="planes_d0")
+        evacuate(values_c2[:], y_c[2][:, 0, :])
+        scatter_weighing(2, values_c2[:], quarters[1])
 
         th_pair = [held([P, 2, QUARTER], F32, "th_e0_%d" % i, tag="th_pair%d" % i) for i in range(2)]
         for th, z in zip(th_pair, z_e0):
@@ -367,7 +374,7 @@ def tile_list_tape_restore_residuals_kernel(
         woven_e0 = held([P, QUARTER, PACK], BF16, "woven_e0")
         weave(woven_e0[:], planes_e0[:])
         after_weave = held([P, 5, QUARTER], F32, "after_weave", tag="planes_e0")
-        weigh(nc.vector, after_weave[:, 2, :], y_c[0][:, 1, :], quarters[1])
+        weigh(nc.vector, after_weave[:, 2, :], y_c[1][:, 0, :], quarters[1])
         quantise_h(0, quarters[3], woven_e0[:])
         scatter_copy(1, after_weave[:, 2, :], quarters[1])
 
@@ -404,7 +411,7 @@ def tile_list_tape_restore_residuals_kernel(
         weigh(nc.gpsimd, last[:, quarters[0]], values_late[:, 3, :], quarters[2])
         scatter_copy(2, last[:, quarters[0]], quarters[2])
         values_e = held([P, 3, QUARTER], F32, "values_e")
-        evacuate(values_late[:, 0, :], y_c[1][:, 1, :])
+        evacuate(values_late[:, 0, :], y_c[2][:, 1, :])
         evacuate(values_late[:, 1, :], y_d[1][:, 1, :])
         evacuate(values_e[:, 0, :], y_e[0][:, 0, :])
         evacuate(values_e[:, 1:3, :], y_e[1][:])

@@ -253,7 +253,6 @@ def tile_list_tape_restore_residuals_kernel(
         th_first = {}
         th_early = held([P, 2 * QUARTER, PACK], F32, "th_early", tag="raw1_%d" % PASS)
         for i in range(2):
-            th_first[(i, 1)] = held([P, PIECE, PACK], F32, "th_first%d" % i)
             th_first[(i, 0)] = th_early[:, pieces[i], :]
             tanh_woven(th_first[(i, 0)], z_product(i, 0, range(PACK), pieces[i]))
         th_c0 = th_early[:, quarters[1], :]
@@ -261,28 +260,32 @@ def tile_list_tape_restore_residuals_kernel(
             tanh_woven(th_c0[:, pieces[i], :], z_product(2 + i, 0, range(PACK), pieces[2 + i]))
         halves = (slice(0, PIECE // 2), slice(PIECE // 2, PIECE))
         z_a1 = z_product(4, 1, range(PACK), pieces[0])
-        for half in halves:
-            tanh_woven(th_first[(0, 1)][:, half, :], z_a1[:, :, half])
+        th_a1 = [held([P, PIECE // 2, PACK], F32, "th_a1_%d" % i) for i in range(2)]
+        for th, half in zip(th_a1, halves):
+            tanh_woven(th[:], z_a1[:, :, half])
+        th_first[(1, 1)] = held([P, PIECE, PACK], F32, "th_first1")
         tanh_woven(th_first[(1, 1)][:], z_product(5, 1, range(PACK), pieces[1]))
         y_a0 = open_y(6, range(0, 1), pieces[0])
         y_ab = bank(2, [P, 2, PIECE], "y")
         w3_passes(y_ab[:, 0:1, :], range(1, 2), pieces[0], opens=True)
         y_a_high = open_y(7, high, pieces[0])
-        hb_0 = held([P, 2, PIECE, PACK], BF16, "hb_0", tag="grouped11")
+        hb_0 = held([P, 2, PIECE, PACK], BF16, "hb_0", tag="raw1_%d" % (PASS + QUARTER))
         hb_a1 = held([P, PIECE, PACK], BF16, "hb_a1")
         for i in range(2):
             gain_woven(nc.vector, hb_0[:, i, :, :], th_first[(i, 0)], 0)
-        quantise_h(0, pieces[0], hb_0[:, 0, :, :])
         rows_a = ((y_a0, range(0, 1)), (y_ab[:, 0:1, :], range(1, 2)), (y_a_high, high))
-        for y, ns in rows_a:
-            w4_passes(y, 0, ns, pieces[0])
-        for half in halves:
-            gain_woven(nc.vector, hb_a1[:, half, :], th_first[(0, 1)][:, half, :], 1)
+        for th, half in zip(th_a1, halves):
+            gain_woven(nc.vector, hb_a1[:, half, :], th[:], 1)
+        scales_a0 = held([P, PIECE], U8, "scales_a0", tag="th_a1_0")
+        quantise_h(0, pieces[0], hb_0[:, 0, :, :], scales_a0[:])
+        w4_passes(y_a0, 0, range(0, 1), pieces[0])
         quantise_h(1, pieces[0], hb_a1[:])
-        scales_b0 = held([P, PIECE], U8, "scales_b0", tag="th_first0")
+        scales_b0 = held([P, PIECE], U8, "scales_b0", tag="th_a1_1")
         quantise_h(0, pieces[1], hb_0[:, 1, :, :], scales_b0[:])
-        for y, ns in rows_a:
-            w4_passes(y, 1, ns, pieces[0], closes=ns.start != 1)
+        w4_passes(y_a0, 1, range(0, 1), pieces[0], closes=True)
+        for y, ns in rows_a[1:]:
+            w4_passes(y, 1, ns, pieces[0])
+            w4_passes(y, 0, ns, pieces[0], closes=ns.start != 1)
         y_b0 = open_y(3, range(0, 1), pieces[1])
         rows_b = ((y_ab[:, 1:2, :], range(1, 2)), (y_b0, range(0, 1)))
         w3_passes(y_ab[:, 1:2, :], range(1, 2), pieces[1])

@@ -265,15 +265,14 @@ def tile_list_tape_restore_residuals_kernel(
             tanh_woven(th[:], z_a1[:, :, half])
         th_first[(1, 1)] = held([P, PIECE, PACK], F32, "th_first1")
         tanh_woven(th_first[(1, 1)][:], z_product(5, 1, range(PACK), pieces[1]))
-        y_a0 = open_y(6, range(0, 1), pieces[0])
-        y_ab = bank(2, [P, 2, PIECE], "y")
+        z_d0 = [z_product(6 + i, 0, ts, quarters[2]) for i, ts in enumerate((low, high))]
+        y_a0 = open_y(4, range(0, 1), pieces[0])
+        y_ab = bank(5, [P, 2, PIECE], "y")
         w3_passes(y_ab[:, 0:1, :], range(1, 2), pieces[0], opens=True)
-        y_a_high = open_y(7, high, pieces[0])
         hb_0 = held([P, 2, PIECE, PACK], BF16, "hb_0", tag="raw1_%d" % (PASS + QUARTER))
         hb_a1 = held([P, PIECE, PACK], BF16, "hb_a1")
         for i in range(2):
             gain_woven(nc.vector, hb_0[:, i, :, :], th_first[(i, 0)], 0)
-        rows_a = ((y_a0, range(0, 1)), (y_ab[:, 0:1, :], range(1, 2)), (y_a_high, high))
         for th, half in zip(th_a1, halves):
             gain_woven(nc.vector, hb_a1[:, half, :], th[:], 1)
         scales_a0 = held([P, PIECE], U8, "scales_a0", tag="th_a1_0")
@@ -283,14 +282,15 @@ def tile_list_tape_restore_residuals_kernel(
         scales_b0 = held([P, PIECE], U8, "scales_b0", tag="th_a1_1")
         quantise_h(0, pieces[1], hb_0[:, 1, :, :], scales_b0[:])
         w4_passes(y_a0, 1, range(0, 1), pieces[0], closes=True)
-        for y, ns in rows_a[1:]:
-            w4_passes(y, 1, ns, pieces[0])
-            w4_passes(y, 0, ns, pieces[0], closes=ns.start != 1)
-        y_b0 = open_y(3, range(0, 1), pieces[1])
+        w4_passes(y_ab[:, 0:1, :], 1, range(1, 2), pieces[0])
+        w4_passes(y_ab[:, 0:1, :], 0, range(1, 2), pieces[0])
+        y_a_high = whole_y(2, high, pieces[0])
+        y_b0 = bank(3, [P, 1, PIECE], "y")
         rows_b = ((y_ab[:, 1:2, :], range(1, 2)), (y_b0, range(0, 1)))
         w3_passes(y_ab[:, 1:2, :], range(1, 2), pieces[1])
-        for y, ns in rows_b:
-            w4_passes(y, 0, ns, pieces[1])
+        w4_passes(y_ab[:, 1:2, :], 0, range(1, 2), pieces[1])
+        w4_passes(y_b0, 0, range(0, 1), pieces[1], opens=True)
+        w3_passes(y_b0, range(0, 1), pieces[1])
         z_c1 = [z_product(i, 1, ts, quarters[1]) for i, ts in enumerate((low, high))]
         values_high = held([P, 2, QUARTER], F32, "values_high")
         evacuate(values_high[:, :, pieces[0]], y_a_high[:])
@@ -313,16 +313,15 @@ def tile_list_tape_restore_residuals_kernel(
         scatter_copy(1, weighed_ab1[:], quarters[0])
         scatter_copy(0, weighed_b0[:], pieces[1])
 
-        z_d1 = [z_product(6 + i, 1, range(PACK), pieces[4 + i]) for i in range(2)]
+        z_d1 = [z_product(2 + i, 1, range(PACK), pieces[4 + i]) for i in range(2)]
         th_pair = [held([P, 2, QUARTER], F32, "th_c1_%d" % i, tag="th_pair%d" % i) for i in range(2)]
         for th, z in zip(th_pair, z_c1):
             tanh_planes(th[:], z)
         evacuate(values_high[:, :, pieces[1]], y_b_high[:])
         weigh(nc.gpsimd, values_high[:], values_high[:], quarters[0])
         scatter_copy(2, values_high[:, 0, :], quarters[0])
-        z_d0 = [z_product(i, 0, ts, quarters[2]) for i, ts in enumerate((low, high))]
         rows_c = (range(0, 1), range(1, 2), high)
-        y_c = [open_y(number, ns, quarters[1]) for number, ns in zip((5, 2, 4), rows_c)]
+        y_c = [open_y(number, ns, quarters[1]) for number, ns in zip((0, 1, 4), rows_c)]
         planes_c1 = held([P, PACK, QUARTER], BF16, "planes_c1")
         gain_planes(planes_c1, th_pair[0], th_pair[1], 1)
         woven_c1 = held([P, QUARTER, PACK], BF16, "woven_c1")
@@ -333,8 +332,8 @@ def tile_list_tape_restore_residuals_kernel(
         for th, z in zip(th_pair, z_d0):
             tanh_planes(th[:], z)
         tanh_woven(th_d1[1][:], z_d1[1])
-        y_d = [open_y(0, low, quarters[2]), open_y(1, high, quarters[2])]
-        z_e0 = [z_product(6 + i, 0, ts, quarters[3]) for i, ts in enumerate((low, high))]
+        y_d = [open_y(6, low, quarters[2]), open_y(7, high, quarters[2])]
+        z_e0 = [z_product(2 + i, 0, ts, quarters[3]) for i, ts in enumerate((low, high))]
         hb_d1 = [held([P, PIECE, PACK], BF16, "hb_d1_0")]
         gain_woven(nc.gpsimd, hb_d1[0][:], th_d1[0][:], 1)
         scales_c = held([P, PASSES, QUARTER], U8, "scales_c", tag="th_d1_0")
@@ -371,7 +370,7 @@ def tile_list_tape_restore_residuals_kernel(
         th_pair = [held([P, 2, QUARTER], F32, "th_e0_%d" % i, tag="th_pair%d" % i) for i in range(2)]
         for th, z in zip(th_pair, z_e0):
             tanh_planes(th[:], z)
-        z_e1 = [z_product(6 + i, 1, range(PACK), pieces[6 + i]) for i in range(2)]
+        z_e1 = [z_product(2 + i, 1, range(PACK), pieces[6 + i]) for i in range(2)]
         planes_e0 = held([P, PACK, QUARTER], BF16, "planes_e0")
         gain_planes(planes_e0, th_pair[0], th_pair[1], 0)
         woven_e0 = held([P, QUARTER, PACK], BF16, "woven_e0")
@@ -392,7 +391,7 @@ def tile_list_tape_restore_residuals_kernel(
         tanh_planes(th_e1_rest[:], z_e1[1])
         gain_woven(nc.gpsimd, woven_e1[:, :PIECE, :], th_e1, 1)
         rows_e = (range(0, 1), range(1, 3), range(3, 4))
-        y_e = [open_y(number, ns, quarters[3]) for number, ns in zip((2, 6, 7), rows_e)]
+        y_e = [open_y(number, ns, quarters[3]) for number, ns in zip((1, 2, 3), rows_e)]
         for y, ns in zip(y_e, rows_e):
             w4_passes(y, 0, ns, quarters[3])
         planes_e1 = held([P, PACK, PIECE], BF16, "planes_e1")

@@ -99,29 +99,22 @@ def tile_list_tape_restore_residuals_kernel(
 
         w1c, w1s = {}, {}
 
-        def quantise_w1(a, b, calls, copies):
+        def quantise_w1(a, b, rows):
             grouped = held([P, PACK, P, PACK], BF16, "grouped%d%d" % (a, b))
             w1c[(a, b)] = held([P, PASS], U32, "w1c%d%d" % (a, b))
             w1s[(a, b)] = held([P, PASS], U8, "w1s%d%d" % (a, b))
-            m0 = 0
-            for copy_rows, rows in copies:
-                m1 = m0 + rows.shape[2] // PACK
-                copy_rows(
-                    out=grouped[:, :, m0:m1, :].rearrange("p t m j -> p m j t"),
-                    in_=rows.rearrange("p j (m t) -> p m j t", t=PACK),
-                )
-                m0 = m1
-            flat = grouped[:].rearrange("p t m j -> p (t m j)")
-            for c0, c1 in calls:
-                nc.vector.quantize_mx(
-                    out=w1c[(a, b)][:, c0:c1].bitcast(FP8X4),
-                    scales=w1s[(a, b)][:, c0:c1],
-                    in_=flat[:, PACK * c0 : PACK * c1],
-                )
+            nc.scalar.copy(
+                out=grouped[:].rearrange("p t m j -> p m j t"), in_=rows.rearrange("p j (m t) -> p m j t", t=PACK)
+            )
+            nc.vector.quantize_mx(
+                out=w1c[(a, b)][:].bitcast(FP8X4),
+                scales=w1s[(a, b)][:],
+                in_=grouped[:].rearrange("p t m j -> p (t m j)"),
+            )
 
-        quantise_w1(1, 0, [(0, PASS)], [(nc.scalar.copy, raw[(1, 0)][:])])
-        quantise_w1(0, 0, [(0, PASS)], [(nc.scalar.copy, raw[(0, 0)][:, :, :PASS])])
-        quantise_w1(0, 1, [(0, PASS)], [(nc.scalar.copy, raw[(0, 0)][:, :, PASS:])])
+        quantise_w1(1, 0, raw[(1, 0)][:])
+        quantise_w1(0, 0, raw[(0, 0)][:, :, :PASS])
+        quantise_w1(0, 1, raw[(0, 0)][:, :, PASS:])
 
         v = [held([P, S], U32, "v%d" % a) for a in range(PASSES)]
 
@@ -133,12 +126,23 @@ def tile_list_tape_restore_residuals_kernel(
         gather(1, 0, QUARTER)
         gather(1, QUARTER, 2 * QUARTER)
         gather(1, 2 * QUARTER, S)
-        quantise_w1(
-            1,
-            1,
-            [(P * t + m0, P * t + m0 + P // 2) for m0 in (0, P // 2) for t in range(PACK)],
-            [(nc.scalar.copy, raw[(1, PASS)][:]), (nc.vector.tensor_copy, raw[(1, PASS + QUARTER)][:])],
-        )
+        half = P // 2
+        w1c[(1, 1)] = held([P, PASS], U32, "w1c11")
+        w1s[(1, 1)] = held([P, PASS], U8, "w1s11")
+        late = [held([P, PACK, half, PACK], BF16, "late%d" % i) for i in range(2)]
+        for i, copy_rows in enumerate((nc.scalar.copy, nc.vector.tensor_copy)):
+            copy_rows(
+                out=late[i][:].rearrange("p t m j -> p m j t"),
+                in_=raw[(1, PASS + QUARTER * i)][:].rearrange("p j (m t) -> p m j t", t=PACK),
+            )
+        for i in range(2):
+            for t in range(PACK):
+                cols = slice(P * t + half * i, P * t + half * (i + 1))
+                nc.vector.quantize_mx(
+                    out=w1c[(1, 1)][:, cols].bitcast(FP8X4),
+                    scales=w1s[(1, 1)][:, cols],
+                    in_=late[i][:, t, :, :].rearrange("p m j -> p (m j)"),
+                )
 
         feats = held([P, N_TILES, S], F32, "feats", tag="tab0")
         for n in range(N_TILES):

from contextlib import ExitStack

import concourse.mybir as mybir

K, T, S, H, N = 1024, 4096, 1024, 1024, 512
FLOPS = 2 * S * (K * H + K * N + H * N)

F32 = mybir.dt.float32
BF16 = mybir.dt.bfloat16
I32 = mybir.dt.int32
U32 = mybir.dt.uint32
U16 = mybir.dt.uint16
U8 = mybir.dt.uint8
FP8X4 = mybir.dt.float8_e4m3fn_x4
FP4X4 = mybir.dt.float4_e2m1fn_x4
ACT = mybir.ActivationFunctionType
MULT = mybir.AluOpType.mult

P = 128
PACK = 4
PASS = P * PACK
PASSES = 2
N_TILES = N // P
PIECE = 128
QUARTER = 256
V_ROW = 8


def tile_list_tape_restore_residuals_kernel(
    tc, tab_words, tab_scales, offs, offs2, w1, gain, w3_words, w3_scales, w4_words, w4_scales, wgo, x0, out
):
    nc = tc.nc
    with ExitStack() as ctx:
        keep = ctx.enter_context(tc.tile_pool(name="keep", bufs=1))
        psum = ctx.enter_context(tc.psum_pool(name="psum", bufs=1))

        def held(shape, dtype, name, tag=None):
            return keep.tile(shape, dtype, name=name, tag=tag or name, align_bytes=64)

        def bank(number, shape, name):
            return psum.tile(shape, F32, tag="bank%d" % number, name=name)

        picks = keep.tile([P, S // 16], U16, name="picks")
        places = keep.tile([P, S // 16], U16, name="places")
        tab = [held([P, T], I32, "tab%d" % a) for a in range(PASSES)]
        tab_sc = held([P, PASSES, T], U8, "tab_sc")
        v_sc = held([P, PASSES, S], U8, "v_sc")
        w3_sc = held([P, PASSES, N], U8, "w3_sc")
        w4_sc = held([P, PASSES, N], U8, "w4_sc")
        nc.vector.memset(tab_sc[:, 0, :].bitcast(I32), 0)
        nc.gpsimd.memset(tab_sc[:, 1, :].bitcast(I32), 0)
        nc.vector.memset(v_sc[:].bitcast(I32), 0)
        nc.vector.memset(w4_sc[:].bitcast(I32), 0)
        nc.vector.memset(w3_sc[:].bitcast(I32), 0)

        raw = {}
        gains = held([P, PASSES, PACK], F32, "gains")
        w3 = held([P, PASSES, N], U32, "w3")
        w4 = held([P, PASSES, 2 * N], U8, "w4")
        weight = held([P, S], F32, "weight")
        picked_sc = held([P, PASSES, S], U8, "picked_sc")

        def load_w1(a, c0, c1):
            raw[(a, c0)] = held([P, PACK, c1 - c0], F32, "raw%d_%d" % (a, c0))
            nc.sync.dma_start(
                out=raw[(a, c0)][:], in_=w1[PASS * a : PASS * (a + 1), c0:c1].rearrange("(p j) c -> p j c", j=PACK)
            )

        def load_tab(a):
            nc.sync.dma_start(out=tab[a][:], in_=tab_words[a].rearrange("p t i -> p (t i)").bitcast(I32))

        def load_scales(sc, src):
            for r in range(4):
                nc.gpsimd.dma_start(
                    out=sc[r:P:32, :, :].bitcast(I32), in_=src[:, r:16:4, :].rearrange("a q c -> q a c").bitcast(I32)
                )

        load_w1(1, 0, PASS)
        nc.sync.dma_start(picks[:], offs)
        nc.sync.dma_start(out=tab_sc[4:P:8, :, :].bitcast(I32), in_=tab_scales.rearrange("a q t -> q a t").bitcast(I32))
        load_w1(0, 0, H)
        load_tab(0)
        for a in range(PASSES):
            nc.vector.tensor_copy(picked_sc[:, a, :], tab_sc[:, a, :].indirect(picks[:]))
        for r in range(4):
            nc.sync.dma_start(
                out=v_sc[V_ROW + r : P : 32, :, :].bitcast(I32), in_=picked_sc[4 + 8 * r : P : 32, :, :].bitcast(I32)
            )
        load_tab(1)
        load_w1(1, PASS, PASS + QUARTER)
        load_w1(1, PASS + QUARTER, H)
        load_scales(w4_sc, w4_scales)
        load_scales(w3_sc, w3_scales)
        nc.sync.dma_start(out=gains[:], in_=gain.rearrange("(b p t) -> p b t", b=PASSES, t=PACK))
        nc.sync.dma_start(out=w3[:].bitcast(I32), in_=w3_words.rearrange("a p c i -> p a (c i)").bitcast(I32))
        nc.sync.dma_start(out=w4[:].bitcast(I32), in_=w4_words.rearrange("a p c -> p a c").bitcast(I32))
        nc.sync.dma_start(places[:], offs2)
        nc.sync.dma_start(out=weight[:], in_=wgo)

        w1c, w1s = {}, {}

        def quantise_w1(a, b, rows):
            grouped = held([P, PACK, P, PACK], BF16, "grouped%d%d" % (a, b))
            w1c[(a, b)] = held([P, PASS], U32, "w1c%d%d" % (a, b))
            w1s[(a, b)] = held([P, PASS], U8, "w1s%d%d" % (a, b))
            nc.scalar.copy(
                out=grouped[:].rearrange("p t m j -> p m j t"), in_=rows.rearrange("p j (m t) -> p m j t", t=PACK)
            )
            nc.vector.quantize_mx(
                out=w1c[(a, b)][:].bitcast(FP8X4),
                scales=w1s[(a, b)][:],
                in_=grouped[:].rearrange("p t m j -> p (t m j)"),
            )

        quantise_w1(1, 0, raw[(1, 0)][:])
        quantise_w1(0, 0, raw[(0, 0)][:, :, :PASS])
        quantise_w1(0, 1, raw[(0, 0)][:, :, PASS:])

        v = [held([P, S], U32, "v%d" % a) for a in range(PASSES)]

        def gather(a, c0, c1):
            nc.vector.tensor_copy(v[a][:, c0:c1], tab[a][:].bitcast(U32).indirect(picks[:, c0 // 16 : c1 // 16]))

        gather(0, 0, S // 2)
        gather(0, S // 2, S)
        gather(1, 0, QUARTER)
        gather(1, QUARTER, 2 * QUARTER)
        gather(1, 2 * QUARTER, S)
        half = P // 2
        w1c[(1, 1)] = held([P, PASS], U32, "w1c11")
        w1s[(1, 1)] = held([P, PASS], U8, "w1s11")
        late = [held([P, PACK, half, PACK], BF16, "late%d" % i) for i in range(2)]
        for i, copy_rows in enumerate((nc.scalar.copy, nc.vector.tensor_copy)):
            copy_rows(
                out=late[i][:].rearrange("p t m j -> p m j t"),
                in_=raw[(1, PASS + QUARTER * i)][:].rearrange("p j (m t) -> p m j t", t=PACK),
            )
        for i in range(2):
            for t in range(PACK):
                cols = slice(P * t + half * i, P * t + half * (i + 1))
                nc.vector.quantize_mx(
                    out=w1c[(1, 1)][:, cols].bitcast(FP8X4),
                    scales=w1s[(1, 1)][:, cols],
                    in_=late[i][:, t, :, :].rearrange("p m j -> p (m j)"),
                )

        feats = held([P, N_TILES, S], F32, "feats", tag="tab0")
        for n in range(N_TILES):
            nc.sync.dma_start(out=feats[:, n, :], in_=x0[P * n : P * (n + 1), :])

        hc = [held([P, S], U32, "hc%d" % b) for b in range(PASSES)]
        hs = {}
        pages = [held([P, S], F32, "page%d" % n) for n in range(N_TILES - 1)]
        low, high = range(0, 2), range(2, 4)
        pieces = [slice(PIECE * i, PIECE * (i + 1)) for i in range(S // PIECE)]
        quarters = [slice(QUARTER * g, QUARTER * (g + 1)) for g in range(S // QUARTER)]

        def width(cols):
            return cols.stop - cols.start

        def z_product(number, b, ts, cols):
            z = bank(number, [P, len(ts), width(cols)], "z")
            for a in range(PASSES):
                for i, t in enumerate(ts):
                    nc.tensor.matmul_mx(
                        out=z[:, i, :],
                        lhsT=w1c[(a, b)][:, P * t : P * (t + 1)].bitcast(FP8X4),
                        lhsT_scale=w1s[(a, b)][:, P * t : P * (t + 1)],
                        rhs=v[a][:, cols].bitcast(FP8X4),
                        rhs_scale=v_sc[V_ROW:, a, cols],
                        start=(a, i) == (0, 0),
                        stop=(a, i) == (PASSES - 1, len(ts) - 1),
                    )
            return z

        def w3_passes(y, ns, cols, opens=False, closes=False):
            for a in range(PASSES):
                for i, n in enumerate(ns):
                    ncols = slice(P * n, P * (n + 1))
                    nc.tensor.matmul_mx(
                        out=y[:, i, :],
                        lhsT=w3[:, a, ncols].bitcast(FP8X4),
                        lhsT_scale=w3_sc[:, a, ncols],
                        rhs=v[a][:, cols].bitcast(FP8X4),
                        rhs_scale=v_sc[V_ROW:, a, cols],
                        start=opens and (a, i) == (0, 0),
                        stop=closes and (a, i) == (PASSES - 1, len(ns) - 1),
                    )

        def w4_passes(y, b, ns, cols, opens=False, closes=False):
            for i, n in enumerate(ns):
                nc.tensor.matmul_mx(
                    out=y[:, i, :],
                    lhsT=w4[:, b, 2 * P * n : 2 * P * (n + 1)].bitcast(FP4X4),
                    lhsT_scale=w4_sc[:, b, P * n : P * (n + 1)],
                    rhs=hc[b][:, cols].bitcast(FP8X4),
                    rhs_scale=hs[(b, cols.start)],
                    start=opens and i == 0,
                    stop=closes and i == len(ns) - 1,
                )

        def open_y(number, ns, cols):
            y = bank(number, [P, len(ns), width(cols)], "y")
            w3_passes(y, ns, cols, opens=True)
            return y

        def whole_y(number, ns, cols):
            y = bank(number, [P, len(ns), width(cols)], "y")
            w4_passes(y, 1, ns, cols, opens=True)
            w4_passes(y, 0, ns, cols)
            w3_passes(y, ns, cols, closes=True)
            return y

        def tanh_woven(th, z):
            nc.scalar.activation(out=th, in_=z[:, :, :].rearrange("p t j -> p j t"), func=ACT.Tanh, scale=-1.0)

        def tanh_planes(th, z):
            nc.scalar.activation(out=th, in_=z[:], func=ACT.Tanh, scale=-1.0)

        def gain_woven(engine, hb, th, b):
            engine.tensor_tensor(hb, th, gains[:, b : b + 1, :].to_broadcast(list(th.shape)), MULT)

        def gain_planes(planes, th_low, th_high, b):
            for t in range(PACK):
                th = (th_low, th_high)[t // 2]
                nc.scalar.activation(out=planes[:, t, :], in_=th[:, t % 2, :], func=ACT.Copy, scale=gains[:, b, t : t + 1])

        def weave(woven, planes):
            nc.scalar.copy(
                out=woven.rearrange("p (c i) t -> p c t i", i=4), in_=planes.rearrange("p t (c i) -> p c t i", i=4)
            )

        def quantise_h(b, cols, woven, plane=None):
            if plane is None:
                plane = held([P, width(cols)], U8, "hs%d_%d" % (b, cols.start))[:]
            hs[(b, cols.start)] = plane
            nc.vector.quantize_mx(out=hc[b][:, cols].bitcast(FP8X4), scales=plane, in_=woven.rearrange("p j t -> p (j t)"))

        def evacuate(values, y):
            nc.scalar.activation(out=values, in_=y, func=ACT.Abs)

        def weigh(engine, weighed, values, cols):
            factor = weight[:, cols]
            if len(values.shape) == 3:
                factor = factor.unsqueeze(1).to_broadcast(list(values.shape))
            engine.tensor_tensor(weighed, values, factor, MULT)

        def window(n, cols):
            return pages[n][:].indirect(places[:, cols.start // 16 : cols.stop // 16])

        def scatter_weighing(n, values, cols):
            nc.vector.tensor_tensor(window(n, cols), values, weight[:, cols], MULT)

        def scatter_copy(n, values, cols):
            nc.vector.tensor_copy(window(n, cols), values)

        th_first = {}
        th_early = held([P, 2 * QUARTER, PACK], F32, "th_early", tag="raw1_%d" % PASS)
        for i in range(2):
            th_first[(i, 0)] = th_early[:, pieces[i], :]
            tanh_woven(th_first[(i, 0)], z_product(i, 0, range(PACK), pieces[i]))
        th_c0 = th_early[:, quarters[1], :]
        for i in range(2):
            tanh_woven(th_c0[:, pieces[i], :], z_product(2 + i, 0, range(PACK), pieces[2 + i]))
        halves = (slice(0, PIECE // 2), slice(PIECE // 2, PIECE))
        z_a1 = z_product(4, 1, range(PACK), pieces[0])
        th_a1 = [held([P, PIECE // 2, PACK], F32, "th_a1_%d" % i) for i in range(2)]
        for th, half in zip(th_a1, halves):
            tanh_woven(th[:], z_a1[:, :, half])
        th_first[(1, 1)] = held([P, PIECE, PACK], F32, "th_first1")
        tanh_woven(th_first[(1, 1)][:], z_product(5, 1, range(PACK), pieces[1]))
        z_d0 = [z_product(6 + i, 0, ts, quarters[2]) for i, ts in enumerate((low, high))]
        y_a0 = open_y(4, range(0, 1), pieces[0])
        y_ab = bank(5, [P, 2, PIECE], "y")
        w3_passes(y_ab[:, 0:1, :], range(1, 2), pieces[0], opens=True)
        hb_0 = held([P, 2, PIECE, PACK], BF16, "hb_0", tag="raw1_%d" % (PASS + QUARTER))
        hb_a1 = held([P, PIECE, PACK], BF16, "hb_a1")
        for i in range(2):
            gain_woven(nc.vector, hb_0[:, i, :, :], th_first[(i, 0)], 0)
        for th, half in zip(th_a1, halves):
            gain_woven(nc.vector, hb_a1[:, half, :], th[:], 1)
        scales_a0 = held([P, PIECE], U8, "scales_a0", tag="th_a1_0")
        quantise_h(0, pieces[0], hb_0[:, 0, :, :], scales_a0[:])
        w4_passes(y_a0, 0, range(0, 1), pieces[0])
        quantise_h(1, pieces[0], hb_a1[:])
        scales_b0 = held([P, PIECE], U8, "scales_b0", tag="th_a1_1")
        quantise_h(0, pieces[1], hb_0[:, 1, :, :], scales_b0[:])
        w4_passes(y_a0, 1, range(0, 1), pieces[0], closes=True)
        w4_passes(y_ab[:, 0:1, :], 1, range(1, 2), pieces[0])
        w4_passes(y_ab[:, 0:1, :], 0, range(1, 2), pieces[0])
        y_a_high = whole_y(2, high, pieces[0])
        y_b0 = bank(3, [P, 1, PIECE], "y")
        rows_b = ((y_ab[:, 1:2, :], range(1, 2)), (y_b0, range(0, 1)))
        w3_passes(y_ab[:, 1:2, :], range(1, 2), pieces[1])
        w4_passes(y_ab[:, 1:2, :], 0, range(1, 2), pieces[1])
        w4_passes(y_b0, 0, range(0, 1), pieces[1], opens=True)
        w3_passes(y_b0, range(0, 1), pieces[1])
        z_c1 = [z_product(i, 1, ts, quarters[1]) for i, ts in enumerate((low, high))]
        values_high = held([P, 2, QUARTER], F32, "values_high")
        evacuate(values_high[:, :, pieces[0]], y_a_high[:])
        hb_b1 = held([P, PIECE, PACK], BF16, "hb_b1", tag="hb_a1")
        gain_woven(nc.vector, hb_b1[:], th_first[(1, 1)][:], 1)
        weighed_a0 = held([P, PIECE], F32, "weighed_a0")
        weigh(nc.vector, weighed_a0[:], y_a0[:, 0, :], pieces[0])
        quantise_h(1, pieces[1], hb_b1[:])
        for y, ns in rows_b:
            w4_passes(y, 1, ns, pieces[1], closes=True)
        y_b_high = whole_y(4, high, pieces[1])

        hb_c0 = held([P, QUARTER, PACK], BF16, "hb_c0", tag="hb_a1")
        gain_woven(nc.gpsimd, hb_c0[:], th_c0, 0)
        scatter_copy(0, weighed_a0[:], pieces[0])
        weighed_ab1 = held([P, QUARTER], F32, "weighed_ab1")
        weighed_b0 = held([P, PIECE], F32, "weighed_b0")
        weigh(nc.vector, weighed_ab1[:], y_ab[:].rearrange("p i j -> p (i j)"), quarters[0])
        weigh(nc.vector, weighed_b0[:], y_b0[:, 0, :], pieces[1])
        scatter_copy(1, weighed_ab1[:], quarters[0])
        scatter_copy(0, weighed_b0[:], pieces[1])

        z_d1 = [z_product(2 + i, 1, range(PACK), pieces[4 + i]) for i in range(2)]
        th_pair = [held([P, 2, QUARTER], F32, "th_c1_%d" % i, tag="th_pair%d" % i) for i in range(2)]
        for th, z in zip(th_pair, z_c1):
            tanh_planes(th[:], z)
        evacuate(values_high[:, :, pieces[1]], y_b_high[:])
        weigh(nc.gpsimd, values_high[:], values_high[:], quarters[0])
        scatter_copy(2, values_high[:, 0, :], quarters[0])
        rows_c = (range(0, 1), range(1, 2), high)
        y_c = [open_y(number, ns, quarters[1]) for number, ns in zip((0, 1, 4), rows_c)]
        planes_c1 = held([P, PACK, QUARTER], BF16, "planes_c1")
        gain_planes(planes_c1, th_pair[0], th_pair[1], 1)
        woven_c1 = held([P, QUARTER, PACK], BF16, "woven_c1")
        weave(woven_c1[:], planes_c1[:])
        th_d1 = [held([P, PIECE, PACK], F32, "th_d1_%d" % i) for i in range(2)]
        tanh_woven(th_d1[0][:], z_d1[0])
        th_pair = [held([P, 2, QUARTER], F32, "th_d0_%d" % i, tag="th_pair%d" % i) for i in range(2)]
        for th, z in zip(th_pair, z_d0):
            tanh_planes(th[:], z)
        tanh_woven(th_d1[1][:], z_d1[1])
        y_d = [open_y(6, low, quarters[2]), open_y(7, high, quarters[2])]
        z_e0 = [z_product(2 + i, 0, ts, quarters[3]) for i, ts in enumerate((low, high))]
        hb_d1 = [held([P, PIECE, PACK], BF16, "hb_d1_0")]
        gain_woven(nc.gpsimd, hb_d1[0][:], th_d1[0][:], 1)
        scales_c = held([P, PASSES, QUARTER], U8, "scales_c", tag="th_d1_0")
        quantise_h(0, quarters[1], hb_c0[:], scales_c[:, 0, :])
        quantise_h(1, quarters[1], woven_c1[:], scales_c[:, 1, :])
        for y, ns, order in zip(y_c, rows_c, ((0, 1), (1, 0), (1, 0))):
            for b in order:
                w4_passes(y, b, ns, quarters[1], closes=b == order[1])

        pages.append(held([P, S], F32, "page3", tag="woven_c1"))
        hb_d1.append(held([P, PIECE, PACK], BF16, "hb_d1_1", tag="hb_a1"))
        gain_woven(nc.gpsimd, hb_d1[1][:], th_d1[1][:], 1)
        scatter_copy(3, values_high[:, 1, :], quarters[0])

        values_c0 = held([P, QUARTER], F32, "values_c0")
        evacuate(values_c0[:], y_c[0][:, 0, :])
        scatter_weighing(0, values_c0[:], quarters[1])
        planes_d0 = held([P, PACK, QUARTER], BF16, "planes_d0")
        gain_planes(planes_d0, th_pair[0], th_pair[1], 0)
        woven_d0 = held([P, QUARTER, PACK], BF16, "woven_d0")
        weave(woven_d0[:], planes_d0[:])
        quantise_h(0, quarters[2], woven_d0[:])
        scales_d1 = held([P, QUARTER], U8, "scales_d1")
        for i in range(2):
            quantise_h(1, pieces[4 + i], hb_d1[i][:], scales_d1[:, pieces[i]])
        hs[(1, quarters[2].start)] = scales_d1[:]
        for y, ns in zip(y_d, (low, high)):
            for b in range(PASSES):
                w4_passes(y, b, ns, quarters[2], closes=b == 1)
        values_c2 = held([P, QUARTER], F32, "values_c2", tag="planes_d0")
        evacuate(values_c2[:], y_c[2][:, 0, :])
        scatter_weighing(2, values_c2[:], quarters[1])

        th_pair = [held([P, 2, QUARTER], F32, "th_e0_%d" % i, tag="th_pair%d" % i) for i in range(2)]
        for th, z in zip(th_pair, z_e0):
            tanh_planes(th[:], z)
        z_e1 = [z_product(2 + i, 1, range(PACK), pieces[6 + i]) for i in range(2)]
        planes_e0 = held([P, PACK, QUARTER], BF16, "planes_e0")
        gain_planes(planes_e0, th_pair[0], th_pair[1], 0)
        woven_e0 = held([P, QUARTER, PACK], BF16, "woven_e0")
        weave(woven_e0[:], planes_e0[:])
        after_weave = held([P, 5, QUARTER], F32, "after_weave", tag="planes_e0")
        weigh(nc.vector, after_weave[:, 2, :], y_c[1][:, 0, :], quarters[1])
        quantise_h(0, quarters[3], woven_e0[:])
        scatter_copy(1, after_weave[:, 2, :], quarters[1])

        evacuate(after_weave[:, 0:2, :], y_d[0][:])
        after_e0 = held([P, 3 * QUARTER], F32, "after_e0", tag="woven_e0")
        woven_e1 = after_e0[:, QUARTER:].bitcast(BF16).rearrange("p (j t) -> p j t", t=PACK)
        weigh(nc.gpsimd, after_e0[:, :QUARTER], after_weave[:, 0, :], quarters[2])
        scatter_copy(0, after_e0[:, :QUARTER], quarters[2])
        th_e1 = after_weave[:, 3:5, :].rearrange("p i (j t) -> p (i j) t", t=PACK)
        th_e1_rest = held([P, PACK, PIECE], F32, "th_e1_rest", tag="th_pair1")
        tanh_woven(th_e1, z_e1[0])
        tanh_planes(th_e1_rest[:], z_e1[1])
        gain_woven(nc.gpsimd, woven_e1[:, :PIECE, :], th_e1, 1)
        rows_e = (range(0, 1), range(1, 3), range(3, 4))
        y_e = [open_y(number, ns, quarters[3]) for number, ns in zip((1, 2, 3), rows_e)]
        for y, ns in zip(y_e, rows_e):
            w4_passes(y, 0, ns, quarters[3])
        planes_e1 = held([P, PACK, PIECE], BF16, "planes_e1")
        gain_planes(planes_e1, th_e1_rest[:, 0:2, :], th_e1_rest[:, 2:4, :], 1)
        woven_rest = held([P, PIECE, PACK], BF16, "woven_rest")
        weave(woven_rest[:], planes_e1[:])
        values_late = held([P, 5, QUARTER], F32, "values_late", tag="planes_e1")
        weigh(nc.gpsimd, values_late[:, 4, :], after_weave[:, 1, :], quarters[2])
        scales_e1 = held([P, QUARTER], U8, "scales_e1")
        quantise_h(1, pieces[7], woven_rest[:], scales_e1[:, pieces[1]])
        quantise_h(1, pieces[6], woven_e1[:, :PIECE, :], scales_e1[:, pieces[0]])
        hs[(1, quarters[3].start)] = scales_e1[:]
        for y, ns in zip(y_e, rows_e):
            w4_passes(y, 1, ns, quarters[3], closes=True)

        last = held([P, S], F32, "last", tag="woven_e0")
        scatter_copy(1, values_late[:, 4, :], quarters[2])
        evacuate(values_late[:, 3, :], y_d[1][:, 0, :])
        weigh(nc.gpsimd, last[:, quarters[0]], values_late[:, 3, :], quarters[2])
        scatter_copy(2, last[:, quarters[0]], quarters[2])
        values_e = held([P, 3, QUARTER], F32, "values_e")
        evacuate(values_late[:, 0, :], y_c[2][:, 1, :])
        evacuate(values_late[:, 1, :], y_d[1][:, 1, :])
        evacuate(values_e[:, 0, :], y_e[0][:, 0, :])
        evacuate(values_e[:, 1:3, :], y_e[1][:])
        evacuate(values_late[:, 2, :], y_e[2][:, 0, :])
        weigh(
            nc.gpsimd,
            last[:, QUARTER : 3 * QUARTER],
            values_late[:, 0:2, :].rearrange("p g j -> p (g j)"),
            slice(QUARTER, 3 * QUARTER),
        )
        weigh(nc.gpsimd, values_e[:, 0, :], values_e[:, 0, :], quarters[3])
        weigh(nc.gpsimd, values_e[:, 1:3, :], values_e[:, 1:3, :], quarters[3])
        weigh(nc.gpsimd, last[:, quarters[3]], values_late[:, 2, :], quarters[3])
        sizes = held([P, N_TILES, S], F32, "sizes", tag="planes_e1")
        for n in high:
            nc.scalar.activation(out=sizes[:, n, :], in_=feats[:, n, :], func=ACT.Abs)
        for n in range(3):
            scatter_copy(n, values_e[:, n, :], quarters[3])
        scatter_copy(3, last[:, QUARTER:], slice(QUARTER, S))

        def weigh_and_store(n, c0, c1, engine, product):
            engine.tensor_tensor(product, pages[n][:, c0:c1], sizes[:, n, c0:c1], MULT)
            nc.sync.dma_start(out=out[P * n : P * (n + 1), c0:c1], in_=product)

        for n in low:
            nc.gpsimd.tensor_tensor(sizes[:, n, :], pages[n][:], feats[:, n, :], MULT)
            nc.scalar.activation(out=feats[:, n, :], in_=sizes[:, n, :], func=ACT.Abs)
            nc.scalar.dma_start(out=out[P * n : P * (n + 1), :], in_=feats[:, n, :])
        for c0 in (0, S // 2):
            weigh_and_store(2, c0, c0 + S // 2, nc.gpsimd, feats[:, 2, c0 : c0 + S // 2])
        for c0 in range(0, S, QUARTER):
            weigh_and_store(3, c0, c0 + QUARTER, nc.vector, sizes[:, 2, c0 : c0 + QUARTER])
